import numpy as np, ml_dtypes
CORES = [24,25,26,27,28,29,30,31]
N = 8
import mx_ref
BF = ml_dtypes.bfloat16
def gcols(t, e):
    v = np.concatenate([t.reshape(8, 16, -1, 4), np.zeros((8, 16, 1, 4), BF)], axis=2)
    return np.ascontiguousarray(np.stack([v[g][:, e[g]] for g in range(8)])).reshape(128, -1)
def tile(rs):
    return np.stack(rs, axis=2).reshape(128, -1).astype(BF)
def cut(t, i, w=512):
    return t[:, w * i:w * i + w]
def pick(q, e):
    c = np.concatenate([q[0].reshape(128, -1, 4), np.zeros((128, 1, 4), np.uint8)], axis=1); s = np.concatenate([q[1], np.ones((16, 1), np.uint8)], axis=1)
    return (np.ascontiguousarray(c[:, e].reshape(128, -1)), np.ascontiguousarray(s[:, e]))
def join(*qs):
    return (np.concatenate([q[0] for q in qs], axis=1), np.concatenate([q[1] for q in qs], axis=1))
def put(q, e, v):
    c, s = q[0].reshape(128, -1, 4).copy(), q[1].copy(); c[:, e] = v[0].reshape(128, -1, 4); s[:, e] = v[1]
    return (c.reshape(128, -1), s)
def pk(c, s):
    return (np.ascontiguousarray(c), mx_ref.live(s))
def emit(q):
    return q[0], q[1]
def packed(v, rng):
    q = [mx_ref.quantize(np.ascontiguousarray(v[r])) for r in range(N)]
    return np.stack([a for a, b in q]), np.stack([mx_ref.plane(b, rng) for a, b in q])
def values_of_codes():
    e, c = np.zeros((128, 128, 4), np.float32), np.zeros((128, 2, 4), np.uint8)
    e[np.arange(128), np.arange(128), 0] = 1
    c[:127, :, 0] = np.arange(256).reshape(2, 128).T[:127]
    return mx_ref.matmul(mx_ref.quantize(e.reshape(128, 512).astype(BF)), (c.reshape(128, 8), np.full((16, 2), 127, np.uint8))).T.reshape(-1).astype(np.float64)
CODE_VALUE, SCALE_VALUE = values_of_codes(), 2.0 ** (np.arange(256) - 127.0)
def decode(q):
    return (CODE_VALUE[q[0]].reshape(16, 8, -1, 4) * SCALE_VALUE[q[1]][:, None, :, None] + 0.0).reshape(128, -1).astype(np.float32)
def f(rng, *shape):
    return mx_ref.flush((rng.standard_normal(shape, dtype=np.float32) * np.exp2(rng.integers(-2, 3, shape[:-1] + (1,)))).astype(BF))
def wide(rng, *shape, cols=0):
    v = rng.standard_normal(shape, dtype=np.float32) * np.exp2(rng.integers(-12, 13, shape)).astype(np.float32)
    if cols: v *= np.repeat(np.exp2(rng.integers(-cols, cols + 1, shape[:-2] + (1, shape[-1] // 4))) * (rng.random(shape[:-2] + (1, shape[-1] // 4)) > 0.0625), 4, axis=-1).astype(np.float32)
    return mx_ref.flush(v.astype(BF))
C, L1, H1, L2, H2, K, R = 256, 96, 160, 64, 80, 96, 3
def big(v):
    v = v.astype(np.float32)
    v[np.abs(v) < np.float32(2.0 ** -16)] = 0
    return v.astype(BF)
def numbers_of(rng):
    return {"x": big(f(rng, N, 128, 4 * C)), "u": np.array(f(rng, N, 128, 512)), "v": np.array(f(rng, N, 128, 512))}
def layers(rng):
    return big(f(rng, N, 128, 2048)).reshape(N, 8, 16, 4, 8, 16, 4)
def weights(rng, w):
    c, p = packed(np.ascontiguousarray(w).reshape(N, 128, 2048), rng)
    return {"wc": c, "ws": p}
def setup_inputs(rng):
    return {**numbers_of(rng), **weights(rng, layers(rng))}
def setup_inputs_ties(rng):
    d = numbers_of(rng)
    x = d["x"].reshape(N, 8, 16, C, 4)
    x[:, :, 0] = 0
    x[:, :, 0, :, :2] = np.where(rng.random((N, 8, C, 2)) < 0.125, 3, rng.integers(1, 3, (N, 8, C, 2))).astype(np.float32).astype(BF)
    u = d["u"].reshape(N, 128, 128, 4)
    u[:, :, ::16] = 0
    u[:, :, 1::16] = 0
    e = int(rng.integers(N))
    k = rng.permutation(N - 2) % 2 * 2.0 - 1.0
    for i in range(N - 2):
        r = (e + 1 + i) % N
        for h in range(0, 128, 16):
            u[r, h, h, 0] = k[i]
            u[r, h, h + 1, 1] = k[i]
    w = layers(rng)
    w[:, :, :, :, :, 0] = 0
    return {"x": x.reshape(N, 128, 4 * C), "u": u.reshape(N, 128, 512), "v": d["v"], **weights(rng, w)}
def setup_inputs_near(rng):
    d = numbers_of(rng)
    x = d["x"].astype(np.float32).reshape(N, 8, 16, C, 4)
    x[:, :, 0] = 0
    x[:, :, 8:] = 0
    u = d["u"].reshape(N, 128, 128, 4)
    u[:, :, ::16] = 0
    u[:, :, 1::16] = 0
    o = rng.permutation(N) % 4
    for r in range(N):
        k = 1.0 if o[r] == 0 else 2.0 ** -30
        if o[r] < 3:
            s = rng.integers(0, 16, (8, C))
            x[r, :, 8] = ((s[:, :, None] >> np.arange(4)) & 1) * np.exp2(np.arange(4) - 23.0)
        if o[r] < 2:
            x[r, :, 0, :, 0] = 1.0 - 2.0 * o[r]
            x[r, :, 11, :, 0] = 2.0 ** -10
        if o[r] == 2: x[r, :, 0, :, 0] = -1.0 * (rng.random((8, C)) < 0.25)
        if o[r] == 3:
            s = rng.random((8, C)) < 0.25
            x[r, :, 10, :, 0] = np.where(s, 9.0, 0.0) * 2.0 ** -32
            x[r, :, 12, :, 0] = np.where(s, 0.0, 8.0) * 2.0 ** -32
        for h in range(0, 128, 16):
            for i in (h, h + 1):
                u[r, h, i, 0] = 1.0 if o[r] == 2 else k
                u[r, h + 8, i] = k
                u[r, h + 10, i, 0] = k * 1.125
                u[r, h + 11, i, 0] = k
                u[r, h + 12, i, 0] = k * 1.25
    w = layers(rng)
    w[:, :, :, :, :, 0] = 0
    w[:, :, :, :, :, 8:] = 0
    return {"x": x.reshape(N, 128, 4 * C).astype(BF), "u": u.reshape(N, 128, 512), "v": d["v"], **weights(rng, w)}
def setup_inputs_huge(rng):
    d = numbers_of(rng)
    e = rng.permutation(N)
    x = -0.6 - 0.4 * rng.random((N, 8, 16, C, 4))
    a = 0.9 + 0.1 * rng.random((N, 128, 128, 4))
    x[e[0], :, :15] = -1.0
    for i in (L1 - 1, H1 + 1): x[e[0], :, :, i] = -0.625
    a[e[0]] = 1.0
    u = d["u"].astype(np.float32).reshape(N, 128, 128, 4)
    for r in range(N):
        both = r in e[1::2]
        if both: x[r] *= rng.choice([-1.0, 1.0], (8, 1, C, 1))
        for h in range(0, 128, 16):
            i = slice(h, h + 16) if both else slice(0, 128)
            u[r, :, h:h + 2] = 0
            u[r, i, h:h + 2] = 2.0 ** 30 * a[r, i, h:h + 2]
    w = np.zeros((N, 128, 4, 128, 4), np.float32)
    i = np.arange(128)
    for b in range(4): w[:, i, b, i, b] = -1
    return {"x": (2.0 ** 30 * x).astype(np.float32).reshape(N, 128, 4 * C).astype(BF), "u": u.astype(BF).reshape(N, 128, 512), "v": d["v"], **weights(rng, w.astype(BF))}
def setup_inputs_edge(rng):
    d = numbers_of(rng)
    x = d["x"].reshape(N, 8, 16, C, 4)
    c = np.where(rng.random((N, 8)) < 0.25, rng.integers(L1, H1 + 1, (N, 8)), rng.choice([L1, H1], (N, 8)))
    k = np.where(rng.random((N, 8)) < 0.25, rng.integers(L2, H2 + 1, (N, 8)), rng.choice([L2, H2], (N, 8)))
    e = int(rng.integers(N))
    for r in (e, (e + 1) % N):
        c[r] = H1
        k[r] = L2
    x[:, :, 0] = 0
    x[:, :, 0, :, :2] = rng.integers(-1, 2, (N, 8, C, 2)).astype(np.float32).astype(BF)
    for i in (L1 - 1, H1 + 1): x[:, :, 0, i, 0] = 4.0
    for i in (L2 - 1, H2 + 1): x[:, :, 0, i, 1] = 4.0
    for r in range(N):
        for g in range(8):
            x[r, g, 0, c[r, g], 0] = 2.0
            x[r, g, 0, k[r, g], 1] = 2.0
    n = (N, 8, 8, C, 4)
    s = np.exp2(-1.0 * rng.integers(8, 15, n)) * (1.0 + (2 * rng.integers(0, 64, n) + 1) * 2.0 ** -7) * rng.choice([-1.0, 1.0], n)
    s[:, :, 0, :, 0] = 1.96875 * rng.choice([-1.0, 1.0], (N, 8, C))
    x[:, :, 8:] = s.astype(np.float32).astype(BF)
    u = d["u"].reshape(N, 128, 128, 4)
    u[:, :, ::16] = 0
    u[:, :, 1::16] = 0
    for h in range(0, 128, 16):
        u[:, h, h, 0] = 1
        u[:, h, h + 1, 1] = 1
    return {"x": x.reshape(N, 128, 4 * C), "u": u.reshape(N, 128, 512), "v": d["v"], **weights(rng, layers(rng))}
def setup_inputs_spread(rng):
    d = setup_inputs(rng)
    d["x"] = big(wide(rng, N, 128, 4 * C, cols=6))
    return d
def check_inputs(d):
    b = []
    for k in ("x", "u", "v"):
        a = np.abs(d[k].astype(np.float32))
        if not (np.isfinite(a).all() and ((a == 0) | (a >= 2.0 ** -30) & (a <= 2.0 ** 30)).all()): b.append("a value of " + k)
    none, least, most = [emit(mx_ref.quantize(np.full((128, 16), k, np.float32).astype(BF)))[1][0, 0] for k in (0.0, 2.0 ** -30, 2.0 ** 30)]
    for r in range(N):
        if ((d["wc"][r] == 0x7F) | (d["wc"][r] == 0xFF)).any(): b.append("wc: a code that is no number")
        s = mx_ref.live(d["ws"][r])
        if ((s != none) & ((s < least) | (s > most))).any(): b.append("ws: a scale out of range")
    return b
def folded(c, k):
    p = np.arange(C)
    q = np.where(p < c, c - 1 - p, p - c)
    z = np.where(q < k, k - 1 - q, q - k)
    right = (p >= c).astype(np.int64)
    leaf = np.where(q < k, right, 3 - right)
    o = np.argsort(4 * z + leaf, axis=1)
    zo = np.take_along_axis(z, o, axis=1)
    first = np.ones((8, C), bool)
    first[:, 1:] = zo[:, 1:] != zo[:, :-1]
    low, above = np.full((8, K), -1), C + z
    g, j = np.nonzero(first)
    low[g, zo[g, j]] = o[g, j]
    g, j = np.nonzero(~first)
    above[g, o[g, j - 1]] = o[g, j]
    return o, low, above
def reference(x, u, v, wc, ws):
    qu = [mx_ref.quantize(u[r]) for r in range(N)]
    lay = [pk(wc[r], ws[r]) for r in range(N)]
    now = [x[r] for r in range(N)]
    for t in range(R):
        own, folds, sent = [], [], []
        for r in range(N):
            q = mx_ref.quantize(now[r])
            own.append(decode(q))
            s = mx_ref.matmul(qu[r], q) + np.float32(0.0)
            c = L1 + np.argmax(s[::16, L1:H1 + 1], axis=1)
            k = L2 + np.argmax(s[1::16, L2:H2 + 1], axis=1)
            folds.append(folded(c[:, None], k[:, None]))
            sent.append(mx_ref.quantize(gcols(now[r], folds[r][1])))
        came = decode(join(*sent)).astype(BF)
        for r in range(N):
            o, low, above = folds[r]
            a = np.concatenate([own[r].astype(BF), cut(came, (r + 1) % N, 4 * K)], axis=1)
            z = mx_ref.quantize(((own[r] + gcols(a, above).astype(np.float32)) * np.float32(0.5)).astype(BF))
            made = tile([mx_ref.matmul(pick(lay[r], np.arange(128 * b, 128 * b + 128)), z) * np.float32(0.03125) + own[r][:, b::4] for b in range(4)])
            now[r] = gcols(made, o)
    y, lo = np.zeros((N, 128, C), np.float32), np.zeros((N, 8, C), np.float32)
    oc, osc = np.zeros((N, 128, 4 * C), np.uint8), np.zeros((N, 16, C), np.uint8)
    for r in range(N):
        q = mx_ref.quantize(now[r])
        y[r] = mx_ref.matmul(mx_ref.quantize(v[r]), q)
        lo[r] = folds[r][0]
        oc[r], osc[r] = emit(q)
    return {"y": y, "lo": lo, "oc": oc, "osc": osc}

@@ -1,0 +1,414 @@
+from concourse.mybir import dt, AluOpType as A, AxisListType, ActivationFunctionType as F
+
+R, C, K = 3, 256, 96
+PAD = 80
+XWID = 4 * (C + 2 * PAD)
+XB = 4 * PAD
+AWID = C + K
+BIG = 1000.0
+
+WORK = {}
+_n = [0]
+for _name, _w in (("NEG", 72), ("PC", 72), ("PK", 24), ("MC", 72), ("MK", 24), ("C4", 1), ("K4", 1), ("S15", 1), ("T3", 1),
+                  ("QT", 1), ("J", 16), ("J1", 16), ("H1", 16), ("I1", 16), ("ZQ", 8),
+                  ("mk", 8), ("f", 1), ("w1", 8), ("r0", 8), ("m", 8), ("r", 8),
+                  ("c", 1), ("k", 1), ("n3", 1), ("n2", 1), ("cpk", 1), ("k2", 1), ("c2", 1), ("tau", 1), ("kb", 1), ("km1", 1),
+                  ("nch", 1), ("nk", 1), ("nkw", 1), ("rl", 1), ("rho", 1), ("br", 1), ("bt", 1), ("bn", 1), ("a", 1),
+                  ("Rr", 16), ("ae", 16), ("ay", 16), ("w", 16),
+                  ("x1", 16), ("x2", 16), ("x3", 16), ("y1", 16), ("y2", 16), ("v", 16), ("v0", 16), ("v1", 16), ("v2", 16),
+                  ("v3", 16), ("o1", 16), ("o2", 16), ("o3", 16), ("o4", 16), ("mn", 16), ("mm", 16),
+                  ("l2", 16), ("l3", 16), ("l4", 16), ("m1", 16), ("m2", 16), ("t1", 16), ("t2", 16), ("t3", 16), ("u", 16),
+                  ("N", 16), ("I", 16), ("mo", 16), ("zl", 16), ("xx", 16), ("ti", 16),
+                  ("gg", 16), ("km", 16), ("zk", 16), ("D", 16), ("gD", 16)):
+    WORK[_name] = (_n[0], _w)
+    _n[0] += -(-_w // 8) * 8
+
+SCRATCH = {
+    "wk": ("sbuf", [128, _n[0]], "float32"),
+    "IP": ("sbuf", [128, 1], "int32"), "M16": ("sbuf", [128, 16], "int32"), "UI": ("sbuf", [128, 16], "int32"),
+    "I15": ("sbuf", [128, 1], "int32"), "I3": ("sbuf", [128, 1], "int32"), "ZI": ("sbuf", [128, 16], "int32"),
+    "PLACE": ("sbuf", [128, C], "float32"), "LOF": ("sbuf", [128, C], "float32"), "YO": ("sbuf", [128, C], "float32"),
+    "UO": ("sbuf", [128, 16], "uint16"), "LB1": ("sbuf", [128, 16], "uint16"), "LB2": ("sbuf", [128, 8], "uint16"),
+    "LC": ("sbuf", [128, 16], "uint16"), "LO": ("sbuf", [128, 16], "uint16"),
+    "ONE": ("sbuf", [128, 516], "bfloat16"), "EB": ("sbuf", [128, 516], "bfloat16"), "EB2": ("sbuf", [128, 516], "bfloat16"),
+    "UT": ("sbuf", [128, 512], "bfloat16"), "VT": ("sbuf", [128, 512], "bfloat16"), "BT": ("sbuf", [128, 512], "bfloat16"),
+    "ZT": ("sbuf", [128, 4 * C], "bfloat16"), "YS": ("sbuf", [128, 4 * C], "bfloat16"), "AW": ("sbuf", [128, 4 * AWID], "bfloat16"),
+    "FH": ("sbuf", [128, 2 * C], "bfloat16"), "AS": ("sbuf", [128, 2 * C], "bfloat16"),
+}
+for _name, _w in (("E", 512), ("EH", 256), ("QU", 128), ("UC", 256), ("QV", 128), ("W", 512), ("QZ", 256), ("QM0", 128), ("QM1", 128),
+                  ("QM2", 128), ("QX0", AWID), ("QX1", AWID), ("QX2", AWID), ("QX3", C), ("QB0", 128), ("QB1", 128), ("QB2", 128)):
+    SCRATCH[_name + "c"] = ("sbuf", [128, _w], "float8_e4m3fn_x4")
+    SCRATCH[_name + "p"] = ("sbuf", [128, _w], "uint8")
+for _t in range(R + 1):
+    SCRATCH["XW%d" % _t] = ("sbuf", [128, XWID], "bfloat16")
+for _b in range(8):
+    SCRATCH["p%d" % _b] = ("psum", [128, 512], "float32")
+LOADS = ["xm", "xa", "xb", "u", "v", "wc", "ws"]
+STORES = ["oc", "os0", "os1", "os2", "os3", "y0", "y1", "lo"]
+SEMAPHORES = ["cv", "cs", "ct", "cg"] + ["d_" + n for n in LOADS + STORES] + ["arr%d" % t for t in range(R)] + ["loc%d" % t for t in range(R)]
+
+
+def rank_program(g, core, T, topo):
+    rank = T.rank_of(core)
+    if rank is None:
+        return
+    V, S, P, Y = g.vector, g.scalar, g.tensor, g.sync
+    queue = {"v": V, "s": S, "t": P, "g": g, "y": Y}
+    count = {}
+    waited = {}
+    known = {q: {} for q in queue}
+    behind = {}
+    log = {}
+
+    def need(q, name, a, b, write, out):
+        for x in log.get(name, ()):
+            if x[0] < b and a < x[1]:
+                if x[3] != q:
+                    if write or x[2] or name[0] == "p" and name[1:].isdigit():
+                        out.append(x[4])
+                elif x[2] and not write:
+                    out.append(x[4])
+
+    def note(q, name, a, b, write, ev):
+        rows = log.setdefault(name, [])
+        if write:
+            rows[:] = [x for x in rows if not (a <= x[0] and x[1] <= b)]
+        rows.append((a, b, write, q, ev))
+
+    def wait(q, ev):
+        sem, val = ev
+        if known[q].get(sem, 0) >= val:
+            return
+        queue[q].wait_ge(T.sem[sem], val)
+        waited[sem] = max(waited.get(sem, 0), val)
+        for s, n in list(behind.get(ev, {}).items()) + [(sem, val)]:
+            known[q][s] = max(known[q].get(s, 0), n)
+
+    def pre(q, rd, wr):
+        evs = []
+        for r in rd:
+            need(q, r[0], r[1], r[2], False, evs)
+        for r in wr:
+            need(q, r[0], r[1], r[2], True, evs)
+        most = {}
+        for s, n in evs:
+            most[s] = max(most.get(s, 0), n)
+        for s in sorted(most, key=lambda s: (s == "c" + q, s)):
+            wait(q, (s, most[s]))
+
+    def emit(q, fn, rd, wr):
+        pre(q, rd, wr)
+        sem = "c" + q
+        count[sem] = count.get(sem, 0) + 1
+        fn().then_inc(T.sem[sem], 1)
+        ev = (sem, count[sem])
+        behind[ev] = dict(known[q])
+        for r in rd:
+            note(q, r[0], r[1], r[2], False, ev)
+        for r in wr:
+            note(q, r[0], r[1], r[2], True, ev)
+
+    def dma(q, name, out, in_, rd, wr):
+        pre(q, rd, wr)
+        sem = "d_" + name
+        count[sem] = 16
+        queue[q].dma_start(out, in_).then_inc(T.sem[sem], 16)
+        ev = (sem, 16)
+        behind[ev] = dict(known[q])
+        for r in rd:
+            note(sem, r[0], r[1], r[2], False, ev)
+        for r in wr:
+            note(sem, r[0], r[1], r[2], True, ev)
+
+    def reg(n):
+        return ("wk", WORK[n][0], WORK[n][0] + WORK[n][1])
+
+    def cut(n, a, b):
+        return ("wk", WORK[n][0] + a, WORK[n][0] + b)
+
+    def norm(x):
+        return reg(x) if isinstance(x, str) else x
+
+    def ap(x):
+        return T[x[0]][:, x[1]:x[2]]
+
+    def lanes(name, a, b):
+        return [(name + "#%d" % i, a, b) for i in range(4)]
+
+    def ts(out, in0, s1, s2, op0, op1=None):
+        out, in0 = norm(out), norm(in0)
+        rd = [in0]
+        sc = []
+        for s in (s1, s2):
+            if isinstance(s, (str, tuple)):
+                s = norm(s)
+                rd.append(s)
+                s = ap(s)
+            sc.append(s)
+        if op1 is None:
+            emit("v", lambda: V.tensor_scalar(ap(out), ap(in0), sc[0], None, op0), rd, [out])
+        else:
+            emit("v", lambda: V.tensor_scalar(ap(out), ap(in0), sc[0], sc[1], op0, op1), rd, [out])
+
+    def tt(out, x, y, op):
+        out, x, y = norm(out), norm(x), norm(y)
+        emit("v", lambda: V.tensor_tensor(ap(out), ap(x), ap(y), op), [x, y], [out])
+
+    def act(out, x, scale, bias, func=F.Identity):
+        out, x = norm(out), norm(x)
+        rd = [x]
+        if isinstance(bias, (str, tuple)):
+            bias = norm(bias)
+            rd.append(bias)
+            bias = ap(bias)
+        emit("s", lambda: S.activation(ap(out), ap(x), func, bias=bias, scale=scale), rd, [out])
+
+    def quant(dst, a, n, src, sa, rd):
+        emit("v", lambda: V.quantize_mx(T[dst + "c"][:, a:a + n], T[dst + "p"][:, a:a + n], T[src][:, sa:sa + 4 * n]), rd, [(dst, a, a + n)])
+
+    def mm(bank, n, st, sa, mv, ma, start=True, stop=True):
+        emit("t", lambda: P.matmul_mx(T["p%d" % bank][:, 0:n], T[st + "c"][:, sa:sa + 128], T[st + "p"][:, sa:sa + 128],
+                                      T[mv + "c"][:, ma:ma + n], T[mv + "p"][:, ma:ma + n], start, stop),
+             [(st, sa, sa + 128), (mv, ma, ma + n)], [("p%d" % bank, 0, 512)])
+
+    def fill(name, a, b, val, wr=None):
+        emit("v", lambda: V.memset(T[name][:, a:b], val), [], wr or [(name, a, b)])
+
+    def psum_copy(q, out, oa, bank, a, b, scale):
+        rd, wr = [("p%d" % bank, 0, 512)], [(out, oa, oa + b - a)]
+        src, to = T["p%d" % bank][:, a:b], T[out][:, oa:oa + b - a]
+        if q == "v":
+            emit("v", lambda: V.tensor_scalar(to, src, scale, None, A.mult), rd, wr)
+        else:
+            emit("s", lambda: S.activation(to, src, F.Copy, scale=scale), rd, wr)
+
+    def gather(q, out, win, off, rd, wr):
+        if q == "v":
+            emit("v", lambda: V.tensor_copy(out, win.indirect(off)), rd, wr)
+        else:
+            emit("s", lambda: S.activation(out, win.indirect(off), F.Copy), rd, wr)
+
+    for name, a, b in (("xm", 64, 192), ("xa", 0, 64), ("xb", 192, 256)):
+        dma("y", name, T.XW0[:, XB + 4 * a:XB + 4 * b], T.x[:, 4 * a:4 * b], [], lanes("XW0", a, b))
+    dma("s", "u", T.UT[:, 0:512], T.u[:, 0:512], [], [("UT", 0, 512)])
+    dma("y", "wc", T.Wc[:, 0:512].bitcast(dt.uint8), T.wc[:, 0:2048], [], [("W", 0, 512)])
+    dma("y", "ws", T.Wp[:, 0:512], T.ws[:, 0:512], [], [("Ws", 0, 512)])
+    dma("y", "v", T.VT[:, 0:512], T.v[:, 0:512], [], [("VT", 0, 512)])
+
+    fill("ONE", 0, 516, 32.0)
+    emit("g", lambda: g.iota(T.UI[:, 0:16], [[1, 2], [16, 8]], 0, 0), [], [("UI", 0, 16)])
+    emit("g", lambda: g.iota(T.IP[:, 0:1], [[1, 1]], 0, 1), [], [("IP", 0, 1)])
+    emit("g", lambda: g.iota(T.M16[:, 0:16], [[16, 16]], 0, 0), [], [("M16", 0, 16)])
+    emit("g", lambda: g.affine_select(T.EB[:, 0:516], T.ONE[:, 0:516], [[-1, 516]], A.is_equal, 0.0, 4, 4), [("ONE", 0, 516)], [("EB", 0, 516)])
+    emit("g", lambda: g.iota(T.PLACE[:, 0:C], [[1, C]], 0, 0, allow_small_or_imprecise_dtypes=True), [], [("PLACE", 0, C)])
+    fill("XW0", 0, XB, 0.0, lanes("XW0", -PAD, 0))
+    fill("wk", WORK["NEG"][0], WORK["NEG"][0] + 72, -1.0e29)
+    fill("wk", WORK["MK"][0] + 17, WORK["MK"][0] + 18, 256.0)
+    fill("BT", 384, 512, 0.0, lanes("BT", 96, 128))
+    emit("v", lambda: V.tensor_copy(T.UO[:, 0:16], T.UI[:, 0:16]), [("UI", 0, 16)], [("UO", 0, 16)])
+    ts(("I15", 0, 1), ("IP", 0, 1), 15, None, A.bitwise_and)
+    ts(("I3", 0, 1), ("IP", 0, 1), 3, None, A.bitwise_and)
+    emit("v", lambda: V.tensor_copy(ap(reg("S15")), T.I15[:, 0:1]), [("I15", 0, 1)], [reg("S15")])
+    emit("v", lambda: V.tensor_copy(ap(reg("T3")), T.I3[:, 0:1]), [("I3", 0, 1)], [reg("T3")])
+    ts("J", ("M16", 0, 16), "S15", None, A.add)
+    ts(cut("MC", 65, 66), "T3", 382.0, None, A.add)
+    ts("QT", "T3", -0.25, 0.5, A.mult, A.add)
+    ts("I1", "J", "T3", 322.0, A.subtract, A.add)
+    ts("ZQ", cut("J", 0, 8), "T3", 258.0, A.subtract, A.add)
+    fill("XW0", XB + 4 * C, XWID, 0.0, lanes("XW0", C, C + PAD))
+    for i in (1, 2):
+        for a in (0, XB + 4 * C):
+            j = -PAD if a == 0 else C
+            emit("s", lambda: S.activation(T["XW%d" % i][:, a:a + XB], T.XW0[:, 0:XB], F.Copy), lanes("XW0", -PAD, 0), lanes("XW%d" % i, j, j + PAD))
+    quant("QU", 0, 128, "UT", 0, [("UT", 0, 512)])
+    quant("QM0", 0, 128, "XW0", XB + 4 * 64, lanes("XW0", 64, 192))
+    emit("s", lambda: S.activation(T.UCp[:, 0:256], T.QUp[:, 0:128].indirect(T.UO[:, 0:16]), F.Copy), [("QU", 0, 128), ("UO", 0, 16)], [("UCs", 0, 256)])
+    act(("EB2", 0, 516), ("EB", 0, 516), 1.0 / 64, 0.0)
+    emit("v", lambda: V.tensor_copy(T.UCc[:, 0:256].bitcast(dt.uint32), T.QUc[:, 0:128].bitcast(dt.uint32).indirect(T.UO[:, 0:16])),
+         [("QU", 0, 128), ("UO", 0, 16)], [("UC", 0, 256)])
+
+    dst = T.cores[(rank - 1) % len(T.cores)]
+    rid, pid = topo.addr(dst)[:2]
+    mask = topo.mask(core, dst)
+    lands = 2 * len(topo.engines(core, dst))
+
+    def e_tile(b):
+        return ("E", 128 * b, 1.0 / 64) if b < 2 else ("EH", 128 * b - 256, 1.0)
+
+    for t in range(R):
+        last = t == R - 1
+        XW, QX, QM, QB = "XW%d" % t, "QX%d" % t, "QM%d" % t, "QB%d" % t
+        NX = "XW%d" % (t + 1)
+        if t == 0:
+            pre("t", [("UCs", 0, 256)], [])
+        else:
+            quant(QM, 0, 128, XW, XB + 4 * 64, lanes(XW, 64, 192))
+        mm(5, 128, "UC", 128, QM, 0)
+        mm(4, 128, "UC", 0, QM, 0)
+        if t > 0:
+            for a in (0, 192):
+                gather("v", T[XW][:, XB + 4 * a + 1:XB + 4 * a + 256:4], T.YS[:, C:2 * C], T.LO[:, a // 16:a // 16 + 4],
+                       [("YS", C, 2 * C), ("LO", 0, 16)], [(XW + "#1", a, a + 64)])
+        emit("v", lambda: V.tensor_tensor_scan(ap(cut("PK", 0, 17)), T.p5[:, 0:17], ap(cut("NEG", 0, 17)), -1.0e29, A.max, A.max),
+             [("p5", 0, 512), reg("NEG")], [cut("PK", 0, 17)])
+        emit("v", lambda: V.tensor_tensor_scan(ap(cut("PC", 0, 65)), T.p4[:, 32:97], ap(cut("NEG", 0, 65)), -1.0e29, A.max, A.max),
+             [("p4", 0, 512), reg("NEG")], [cut("PC", 0, 65)])
+        ts(cut("MK", 0, 17), cut("PK", 0, 17), cut("PK", 16, 17), 4.0, A.is_lt, A.mult)
+        ts(cut("MC", 0, 65), cut("PC", 0, 65), cut("PC", 64, 65), 4.0, A.is_lt, A.mult)
+        emit("v", lambda: V.tensor_reduce(ap(reg("K4")), ap(cut("MK", 0, 18)), AxisListType.X, A.add), [cut("MK", 0, 18)], [reg("K4")])
+        emit("v", lambda: V.tensor_reduce(ap(reg("C4")), ap(cut("MC", 0, 66)), AxisListType.X, A.add), [cut("MC", 0, 66)], [reg("C4")])
+        act("k2", "K4", 0.5, 0.0)
+        act("c", "C4", 0.25, "QT")
+        ts("mk", "ZQ", "K4", -2.0, A.is_gt, A.mult)
+        ts(("LB1", 0, 16), "I1", "C4", "K4", A.add, A.subtract)
+        ts("f", "K4", 2.0, "C4", A.mult, A.is_lt)
+        ts("w1", "mk", "K4", "K4", A.mult, A.add)
+        act("cpk", "K4", 0.25, "c")
+        ts("m", "mk", "f", 1.0, A.mult, A.add)
+        tt("r0", "ZQ", "w1", A.subtract)
+        ts("x2", "J", "c", "k2", A.is_ge, A.mult)
+        tt("r", "r0", "m", A.mult)
+        ts("x3", "J", "cpk", "k2", A.is_ge, A.mult)
+        ts(("LB2", 0, 8), "r", "C4", float(XB), A.add, A.add)
+        tt("y2", "x2", "x3", A.subtract)
+        allx = lanes(XW, -PAD, C + PAD)
+        gather("s", T.BT[:, 0:256], T[XW][:, 0:XWID], T.LB1[:, 0:16], allx + [("LB1", 0, 16)], lanes("BT", 0, 64))
+        gather("v", T.BT[:, 256:384], T[XW][:, 0:XWID], T.LB2[:, 0:8], allx + [("LB2", 0, 8)], lanes("BT", 64, 96))
+        quant(QB, 0, 128, "BT", 0, lanes("BT", 0, 128))
+        pre("g", [(QB, 0, 96)], [])
+        g.remote_dma(out_ap=T[QX + "c"][:, C:AWID].bitcast(dt.uint8), in_ap=T[QB + "c"][:, 0:K].bitcast(dt.uint8),
+                     remote_sem=T.sem["arr%d" % t], local_sem=T.sem["loc%d" % t], pid=pid, routing_id=rid, dma_engine_mask=mask)
+        g.remote_dma(out_ap=T[QX + "p"][:, C:AWID], in_ap=T[QB + "p"][:, 0:K],
+                     remote_sem=T.sem["arr%d" % t], local_sem=T.sem["loc%d" % t], pid=pid, routing_id=rid, dma_engine_mask=mask)
+        count["arr%d" % t] = lands
+        count["loc%d" % t] = lands
+        note("remote", QX, C, AWID, True, ("arr%d" % t, lands))
+        act("n3", "K4", -0.25, "c")
+        act("c2", "c", 2.0, -256.5)
+        act("rl", "k2", -1.0, "c", F.Relu)
+        act("n2", "cpk", -1.0, 256.0)
+        act("bn", "n3", BIG, 0.0)
+        act("kb", "K4", 0.25, -128.25)
+        act("Rr", "J", -1.0, "c2")
+        act("x1", "J", -BIG, "bn", F.Relu)
+        act("l3", "J", 0.5, "kb")
+        act("tau", "cpk", 2.0, -256.0)
+        act("rho", "rl", 1.0, "k2")
+        act("nkw", "K4", -0.5, -255.5)
+        act("bt", "tau", -BIG, BIG)
+        act("br", "rho", BIG, 0.0)
+        act("nch", "c", -1.0, 0.5)
+        act("o2", "J", BIG, "bt", F.Relu)
+        act("o1", "J", -BIG, "br", F.Relu)
+        act("w", "J", 1.0, "nkw")
+        act("ae", "J", 1.0, "nch", F.Abs)
+        act("nk", "K4", -0.25, 0.0)
+        act("k", "K4", 0.25, 0.0)
+        act("ay", "ae", 1.0, "nk", F.Abs)
+        act("km1", "K4", 0.25, -1.0)
+        quant(QX, 0, C, XW, XB, lanes(XW, 0, C))
+        if t == 0:
+            for b in (0, 1):
+                quant("E", 128 * b, 128, "EB", 4 - b, [("EB", 0, 516)])
+            for b in (2, 3):
+                quant("EH", 128 * b - 256, 128, "EB2", 4 - b, [("EB2", 0, 516)])
+        for b in range(4):
+            e, ea, sc = e_tile(b)
+            mm(b, C, e, ea, QX, 0)
+            psum_copy("s", "AW", AWID * b, b, 0, C, sc)
+            if b < 2:
+                emit("g", lambda: g.affine_select(T.FH[:, C * b:C * b + C], T.AW[:, AWID * b:AWID * b + C], [[1, C]], A.is_ge, 0.0, 0, 0),
+                     [("AW", AWID * b, AWID * b + C)], [("FH", C * b, C * b + C)])
+        if t == 0:
+            ts("J1", "J", -1.0, None, A.add)
+            ts("H1", "J", 0.25, -0.375, A.mult, A.add)
+        ts("a", "n2", "n3", None, A.min)
+        tt("y1", "Rr", "x1", A.add)
+        ts("l2", "J1", "a", 1.0 / 3, A.subtract, A.mult)
+        ts("l4", "J", "k2", "a", A.subtract, A.subtract)
+        tt("v", "y1", "y2", A.add)
+        tt("m1", "l2", "l3", A.max)
+        tt("m2", "l4", "H1", A.max)
+        ts("v0", "v", -0.5, BIG, A.is_gt, A.mult)
+        ts("v1", "v", -255.75, BIG, A.is_lt, A.mult)
+        tt(("ZI", 0, 16), "m1", "m2", A.max)
+        z = ("ZI", 0, 16)
+        tt("v2", "v0", "v1", A.add)
+        tt("o3", "o1", "o2", A.add)
+        ts("t2", z, "n2", None, A.min)
+        tt("v3", "v2", "v", A.add)
+        tt("o4", "o3", "w", A.add)
+        ts("t3", z, "n3", None, A.min)
+        tt("mn", "o4", "ay", A.min)
+        ts("t1", z, "km1", 2.0, A.min, A.mult)
+        tt("mm", "v3", "mn", A.min)
+        tt("u", "t2", "t3", A.add)
+        ts(("LC", 0, 16), "mm", 255.5, None, A.add)
+        tt("N", "u", "t1", A.add)
+        ts("zk", z, "k", 0.5, A.subtract, A.add)
+        tt("I", "J", "N", A.subtract)
+        ts("zl", z, "n2", 1.0, A.is_lt, A.add)
+        ts("mo", "I", 2.0, 2.0, A.is_ge, A.mult)
+        ts("ti", "I", -2.0, 1.0, A.mult, A.add)
+        tt("xx", "mo", "zl", A.mult)
+        ts("km", "mo", "k", None, A.mult)
+        tt("gg", "ti", "xx", A.add)
+        if t == 0:
+            for b in (2, 3):
+                quant("E", 128 * b, 128, "EB", 4 - b, [("EB", 0, 516)])
+        for b in (0, 2, 1, 3):
+            e, ea, sc = e_tile(b)
+            mm(4 + b, 128, e, ea, QX, AWID - 128)
+        for b in (2, 3):
+            psum_copy("s", "AW", AWID * b + C, 4 + b, 128 - K, 128, 1.0)
+        for b in (2, 3):
+            gather("s", T.AS[:, C * b - 2 * C:C * b - C], T.AW[:, AWID * b:AWID * b + AWID], T.LC[:, 0:16],
+                   [("AW", AWID * b, AWID * b + AWID), ("LC", 0, 16)], [("AS", C * b - 2 * C, C * b - C)])
+        for b in (0, 1):
+            psum_copy("v", "AW", AWID * b + C, 4 + b, 128 - K, 128, 1.0 / 64)
+        for b in (0, 1):
+            w = T.AW[:, AWID * b:AWID * b + AWID]
+            emit("v", lambda: V.tensor_tensor(T.ZT[:, b:4 * C:4], w.indirect(T.LC[:, 0:16]), T.FH[:, C * b:C * b + C], A.add),
+                 [("AW", AWID * b, AWID * b + AWID), ("FH", C * b, C * b + C), ("LC", 0, 16)], [("ZT#%d" % b, 0, C)])
+        for b in (2, 3):
+            emit("v", lambda: V.tensor_tensor(T.ZT[:, b:4 * C:4], T.AS[:, C * b - 2 * C:C * b - C], T["p%d" % b][:, 0:C], A.add),
+                 [("AS", C * b - 2 * C, C * b - C), ("p%d" % b, 0, 512)], [("ZT#%d" % b, 0, C)])
+        tt("D", "zk", "km", A.add)
+        quant("QZ", 0, C, "ZT", 0, lanes("ZT", 0, C))
+        for b in (0, 2, 1, 3):
+            mm(4 + b, C, "E", 128 * b, QX, 0, True, False)
+        if t == 0:
+            pre("t", [("Ws", 0, 512)], [])
+        for b in range(4):
+            mm(4 + b, C, "W", 128 * b, "QZ", 0, False, True)
+        tt("gD", "gg", "D", A.mult)
+        ts(("LO", 0, 16), "gD", "c", -0.5, A.add, A.add)
+
+        def page(q, b, a, n):
+            gather(q, T[NX][:, XB + 4 * a + b:XB + 4 * a + 4 * n:4], T.YS[:, C * b:C * b + C], T.LO[:, a // 16:(a + n) // 16],
+                   [("YS", C * b, C * b + C), ("LO", 0, 16)], [(NX + "#%d" % b, a, a + n)])
+        for b in range(4):
+            psum_copy("sv"[b % 2], "YS", C * b, 4 + b, 0, C, 0.03125)
+        for b in range(4):
+            page("sv"[b % 2], b, 0 if last else 64, C if last else 128)
+        if not last:
+            for b in (0, 2, 3):
+                page("s", b, 0, 64)
+                page("s", b, 192, 64)
+    XW, QX = "XW%d" % R, "QX%d" % R
+    quant("QV", 0, 128, "VT", 0, [("VT", 0, 512)])
+    for h in range(2):
+        quant(QX, 128 * h, 128, XW, XB + 512 * h, lanes(XW, 128 * h, 128 * h + 128))
+    for h in range(2):
+        mm(h, 128, "QV", 0, QX, 128 * h)
+        psum_copy("v", "YO", 128 * h, h, 0, 128, 1.0)
+    gather("s", T.LOF[:, 0:C], T.PLACE[:, 0:C], T.LO[:, 0:16], [("PLACE", 0, C), ("LO", 0, 16)], [("LOF", 0, C)])
+    dma("y", "oc", T.oc[:, 0:4 * C], T[QX + "c"][:, 0:C].bitcast(dt.uint8), [(QX, 0, C)], [])
+    dma("s", "lo", T.lo[:, 0:C], T.LOF[0:128:16, 0:C], [("LOF", 0, C)], [])
+    for i in range(4):
+        dma("yyss"[i], "os%d" % i, T.osc[4 * i:4 * i + 4, 0:C], T[QX + "p"][32 * i:32 * i + 4, 0:C], [(QX, 0, C)], [])
+    for h in range(2):
+        dma("y", "y%d" % h, T.y[:, 128 * h:128 * h + 128], T.YO[:, 128 * h:128 * h + 128], [("YO", 128 * h, 128 * h + 128)], [])
+    for sem in sorted(count, key=lambda s: (s[0] == "d", s)):
+        if waited.get(sem, 0) < count[sem]:
+            wait("g", (sem, count[sem]))

@@ -1,35 +1,35 @@
 from concourse.mybir import dt, AluOpType as A, AxisListType, ActivationFunctionType as F
 
 R, C, K = 3, 256, 96
-PAD = 80
+PAD = 48
 XWID = 4 * (C + 2 * PAD)
 XB = 4 * PAD
 AWID = C + K
-BIG = 1000.0
+BIG = 4096.0
+SA, SB = 64, 176
 
 WORK = {}
 _n = [0]
-for _name, _w in (("NEG", 72), ("PC", 72), ("PK", 24), ("MC", 72), ("MK", 24), ("C4", 1), ("K4", 1), ("S15", 1), ("T3", 1),
-                  ("QT", 1), ("J", 16), ("J1", 16), ("H1", 16), ("I1", 16), ("ZQ", 8),
-                  ("mk", 8), ("f", 1), ("w1", 8), ("r0", 8), ("m", 8), ("r", 8),
-                  ("c", 1), ("k", 1), ("n3", 1), ("n2", 1), ("cpk", 1), ("k2", 1), ("c2", 1), ("tau", 1), ("kb", 1), ("km1", 1),
-                  ("nch", 1), ("nk", 1), ("nkw", 1), ("rl", 1), ("rho", 1), ("br", 1), ("bt", 1), ("bn", 1), ("a", 1),
-                  ("Rr", 16), ("ae", 16), ("ay", 16), ("w", 16),
-                  ("x1", 16), ("x2", 16), ("x3", 16), ("y1", 16), ("y2", 16), ("v", 16), ("v0", 16), ("v1", 16), ("v2", 16),
-                  ("v3", 16), ("o1", 16), ("o2", 16), ("o3", 16), ("o4", 16), ("mn", 16), ("mm", 16),
-                  ("l2", 16), ("l3", 16), ("l4", 16), ("m1", 16), ("m2", 16), ("t1", 16), ("t2", 16), ("t3", 16), ("u", 16),
-                  ("N", 16), ("I", 16), ("mo", 16), ("zl", 16), ("xx", 16), ("ti", 16),
-                  ("gg", 16), ("km", 16), ("zk", 16), ("D", 16), ("gD", 16)):
-    WORK[_name] = (_n[0], _w)
-    _n[0] += -(-_w // 8) * 8
+for _name, _w, _m in (("NEG", 72, 1), ("PC", 72, 1), ("PK", 24, 1), ("MC", 72, 1), ("MK", 24, 1), ("C4", 1, 1), ("K4", 1, 1), ("sg", 1, 1),
+                      ("PB", 5, 1), ("NB", 5, 1), ("M16", 16, 1), ("M8", 32, 1), ("J32", 32, 1), ("Z0", 8, 1), ("cb32", 1, 1), ("J", 16, 1),
+                      ("I1", 16, 1), ("Z", 8, 1), ("Z2", 8, 1), ("B0", 8, 2), ("B1", 8, 2), ("BO", 8, 2),
+                      ("J4h", 16, 1), ("Jq", 16, 1), ("NK", 16, 1), ("nthr", 1, 1), ("thr", 1, 1), ("ae", 16, 1),
+                      ("D0", 16, 3), ("D1", 16, 3), ("DO", 16, 3), ("pm", 16, 1), ("dh", 16, 1), ("E0", 16, 2), ("E1", 16, 2), ("EO", 16, 2),
+                      ("ac4", 1, 1), ("s", 1, 1), ("K4m", 1, 1), ("cm", 1, 1),
+                      ("JO32", 32, 1), ("J4O32", 32, 1), ("L032", 32, 2), ("L132", 32, 2), ("LM32", 32, 2), ("Et32", 32, 1), ("gt32", 32, 1),
+                      ("Dt32", 32, 1), ("gD32", 32, 1),
+                      ("JO16", 16, 1), ("J4O16", 16, 1), ("L016", 16, 2), ("L116", 16, 2), ("LM16", 16, 2), ("Et16", 16, 1), ("gt16", 16, 1),
+                      ("Dt16", 16, 1), ("gD16", 16, 1)):
+    WORK[_name] = (_n[0], _w, _m)
+    _n[0] += -(-_w * _m // 8) * 8
 
 SCRATCH = {
     "wk": ("sbuf", [128, _n[0]], "float32"),
-    "IP": ("sbuf", [128, 1], "int32"), "M16": ("sbuf", [128, 16], "int32"), "UI": ("sbuf", [128, 16], "int32"),
-    "I15": ("sbuf", [128, 1], "int32"), "I3": ("sbuf", [128, 1], "int32"), "ZI": ("sbuf", [128, 16], "int32"),
+    "IP": ("sbuf", [128, 1], "int32"), "IB": ("sbuf", [128, 8], "int32"), "UI": ("sbuf", [128, 16], "int32"),
+    "NI": ("sbuf", [128, 32], "int32"), "PI": ("sbuf", [128, 32], "int32"), "HI": ("sbuf", [128, 32], "int32"),
     "PLACE": ("sbuf", [128, C], "float32"), "LOF": ("sbuf", [128, C], "float32"), "YO": ("sbuf", [128, C], "float32"),
     "UO": ("sbuf", [128, 16], "uint16"), "LB1": ("sbuf", [128, 16], "uint16"), "LB2": ("sbuf", [128, 8], "uint16"),
-    "LC": ("sbuf", [128, 16], "uint16"), "LO": ("sbuf", [128, 16], "uint16"),
+    "LC": ("sbuf", [128, 16], "uint16"), "LO": ("sbuf", [128, 32], "uint16"),
     "ONE": ("sbuf", [128, 516], "bfloat16"), "EB": ("sbuf", [128, 516], "bfloat16"), "EB2": ("sbuf", [128, 516], "bfloat16"),
     "UT": ("sbuf", [128, 512], "bfloat16"), "VT": ("sbuf", [128, 512], "bfloat16"), "BT": ("sbuf", [128, 512], "bfloat16"),
     "ZT": ("sbuf", [128, 4 * C], "bfloat16"), "YS": ("sbuf", [128, 4 * C], "bfloat16"), "AW": ("sbuf", [128, 4 * AWID], "bfloat16"),
@@ -39,7 +39,7 @@ for _name, _w in (("E", 512), ("EH", 256), ("QU", 128), ("UC", 256), ("QV", 128)
                   ("QM2", 128), ("QX0", AWID), ("QX1", AWID), ("QX2", AWID), ("QX3", C), ("QB0", 128), ("QB1", 128), ("QB2", 128)):
     SCRATCH[_name + "c"] = ("sbuf", [128, _w], "float8_e4m3fn_x4")
     SCRATCH[_name + "p"] = ("sbuf", [128, _w], "uint8")
-for _t in range(R + 1):
+for _t in range(2):
     SCRATCH["XW%d" % _t] = ("sbuf", [128, XWID], "bfloat16")
 for _b in range(8):
     SCRATCH["p%d" % _b] = ("psum", [128, 512], "float32")
@@ -120,48 +120,54 @@ def rank_program(g, core, T, topo):
         for r in wr:
             note(sem, r[0], r[1], r[2], True, ev)
 
-    def reg(n):
-        return ("wk", WORK[n][0], WORK[n][0] + WORK[n][1])
+    def opd(x):
+        if isinstance(x, str):
+            name, _, slot = x.partition("#")
+            a, w, m = WORK[name]
+            if slot:
+                return T.wk[:, a + int(slot):a + w * m:m], [(x, 0, w)]
+            return T.wk[:, a:a + w * m], [(x, 0, w)] if m == 1 else [("%s#%d" % (x, i), 0, w) for i in range(m)]
+        if x[0] in WORK:
+            a = WORK[x[0]][0]
+            return T.wk[:, a + x[1]:a + x[2]], [x]
+        return T[x[0]][:, x[1]:x[2]], [x]
 
-    def cut(n, a, b):
-        return ("wk", WORK[n][0] + a, WORK[n][0] + b)
+    def call(q, fn, out, *ins):
+        o, wr = opd(out)
+        rd, args = [], []
+        for x in ins:
+            if isinstance(x, (str, tuple)):
+                x, r = opd(x)
+                rd += r
+            args.append(x)
+        emit(q, lambda: fn(o, *args), rd, wr)
 
-    def norm(x):
-        return reg(x) if isinstance(x, str) else x
-
-    def ap(x):
-        return T[x[0]][:, x[1]:x[2]]
-
-    def lanes(name, a, b):
-        return [(name + "#%d" % i, a, b) for i in range(4)]
+    def lanes(name, a, b, which=range(4)):
+        return [(name + "#%d" % i, a, b) for i in which]
 
     def ts(out, in0, s1, s2, op0, op1=None):
-        out, in0 = norm(out), norm(in0)
-        rd = [in0]
-        sc = []
-        for s in (s1, s2):
-            if isinstance(s, (str, tuple)):
-                s = norm(s)
-                rd.append(s)
-                s = ap(s)
-            sc.append(s)
         if op1 is None:
-            emit("v", lambda: V.tensor_scalar(ap(out), ap(in0), sc[0], None, op0), rd, [out])
+            call("v", lambda o, x, a: V.tensor_scalar(o, x, a, None, op0), out, in0, s1)
         else:
-            emit("v", lambda: V.tensor_scalar(ap(out), ap(in0), sc[0], sc[1], op0, op1), rd, [out])
+            call("v", lambda o, x, a, b: V.tensor_scalar(o, x, a, b, op0, op1), out, in0, s1, s2)
 
     def tt(out, x, y, op):
-        out, x, y = norm(out), norm(x), norm(y)
-        emit("v", lambda: V.tensor_tensor(ap(out), ap(x), ap(y), op), [x, y], [out])
+        call("v", lambda o, a, b: V.tensor_tensor(o, a, b, op), out, x, y)
+
+    def scan(out, x, y, op0, op1, first=0.0):
+        call("v", lambda o, a, b: V.tensor_tensor_scan(o, a, b, first, op0, op1), out, x, y)
+
+    def total(out, x):
+        call("v", lambda o, a: V.tensor_reduce(o, a, AxisListType.X, A.add), out, x)
+
+    def copy(out, x):
+        call("v", V.tensor_copy, out, x)
+
+    def fill(out, val):
+        call("v", lambda o: V.memset(o, val), out)
 
     def act(out, x, scale, bias, func=F.Identity):
-        out, x = norm(out), norm(x)
-        rd = [x]
-        if isinstance(bias, (str, tuple)):
-            bias = norm(bias)
-            rd.append(bias)
-            bias = ap(bias)
-        emit("s", lambda: S.activation(ap(out), ap(x), func, bias=bias, scale=scale), rd, [out])
+        call("s", lambda o, a, sc, bi: S.activation(o, a, func, bias=bi, scale=sc), out, x, scale, bias)
 
     def quant(dst, a, n, src, sa, rd):
         emit("v", lambda: V.quantize_mx(T[dst + "c"][:, a:a + n], T[dst + "p"][:, a:a + n], T[src][:, sa:sa + 4 * n]), rd, [(dst, a, a + n)])
@@ -171,8 +177,8 @@ def rank_program(g, core, T, topo):
                                       T[mv + "c"][:, ma:ma + n], T[mv + "p"][:, ma:ma + n], start, stop),
              [(st, sa, sa + 128), (mv, ma, ma + n)], [("p%d" % bank, 0, 512)])
 
-    def fill(name, a, b, val, wr=None):
-        emit("v", lambda: V.memset(T[name][:, a:b], val), [], wr or [(name, a, b)])
+    def zeros(name, a, b):
+        emit("v", lambda: V.memset(T[name][:, XB + 4 * a:XB + 4 * b], 0.0), [], lanes(name, a, b))
 
     def psum_copy(q, out, oa, bank, a, b, scale):
         rd, wr = [("p%d" % bank, 0, 512)], [(out, oa, oa + b - a)]
@@ -188,44 +194,71 @@ def rank_program(g, core, T, topo):
         else:
             emit("s", lambda: S.activation(out, win.indirect(off), F.Copy), rd, wr)
 
+    def psum_scan(out, bank, a, n):
+        emit("v", lambda: V.tensor_tensor_scan(opd((out, 0, n))[0], T["p%d" % bank][:, a:a + n], opd(("NEG", 0, n))[0], -1.0e29, A.max, A.max),
+             [("p%d" % bank, 0, 512), ("NEG", 0, 72)], [(out, 0, n)])
+
+    dma("s", "u", T.UT[:, 0:512], T.u[:, 0:512], [], [("UT", 0, 512)])
     for name, a, b in (("xm", 64, 192), ("xa", 0, 64), ("xb", 192, 256)):
         dma("y", name, T.XW0[:, XB + 4 * a:XB + 4 * b], T.x[:, 4 * a:4 * b], [], lanes("XW0", a, b))
-    dma("s", "u", T.UT[:, 0:512], T.u[:, 0:512], [], [("UT", 0, 512)])
     dma("y", "wc", T.Wc[:, 0:512].bitcast(dt.uint8), T.wc[:, 0:2048], [], [("W", 0, 512)])
     dma("y", "ws", T.Wp[:, 0:512], T.ws[:, 0:512], [], [("Ws", 0, 512)])
     dma("y", "v", T.VT[:, 0:512], T.v[:, 0:512], [], [("VT", 0, 512)])
 
-    fill("ONE", 0, 516, 32.0)
-    emit("g", lambda: g.iota(T.UI[:, 0:16], [[1, 2], [16, 8]], 0, 0), [], [("UI", 0, 16)])
-    emit("g", lambda: g.iota(T.IP[:, 0:1], [[1, 1]], 0, 1), [], [("IP", 0, 1)])
-    emit("g", lambda: g.iota(T.M16[:, 0:16], [[16, 16]], 0, 0), [], [("M16", 0, 16)])
+    def iota(out, pattern, step=0):
+        call("g", lambda o: g.iota(o, pattern, 0, step, allow_small_or_imprecise_dtypes=True), out)
+
+    def const(out, n, val):
+        act(out, ("ONE", 0, n), 0.0, val)
+    fill(("ONE", 0, 516), 32.0)
+    iota(("IP", 0, 1), [[1, 1]], 1)
+    iota(("UI", 0, 16), [[1, 2], [16, 8]])
+    iota("M16", [[16, 16]])
+    iota("M8", [[8, 32]])
     emit("g", lambda: g.affine_select(T.EB[:, 0:516], T.ONE[:, 0:516], [[-1, 516]], A.is_equal, 0.0, 4, 4), [("ONE", 0, 516)], [("EB", 0, 516)])
-    emit("g", lambda: g.iota(T.PLACE[:, 0:C], [[1, C]], 0, 0, allow_small_or_imprecise_dtypes=True), [], [("PLACE", 0, C)])
-    fill("XW0", 0, XB, 0.0, lanes("XW0", -PAD, 0))
-    fill("wk", WORK["NEG"][0], WORK["NEG"][0] + 72, -1.0e29)
-    fill("wk", WORK["MK"][0] + 17, WORK["MK"][0] + 18, 256.0)
-    fill("BT", 384, 512, 0.0, lanes("BT", 96, 128))
-    emit("v", lambda: V.tensor_copy(T.UO[:, 0:16], T.UI[:, 0:16]), [("UI", 0, 16)], [("UO", 0, 16)])
-    ts(("I15", 0, 1), ("IP", 0, 1), 15, None, A.bitwise_and)
-    ts(("I3", 0, 1), ("IP", 0, 1), 3, None, A.bitwise_and)
-    emit("v", lambda: V.tensor_copy(ap(reg("S15")), T.I15[:, 0:1]), [("I15", 0, 1)], [reg("S15")])
-    emit("v", lambda: V.tensor_copy(ap(reg("T3")), T.I3[:, 0:1]), [("I3", 0, 1)], [reg("T3")])
-    ts("J", ("M16", 0, 16), "S15", None, A.add)
-    ts(cut("MC", 65, 66), "T3", 382.0, None, A.add)
-    ts("QT", "T3", -0.25, 0.5, A.mult, A.add)
-    ts("I1", "J", "T3", 322.0, A.subtract, A.add)
-    ts("ZQ", cut("J", 0, 8), "T3", 258.0, A.subtract, A.add)
-    fill("XW0", XB + 4 * C, XWID, 0.0, lanes("XW0", C, C + PAD))
-    for i in (1, 2):
-        for a in (0, XB + 4 * C):
-            j = -PAD if a == 0 else C
-            emit("s", lambda: S.activation(T["XW%d" % i][:, a:a + XB], T.XW0[:, 0:XB], F.Copy), lanes("XW0", -PAD, 0), lanes("XW%d" % i, j, j + PAD))
+    iota(("PLACE", 0, C), [[1, C]])
+    ts(("IB", 0, 1), ("IP", 0, 1), 15, None, A.bitwise_and)
+    ts(("IB", 1, 2), ("IP", 0, 1), 3, None, A.bitwise_and)
+    ts(("IB", 2, 3), ("IP", 0, 1), 1, None, A.bitwise_and)
+    ts(("IB", 3, 4), ("IP", 0, 1), 1, 7, A.arith_shift_right, A.bitwise_and)
+    ts(("IB", 4, 5), ("IP", 0, 1), 1, 1, A.arith_shift_right, A.bitwise_and)
+    copy(("UO", 0, 16), ("UI", 0, 16))
+    copy("PB", ("IB", 0, 5))
+    zeros("XW0", -PAD, 0)
+    ts("NB", "PB", -1.0, None, A.mult)
+    zeros("XW0", C, C + PAD)
+    emit("v", lambda: V.memset(T.BT[:, 384:512], 0.0), [], lanes("BT", 96, 128))
+    const("NEG", 72, -1.0e29)
+    const(("MK", 17, 18), 1, 256.0)
+    const(("MC", 65, 66), 1, -640.0)
+    const("B0#0", 8, 0.0)
+    const("NK", 16, -1.0 / 512)
+    const("D0#0", 16, -BIG)
+    const("D1#2", 16, -BIG)
+    const("E0#0", 16, BIG)
+    act("J", "M16", 1.0, ("PB", 0, 1))
+    act("J32", "M8", 1.0, ("PB", 3, 4))
+    act("Z0", ("J", 0, 8), 1.0, ("NB", 1, 2))
+    act("I1", "J", 1.0, XB + 1024.0)
+    act("B1#1", ("J", 0, 8), 1.0, XB + 1280.0)
+    act("Z", "Z0", 1.0, 258.0)
+    act("Z2", "Z0", 2.0, 516.0)
     quant("QU", 0, 128, "UT", 0, [("UT", 0, 512)])
-    quant("QM0", 0, 128, "XW0", XB + 4 * 64, lanes("XW0", 64, 192))
     emit("s", lambda: S.activation(T.UCp[:, 0:256], T.QUp[:, 0:128].indirect(T.UO[:, 0:16]), F.Copy), [("QU", 0, 128), ("UO", 0, 16)], [("UCs", 0, 256)])
-    act(("EB2", 0, 516), ("EB", 0, 516), 1.0 / 64, 0.0)
     emit("v", lambda: V.tensor_copy(T.UCc[:, 0:256].bitcast(dt.uint32), T.QUc[:, 0:128].bitcast(dt.uint32).indirect(T.UO[:, 0:16])),
          [("QU", 0, 128), ("UO", 0, 16)], [("UC", 0, 256)])
+    quant("QM0", 0, 128, "XW0", XB + 4 * 64, lanes("XW0", 64, 192))
+    act("J4h", "J", 4.0, -1022.0)
+    act("Jq", "J", 1.0 / 256, 0.5 / 256 - 1.0)
+
+    def order_constants(w, j, odd):
+        act("JO" + w, j, 1.0, 512.0)
+        act("J4O" + w, j, 4.0, 2.5)
+        act("L1" + w + "#0", j, 2.0, odd)
+    order_constants("32", "J32", ("NB", 4, 5))
+    act("cb32", ("PB", 2, 3), 256.0, 255.625)
+    for a, b in ((-PAD, 0), (C, C + PAD), (SB, 192)):
+        emit("s", lambda: S.activation(T.XW1[:, XB + 4 * a:XB + 4 * b], T.ONE[:, 0:4 * (b - a)], F.Copy, scale=0.0), [("ONE", 0, 516)], lanes("XW1", a, b))
 
     dst = T.cores[(rank - 1) % len(T.cores)]
     rid, pid = topo.addr(dst)[:2]
@@ -235,10 +268,19 @@ def rank_program(g, core, T, topo):
     def e_tile(b):
         return ("E", 128 * b, 1.0 / 64) if b < 2 else ("EH", 128 * b - 256, 1.0)
 
+    def pages(q, name, h, a, b):
+        gather(q, T[name][:, XB + 4 * a + h:XB + 4 * b:2], T.YS[:, 2 * C * h:2 * C * h + 2 * C], T.LO[:, a // 8:b // 8],
+               [("YS", 2 * C * h, 2 * C * h + 2 * C), ("LO", 0, 32)], lanes(name, a, b, (h, h + 2)))
+
+    def ys(b):
+        return C * (2 * (b % 2) + b // 2)
+
     for t in range(R):
         last = t == R - 1
-        XW, QX, QM, QB = "XW%d" % t, "QX%d" % t, "QM%d" % t, "QB%d" % t
-        NX = "XW%d" % (t + 1)
+        XW, QX, QM, QB = "XW%d" % (t % 2), "QX%d" % t, "QM%d" % t, "QB%d" % t
+        NX = "XW%d" % ((t + 1) % 2)
+        n = 16 if last else 32
+        w = str(n)
         if t == 0:
             pre("t", [("UCs", 0, 256)], [])
         else:
@@ -246,31 +288,25 @@ def rank_program(g, core, T, topo):
         mm(5, 128, "UC", 128, QM, 0)
         mm(4, 128, "UC", 0, QM, 0)
         if t > 0:
-            for a in (0, 192):
-                gather("v", T[XW][:, XB + 4 * a + 1:XB + 4 * a + 256:4], T.YS[:, C:2 * C], T.LO[:, a // 16:a // 16 + 4],
-                       [("YS", C, 2 * C), ("LO", 0, 16)], [(XW + "#1", a, a + 64)])
-        emit("v", lambda: V.tensor_tensor_scan(ap(cut("PK", 0, 17)), T.p5[:, 0:17], ap(cut("NEG", 0, 17)), -1.0e29, A.max, A.max),
-             [("p5", 0, 512), reg("NEG")], [cut("PK", 0, 17)])
-        emit("v", lambda: V.tensor_tensor_scan(ap(cut("PC", 0, 65)), T.p4[:, 32:97], ap(cut("NEG", 0, 65)), -1.0e29, A.max, A.max),
-             [("p4", 0, 512), reg("NEG")], [cut("PC", 0, 65)])
-        ts(cut("MK", 0, 17), cut("PK", 0, 17), cut("PK", 16, 17), 4.0, A.is_lt, A.mult)
-        ts(cut("MC", 0, 65), cut("PC", 0, 65), cut("PC", 64, 65), 4.0, A.is_lt, A.mult)
-        emit("v", lambda: V.tensor_reduce(ap(reg("K4")), ap(cut("MK", 0, 18)), AxisListType.X, A.add), [cut("MK", 0, 18)], [reg("K4")])
-        emit("v", lambda: V.tensor_reduce(ap(reg("C4")), ap(cut("MC", 0, 66)), AxisListType.X, A.add), [cut("MC", 0, 66)], [reg("C4")])
-        act("k2", "K4", 0.5, 0.0)
-        act("c", "C4", 0.25, "QT")
-        ts("mk", "ZQ", "K4", -2.0, A.is_gt, A.mult)
+            pages("s", XW, 0, 0, SA)
+            pages("v", XW, 1, 0, SA)
+            pages("s", XW, 0, SB, C)
+            pages("s", XW, 1, SB, C)
+        psum_scan("PK", 5, 0, 17)
+        psum_scan("PC", 4, 32, 65)
+        ts(("MK", 0, 17), ("PK", 0, 17), ("PK", 16, 17), 4.0, A.is_lt, A.mult)
+        ts(("MC", 0, 65), ("PC", 0, 65), ("PC", 64, 65), 4.0, A.is_lt, A.mult)
+        total("K4", ("MK", 0, 18))
+        total("C4", ("MC", 0, 66))
+        ts("sg", ("PC", 32, 33), ("PC", 64, 65), 0.5, A.is_ge, A.subtract)
         ts(("LB1", 0, 16), "I1", "C4", "K4", A.add, A.subtract)
-        ts("f", "K4", 2.0, "C4", A.mult, A.is_lt)
-        ts("w1", "mk", "K4", "K4", A.mult, A.add)
-        act("cpk", "K4", 0.25, "c")
-        ts("m", "mk", "f", 1.0, A.mult, A.add)
-        tt("r0", "ZQ", "w1", A.subtract)
-        ts("x2", "J", "c", "k2", A.is_ge, A.mult)
-        tt("r", "r0", "m", A.mult)
-        ts("x3", "J", "cpk", "k2", A.is_ge, A.mult)
-        ts(("LB2", 0, 8), "r", "C4", float(XB), A.add, A.add)
-        tt("y2", "x2", "x3", A.subtract)
+        ts("B1#0", "Z2", "sg", "K4", A.mult, A.min)
+        ts("B0#1", "Z", "K4", 2.0, A.is_gt, A.mult)
+        ts("L0" + w + "#0", "JO" + w, "K4", None, A.subtract)
+        scan("BO", "B0", "B1", A.mult, A.add)
+        ts("K4m", "K4", -1.0, None, A.add)
+        ts(("LB2", 0, 8), "BO#1", "C4", "K4", A.add, A.subtract)
+        ts("thr", "C4", -1.0 / 1024, None, A.mult)
         allx = lanes(XW, -PAD, C + PAD)
         gather("s", T.BT[:, 0:256], T[XW][:, 0:XWID], T.LB1[:, 0:16], allx + [("LB1", 0, 16)], lanes("BT", 0, 64))
         gather("v", T.BT[:, 256:384], T[XW][:, 0:XWID], T.LB2[:, 0:8], allx + [("LB2", 0, 8)], lanes("BT", 64, 96))
@@ -283,97 +319,79 @@ def rank_program(g, core, T, topo):
         count["arr%d" % t] = lands
         count["loc%d" % t] = lands
         note("remote", QX, C, AWID, True, ("arr%d" % t, lands))
-        act("n3", "K4", -0.25, "c")
-        act("c2", "c", 2.0, -256.5)
-        act("rl", "k2", -1.0, "c", F.Relu)
-        act("n2", "cpk", -1.0, 256.0)
-        act("bn", "n3", BIG, 0.0)
-        act("kb", "K4", 0.25, -128.25)
-        act("Rr", "J", -1.0, "c2")
-        act("x1", "J", -BIG, "bn", F.Relu)
-        act("l3", "J", 0.5, "kb")
-        act("tau", "cpk", 2.0, -256.0)
-        act("rho", "rl", 1.0, "k2")
-        act("nkw", "K4", -0.5, -255.5)
-        act("bt", "tau", -BIG, BIG)
-        act("br", "rho", BIG, 0.0)
-        act("nch", "c", -1.0, 0.5)
-        act("o2", "J", BIG, "bt", F.Relu)
-        act("o1", "J", -BIG, "br", F.Relu)
-        act("w", "J", 1.0, "nkw")
-        act("ae", "J", 1.0, "nch", F.Abs)
-        act("nk", "K4", -0.25, 0.0)
-        act("k", "K4", 0.25, 0.0)
-        act("ay", "ae", 1.0, "nk", F.Abs)
-        act("km1", "K4", 0.25, -1.0)
         quant(QX, 0, C, XW, XB, lanes(XW, 0, C))
+        act("ae", "J4h", -1.0, "C4", F.Abs)
+        act("nthr", "C4", 1.0 / 1024, 0.0)
+        act("D0#1", "J4h", -1.0, "C4", F.Sign)
+        act("D1#0", "ae", -1.0, "K4", F.Sign)
+        act("D0#2", "Jq", -1.0, "nthr")
+        act("D1#1", "NK", "K4", 0.0)
+        act("ac4", "C4", 1.0, 512.5, F.Abs)
+        act("E1#1", "ae", -1.0, "K4", F.Abs)
+        act("s", "K4", -2.0, "ac4")
         if t == 0:
             for b in (0, 1):
                 quant("E", 128 * b, 128, "EB", 4 - b, [("EB", 0, 516)])
+            ts(("EB2", 0, 516), ("EB", 0, 516), 1.0 / 64, None, A.mult)
+            quant("E", 256, 128, "EB", 2, [("EB", 0, 516)])
             for b in (2, 3):
                 quant("EH", 128 * b - 256, 128, "EB2", 4 - b, [("EB2", 0, 516)])
+        act("cm", "C4", 0.25, 255.625 if last else "cb32")
+        act("L1" + w + "#1", "J4O" + w, 1.0, "s")
         for b in range(4):
             e, ea, sc = e_tile(b)
             mm(b, C, e, ea, QX, 0)
-            psum_copy("s", "AW", AWID * b, b, 0, C, sc)
+
+        def f_copy(q, b):
+            psum_copy(q, "AW", AWID * b, b, 0, C, e_tile(b)[2])
             if b < 2:
                 emit("g", lambda: g.affine_select(T.FH[:, C * b:C * b + C], T.AW[:, AWID * b:AWID * b + C], [[1, C]], A.is_ge, 0.0, 0, 0),
                      [("AW", AWID * b, AWID * b + C)], [("FH", C * b, C * b + C)])
+        f_copy("s", 0)
+        act("L0" + w + "#1", "L1" + w + "#1", 1.0 / 3, 1024.0 / 3 - 1.0)
+        f_copy("s", 1)
+        f_copy("s", 2)
+        scan("DO", "D0", "D1", A.subtract, A.max)
+        ts("pm", "DO#2", "thr", 0.5, A.is_le, A.subtract)
+        tt("dh", "DO#2", "pm", A.mult)
+        scan("LM" + w, "L0" + w, "L1" + w, A.max, A.max)
+        ts("E1#0", "dh", 2048.0, "C4", A.mult, A.add)
+        copy(("NI", 0, n), "LM" + w + "#1")
+        ts("E0#1", "E1#0", -1024.0, BIG, A.is_lt, A.mult)
+        ts(("HI", 0, n), ("NI", 0, n), 2, None, A.bitwise_and)
+        scan("EO", "E0", "E1", A.add, A.min)
+        ts(("PI", 0, n), ("NI", 0, n), 1, None, A.bitwise_and)
+        ts(("LC", 0, 16), "EO#1", 0.25, 255.5, A.mult, A.add)
+        f_copy("v", 3)
         if t == 0:
-            ts("J1", "J", -1.0, None, A.add)
-            ts("H1", "J", 0.25, -0.375, A.mult, A.add)
-        ts("a", "n2", "n3", None, A.min)
-        tt("y1", "Rr", "x1", A.add)
-        ts("l2", "J1", "a", 1.0 / 3, A.subtract, A.mult)
-        ts("l4", "J", "k2", "a", A.subtract, A.subtract)
-        tt("v", "y1", "y2", A.add)
-        tt("m1", "l2", "l3", A.max)
-        tt("m2", "l4", "H1", A.max)
-        ts("v0", "v", -0.5, BIG, A.is_gt, A.mult)
-        ts("v1", "v", -255.75, BIG, A.is_lt, A.mult)
-        tt(("ZI", 0, 16), "m1", "m2", A.max)
-        z = ("ZI", 0, 16)
-        tt("v2", "v0", "v1", A.add)
-        tt("o3", "o1", "o2", A.add)
-        ts("t2", z, "n2", None, A.min)
-        tt("v3", "v2", "v", A.add)
-        tt("o4", "o3", "w", A.add)
-        ts("t3", z, "n3", None, A.min)
-        tt("mn", "o4", "ay", A.min)
-        ts("t1", z, "km1", 2.0, A.min, A.mult)
-        tt("mm", "v3", "mn", A.min)
-        tt("u", "t2", "t3", A.add)
-        ts(("LC", 0, 16), "mm", 255.5, None, A.add)
-        tt("N", "u", "t1", A.add)
-        ts("zk", z, "k", 0.5, A.subtract, A.add)
-        tt("I", "J", "N", A.subtract)
-        ts("zl", z, "n2", 1.0, A.is_lt, A.add)
-        ts("mo", "I", 2.0, 2.0, A.is_ge, A.mult)
-        ts("ti", "I", -2.0, 1.0, A.mult, A.add)
-        tt("xx", "mo", "zl", A.mult)
-        ts("km", "mo", "k", None, A.mult)
-        tt("gg", "ti", "xx", A.add)
-        if t == 0:
-            for b in (2, 3):
-                quant("E", 128 * b, 128, "EB", 4 - b, [("EB", 0, 516)])
+            quant("E", 384, 128, "EB", 1, [("EB", 0, 516)])
+        if t == 1:
+            quant("QV", 0, 128, "VT", 0, [("VT", 0, 512)])
         for b in (0, 2, 1, 3):
             e, ea, sc = e_tile(b)
             mm(4 + b, 128, e, ea, QX, AWID - 128)
-        for b in (2, 3):
-            psum_copy("s", "AW", AWID * b + C, 4 + b, 128 - K, 128, 1.0)
-        for b in (2, 3):
+
+        def g_copy(q, b):
+            psum_copy(q, "AW", AWID * b + C, 4 + b, 128 - K, 128, e_tile(b)[2])
+
+        def a_gather(b):
             gather("s", T.AS[:, C * b - 2 * C:C * b - C], T.AW[:, AWID * b:AWID * b + AWID], T.LC[:, 0:16],
                    [("AW", AWID * b, AWID * b + AWID), ("LC", 0, 16)], [("AS", C * b - 2 * C, C * b - C)])
+        g_copy("v", 0)
+        g_copy("s", 2)
+        g_copy("s", 1)
+        g_copy("s", 3)
+        a_gather(2)
         for b in (0, 1):
-            psum_copy("v", "AW", AWID * b + C, 4 + b, 128 - K, 128, 1.0 / 64)
-        for b in (0, 1):
-            w = T.AW[:, AWID * b:AWID * b + AWID]
-            emit("v", lambda: V.tensor_tensor(T.ZT[:, b:4 * C:4], w.indirect(T.LC[:, 0:16]), T.FH[:, C * b:C * b + C], A.add),
+            win = T.AW[:, AWID * b:AWID * b + AWID]
+            emit("v", lambda: V.tensor_tensor(T.ZT[:, b:4 * C:4], win.indirect(T.LC[:, 0:16]), T.FH[:, C * b:C * b + C], A.add),
                  [("AW", AWID * b, AWID * b + AWID), ("FH", C * b, C * b + C), ("LC", 0, 16)], [("ZT#%d" % b, 0, C)])
+        a_gather(3)
+        if t == 0:
+            order_constants("16", "J", ("NB", 2, 3))
         for b in (2, 3):
             emit("v", lambda: V.tensor_tensor(T.ZT[:, b:4 * C:4], T.AS[:, C * b - 2 * C:C * b - C], T["p%d" % b][:, 0:C], A.add),
                  [("AS", C * b - 2 * C, C * b - C), ("p%d" % b, 0, 512)], [("ZT#%d" % b, 0, C)])
-        tt("D", "zk", "km", A.add)
         quant("QZ", 0, C, "ZT", 0, lanes("ZT", 0, C))
         for b in (0, 2, 1, 3):
             mm(4 + b, C, "E", 128 * b, QX, 0, True, False)
@@ -381,28 +399,33 @@ def rank_program(g, core, T, topo):
             pre("t", [("Ws", 0, 512)], [])
         for b in range(4):
             mm(4 + b, C, "W", 128 * b, "QZ", 0, False, True)
-        tt("gD", "gg", "D", A.mult)
-        ts(("LO", 0, 16), "gD", "c", -0.5, A.add, A.add)
-
-        def page(q, b, a, n):
-            gather(q, T[NX][:, XB + 4 * a + b:XB + 4 * a + 4 * n:4], T.YS[:, C * b:C * b + C], T.LO[:, a // 16:(a + n) // 16],
-                   [("YS", C * b, C * b + C), ("LO", 0, 16)], [(NX + "#%d" % b, a, a + n)])
+        ts("Et" + w, ("HI", 0, n), "K4m", -510.5, A.mult, A.add)
+        ts("gt" + w, ("PI", 0, n), -0.5, 0.25, A.mult, A.add)
+        tt("Dt" + w, "Et" + w, ("NI", 0, n), A.add)
+        tt("gD" + w, "Dt" + w, "gt" + w, A.mult)
+        ts(("LO", 0, n), "gD" + w, "cm", None, A.add)
         for b in range(4):
-            psum_copy("sv"[b % 2], "YS", C * b, 4 + b, 0, C, 0.03125)
-        for b in range(4):
-            page("sv"[b % 2], b, 0 if last else 64, C if last else 128)
+            psum_copy("sv"[b % 2], "YS", ys(b), 4 + b, 0, C, 0.03125)
         if not last:
-            for b in (0, 2, 3):
-                page("s", b, 0, 64)
-                page("s", b, 192, 64)
-    XW, QX = "XW%d" % R, "QX%d" % R
-    quant("QV", 0, 128, "VT", 0, [("VT", 0, 512)])
-    for h in range(2):
-        quant(QX, 128 * h, 128, XW, XB + 512 * h, lanes(XW, 128 * h, 128 * h + 128))
+            pages("s", NX, 0, SA, SB)
+            pages("v", NX, 1, SA, SB)
+    XW, QX = "XW%d" % (R % 2), "QX%d" % R
+
+    def page(q, b, a):
+        gather(q, T[XW][:, XB + 4 * a + b:XB + 4 * a + 512:4], T.YS[:, ys(b):ys(b) + C], T.LO[:, a // 16:a // 16 + 8],
+               [("YS", ys(b), ys(b) + C), ("LO", 0, 32)], [(XW + "#%d" % b, a, a + 128)])
+    for b in range(4):
+        page("sv"[b % 2], b, 0)
+    page("s", 0, 128)
+    page("s", 2, 128)
+    quant(QX, 0, 128, XW, XB, lanes(XW, 0, 128))
+    page("v", 1, 128)
+    page("v", 3, 128)
+    quant(QX, 128, 128, XW, XB + 512, lanes(XW, 128, 256))
+    gather("s", T.LOF[:, 0:C], T.PLACE[:, 0:C], T.LO[:, 0:16], [("PLACE", 0, C), ("LO", 0, 32)], [("LOF", 0, C)])
     for h in range(2):
         mm(h, 128, "QV", 0, QX, 128 * h)
         psum_copy("v", "YO", 128 * h, h, 0, 128, 1.0)
-    gather("s", T.LOF[:, 0:C], T.PLACE[:, 0:C], T.LO[:, 0:16], [("PLACE", 0, C), ("LO", 0, 16)], [("LOF", 0, C)])
     dma("y", "oc", T.oc[:, 0:4 * C], T[QX + "c"][:, 0:C].bitcast(dt.uint8), [(QX, 0, C)], [])
     dma("s", "lo", T.lo[:, 0:C], T.LOF[0:128:16, 0:C], [("LOF", 0, C)], [])
     for i in range(4):

@@ -7,19 +7,39 @@ XB = 4 * PAD
 AWID = C + K
 BIG = 4096.0
 SA, SB = 64, 176
+NS = 14
+ORDER = """
+ad_u:s ad_xm:y aIP:g aM16:g ad_xa:y ad_xb:y ad_wc:y ad_ws:y ad_v:y aONE:v aEB:v aEBd:g 0NK:s aIB:v aIB2:v aIB1:v aIB4:v aJ4h32:s 0E0#0:s aCS1:s
+0NK32:s aIB3:v aUI:g aMK17:v aPB:v aCS:s aE0:v aB0#0:s aJ16:v 0XW1_224:s aMC65:s aCS2:s 0D0#0:s aNEG:s aNB:s aUO:v 0D1#2:s aEB2:s aQU:v aM8:g aJ:v
+aUs1:s aUs0:s aZ0:s aB1#1:s aUc1:v aUc0:v aQM:v aXW0_0:v 0H3:v 0S1:t aZ:s 0PK:v 0S0:t 0PC:v aJq:s aZ2:s aJO:s aJ4h:s 0MK:v 0sg:v aI1:s aXW0_304:s
+0K4:v 0MC:v aBT0:s 0B0#1:v 0B1#0:v 0C4:v 0BO:v 0LB:v 0cs:s 0LB16:v 0Ba:s 0ae:s 0D0#2:s 0D1#0:s 0Bb:v 0D1#1:s 0J4O:v 0s:s 0QB:v 0QX:v 0D0#1:s 0E2:v
+0DO:v 0F0:t 0L0#0:s 0F3:t 0E1:v 0L1#1:s 0pm:v 0F2:t 0cb:s 0L1#0:v 0dh:v 0L0#1:v 0f0:s 0H1:v 0E1#0:s 0E1#1:s 0XW1_0:v 0LM:v 0E0#1:v 0B>:g 0lcb:s 0X10:t
+0F1:t 0K4m:s 0f3:s 0f2:s 0NI:v 0h2:s 0EO:v 0HI:v 0X12:t 0PI:v 0f1:s 0gt:v 0h0:g 0XW1_304:v 0G0:t 0g0:s 0Et:v 0G2:t 0G1:t 0LC:v 0G3:t 0E3:v 0g1:s
+0X00:t 0g2:v 0Dt:v 0g3:s 0X02:t 0zz0:v 0A0:s 0z03:v 0X01:t 0A1:s 0X03:t 0z01:v 0gD:v 0QZ0:v 0z11:v 0W01:t 0y01:s 0W00:t 0z13:v 0QZ1:v 0W03:t 0W02:t
+0y00:s 0y02:s 0X11:t 0X13:t 0W10:t 0y10:s 0W11:t 0LO:v 0y03:v 0W12:t 0W13:t 0y11:v 0y13:v 0y12:s 0pg0_64:s 0pg1_64:v 1pg0_0:s 1QM:v 1pg1_176:s 1S1:t
+1PK:v 1S0:t 1PC:v 1pg0_176:s 1MK:v 1sg:v 1K4:v 1D1#1:s 1MC:v 1B1#0:v 1B0#1:v 1pg1_0:s 1C4:v 1BO:v 1LB:v 1D0#1:s 1cs:s 1LB16:v 1Bb:v 1Ba:s 1D0#2:v
+1ae:s 1QB:v 1D1#0:s 1L0#0:s 1E1#1:s 1QX:v 1F0:t 1DO:v 1K4m:v 1s:s 1pm:v 1F2:t 1L1#1:s 1L0#1:s 1f0:s 1dh:v 1LM:v 1E1#0:v 1B>:g 1F1:t 1F3:t 1NI:v 1f2:s
+1f1:s 1G2:t 1E0#1:v 1G3:t 1HI:v 1EO:v 1g2:s 1Et:v 1G0:t 1G1:t 1h0:g 1LC:v 1X10:t 1X02:t 1h2:v 1g0:v 1g3:s 1X03:t 1PI:v 1zz0:v 1X12:t 1g1:s 1f3:s 1A0:s
+1z03:v 1z01:v 1Dt:v 1X00:t 1X01:t 1QZ0:v 1W00:t 1A1:s 1W03:t 1W02:t 1W01:t 1z11:v 1X11:t 1y00:s 1z13:v 1gt:v 1X13:t 1QZ1:v 1y02:s 1W10:t 1W11:t 1y01:s
+1y03:s 1gD:v 1LO:v 1y10:s 1W12:t 1y12:s 1W13:t 1pg0_64:s 1y11:v 2pg0_0:s 1y13:v 1pg1_64:v 2QM:v 2pg1_0:s 1QV:v 2S1:t 2PK:v 2S0:t 2PC:v 2MK:v
+2pg1_176:s 2sg:v 2K4:v 2pg0_176:s 2MC:v 2B0#1:v 2B1#0:v 2C4:v 2ae:s 2BO:v 2LB:v 2Ba:s 2LB16:v 2Bb:v 2cs:v 2D1#1:s 2QB:v 2QX:v 2F0:t 2F2:t 2s:s 2D0#1:s
+2B>:g 2D0#2:s 2D1#0:s 2F1:t 2L0#0:s 2F3:t 2DO:v 2K4m:s 2pm:v 2L1#1:s 2L0#1:s 2G0:t 2E1#1:s 2G3:t 2dh:v 2LM:v 2E1#0:v 2NI:v 2E0#1:v 2HI:v 2f0:s 2f2:s
+2f1:s 2EO:v 2G2:t 2PI:v 2LC:v 2h0:g 2g0:s 2G1:t 2g3:s 2X10:t 2h2:v 2g2:v 2X00:t 2f3:s 2X12:t 2g1:s 2X03:t 2Et:v 2X02:t 2A0:s 2zz0:v 2A1:s 2z01:v
+2z03:v 2X01:t 2Dt:v 2QZ0:v 2W00:t 2z11:v 2z13:v 2X11:t 2W02:t 2W01:t 2gt:v 2QZ1:v 2y00:s 2W03:t 2X13:t 2gD:v 2W10:t 2y02:s 2W11:t 2y01:s 2W12:t 2y10:s
+2y12:s 2OF:v 2LO:v 2y03:s 2y11:v 2W13:t 2y13:v zpg0_0:s 2OT:v zOC:s zpg1_0:v zd_lo0:y zQX0:v zV0:t zd_lo1:y zd_oc0:y zpg1_128:v zpg0_128:s zQX1:v
+zy0:s zd_y0:s zV1:t zd_os3:y zd_oc1:s zd_os1:y zd_os2:y zd_os0:s zy1:s zd_y1:y
+"""
 
 WORK = {}
 _n = [0]
 for _name, _w, _m in (("NEG", 72, 1), ("PC", 72, 1), ("PK", 24, 1), ("MC", 72, 1), ("MK", 24, 1), ("C4", 1, 1), ("K4", 1, 1), ("sg", 1, 1),
-                      ("PB", 5, 1), ("NB", 5, 1), ("M16", 16, 1), ("M8", 32, 1), ("J32", 32, 1), ("Z0", 8, 1), ("cb32", 1, 1), ("J", 16, 1),
+                      ("PB", 5, 1), ("NB", 5, 1), ("M16", 16, 1), ("M8", 32, 1), ("J", 32, 1), ("Z0", 8, 1), ("cb", 1, 1), ("J16", 16, 1),
                       ("I1", 16, 1), ("Z", 8, 1), ("Z2", 8, 1), ("B0", 8, 2), ("B1", 8, 2), ("BO", 8, 2),
-                      ("J4h", 16, 1), ("Jq", 16, 1), ("NK", 16, 1), ("nthr", 1, 1), ("thr", 1, 1), ("ae", 16, 1),
-                      ("D0", 16, 3), ("D1", 16, 3), ("DO", 16, 3), ("pm", 16, 1), ("dh", 16, 1), ("E0", 16, 2), ("E1", 16, 2), ("EO", 16, 2),
-                      ("ac4", 1, 1), ("s", 1, 1), ("K4m", 1, 1), ("cm", 1, 1),
-                      ("JO32", 32, 1), ("J4O32", 32, 1), ("L032", 32, 2), ("L132", 32, 2), ("LM32", 32, 2), ("Et32", 32, 1), ("gt32", 32, 1),
-                      ("Dt32", 32, 1), ("gD32", 32, 1),
-                      ("JO16", 16, 1), ("J4O16", 16, 1), ("L016", 16, 2), ("L116", 16, 2), ("LM16", 16, 2), ("Et16", 16, 1), ("gt16", 16, 1),
-                      ("Dt16", 16, 1), ("gD16", 16, 1)):
+                      ("J4h", 33, 1), ("Jq", 32, 1), ("NK", 33, 1), ("CS", 3, 1), ("cs", 3, 1), ("ae", 33, 1), ("lcb", 1, 1),
+                      ("D0", 32, 3), ("D1", 33, 3), ("DO", 32, 3), ("pm", 32, 1), ("dh", 32, 1), ("E0", 32, 2), ("E1", 32, 2), ("EO", 32, 2),
+                      ("s", 1, 1), ("K4m", 1, 1),
+                      ("JO", 32, 1), ("J4O", 32, 1), ("L0", 32, 2), ("L1", 32, 2), ("LM", 32, 2), ("Et", 32, 1), ("gt", 32, 1),
+                      ("Dt", 32, 1), ("gD", 32, 1), ("OF", 32, 1), ("OT", 16, 2), ("OC", 16, 1)):
     WORK[_name] = (_n[0], _w, _m)
     _n[0] += -(-_w * _m // 8) * 8
 
@@ -27,10 +47,10 @@ SCRATCH = {
     "wk": ("sbuf", [128, _n[0]], "float32"),
     "IP": ("sbuf", [128, 1], "int32"), "IB": ("sbuf", [128, 8], "int32"), "UI": ("sbuf", [128, 16], "int32"),
     "NI": ("sbuf", [128, 32], "int32"), "PI": ("sbuf", [128, 32], "int32"), "HI": ("sbuf", [128, 32], "int32"),
-    "PLACE": ("sbuf", [128, C], "float32"), "LOF": ("sbuf", [128, C], "float32"), "YO": ("sbuf", [128, C], "float32"),
-    "UO": ("sbuf", [128, 16], "uint16"), "LB1": ("sbuf", [128, 16], "uint16"), "LB2": ("sbuf", [128, 8], "uint16"),
-    "LC": ("sbuf", [128, 16], "uint16"), "LO": ("sbuf", [128, 32], "uint16"),
-    "ONE": ("sbuf", [128, 516], "bfloat16"), "EB": ("sbuf", [128, 516], "bfloat16"), "EB2": ("sbuf", [128, 516], "bfloat16"),
+    "YO": ("sbuf", [128, C], "float32"),
+    "UO": ("sbuf", [128, 16], "uint16"), "LB": ("sbuf", [128, 24], "uint16"),
+    "LC": ("sbuf", [128, 32], "uint16"), "LO": ("sbuf", [128, 32], "uint16"),
+    "ONE": ("sbuf", [128, 192], "bfloat16"), "EB": ("sbuf", [128, 516], "bfloat16"), "EB2": ("sbuf", [128, 516], "bfloat16"),
     "UT": ("sbuf", [128, 512], "bfloat16"), "VT": ("sbuf", [128, 512], "bfloat16"), "BT": ("sbuf", [128, 512], "bfloat16"),
     "ZT": ("sbuf", [128, 4 * C], "bfloat16"), "YS": ("sbuf", [128, 4 * C], "bfloat16"), "AW": ("sbuf", [128, 4 * AWID], "bfloat16"),
     "FH": ("sbuf", [128, 2 * C], "bfloat16"), "AS": ("sbuf", [128, 2 * C], "bfloat16"),
@@ -44,16 +64,354 @@ for _t in range(2):
 for _b in range(8):
     SCRATCH["p%d" % _b] = ("psum", [128, 512], "float32")
 LOADS = ["xm", "xa", "xb", "u", "v", "wc", "ws"]
-STORES = ["oc", "os0", "os1", "os2", "os3", "y0", "y1", "lo"]
+STORES = ["oc0", "oc1", "os0", "os1", "os2", "os3", "y0", "y1", "lo0", "lo1"]
 SEMAPHORES = ["cv", "cs", "ct", "cg"] + ["d_" + n for n in LOADS + STORES] + ["arr%d" % t for t in range(R)] + ["loc%d" % t for t in range(R)]
 
 
-def rank_program(g, core, T, topo):
+def plan(g, core, T, topo):
     rank = T.rank_of(core)
-    if rank is None:
+    V, S, P = g.vector, g.scalar, g.tensor
+    queue = {"v": V, "s": S, "t": P, "g": g, "y": g.sync}
+    steps = {}
+    part = ["a"]
+
+    def step(name, qs, fn, rd, wr, kind="c"):
+        name = part[0] + name
+        assert name not in steps
+        steps[name] = (kind, qs, fn, rd, wr)
+
+    def dma(qs, name, out, in_, rd, wr):
+        step("d_" + name, qs, lambda q: queue[q].dma_start(out, in_), rd, wr, "d_" + name)
+
+    def opd(x):
+        if isinstance(x, str):
+            name, _, slot = x.partition("#")
+            a, w, m = WORK[name]
+            if slot:
+                return T.wk[:, a + int(slot):a + w * m:m], [(x, 0, w)]
+            return T.wk[:, a:a + w * m], [(x, 0, w)] if m == 1 else [("%s#%d" % (x, i), 0, w) for i in range(m)]
+        if x[0] in WORK:
+            a, w, m = WORK[x[0]]
+            return T.wk[:, a + x[1]:a + x[2]], [x] if m == 1 else [("%s#%d" % (x[0], i), 0, w) for i in range(m) if x[2] - x[1] > 1 or x[1] % m == i]
+        return T[x[0]][:, x[1]:x[2]], [x]
+
+    def call(qs, fn, out, *ins):
+        o, wr = opd(out)
+        rd, args = [], []
+        for x in ins:
+            if isinstance(x, (str, tuple)):
+                x, r = opd(x)
+                rd += r
+            args.append(x)
+        step(out if isinstance(out, str) else out[0] + str(out[1] or ""), qs, lambda q: fn(q, o, *args), rd, wr)
+
+    def lanes(name, a, b, which=range(4)):
+        return [(name + "#%d" % i, a, b) for i in which]
+
+    def ts(out, in0, s1, s2, op0, op1=None):
+        if op1 is None:
+            call("v", lambda q, o, x, a: V.tensor_scalar(o, x, a, None, op0), out, in0, s1)
+        else:
+            call("v", lambda q, o, x, a, b: V.tensor_scalar(o, x, a, b, op0, op1), out, in0, s1, s2)
+
+    def tt(out, x, y, op):
+        call("v", lambda q, o, a, b: V.tensor_tensor(o, a, b, op), out, x, y)
+
+    def scan(out, x, y, op0, op1, first=0.0):
+        call("v", lambda q, o, a, b: V.tensor_tensor_scan(o, a, b, first, op0, op1), out, x, y)
+
+    def total(out, x):
+        call("v", lambda q, o, a: V.tensor_reduce(o, a, AxisListType.X, A.add), out, x)
+
+    def copy(out, x):
+        call("v", lambda q, o, a: V.tensor_copy(o, a), out, x)
+
+    def act(out, x, scale, bias, func):
+        call("s", lambda q, o, a, sc, bi: S.activation(o, a, func, bias=bi, scale=sc), out, x, scale, bias)
+
+    def times_plus(q, o, a, sc, bi):
+        return V.tensor_scalar(o, a, sc, bi, A.mult, A.add) if q == "v" else S.activation(o, a, F.Identity, bias=bi, scale=sc)
+
+    def lin(qs, out, x, scale, bias):
+        call(qs, times_plus, out, x, scale, bias)
+
+    def scaled(name, qs, to, src, sc, rd, wr):
+        step(name, qs, lambda q: V.tensor_scalar(to, src, sc, None, A.mult) if q == "v" else S.activation(to, src, F.Copy, scale=sc), rd, wr)
+
+    def quant(name, dst, a, n, src, sa, rd):
+        step(name, "v", lambda q: V.quantize_mx(T[dst + "c"][:, a:a + n], T[dst + "p"][:, a:a + n], T[src][:, sa:sa + 4 * n]), rd, [(dst, a, a + n)])
+
+    def mm(name, bank, n, st, sa, mv, ma, start=True, stop=True):
+        step(name, "t", lambda q: P.matmul_mx(T["p%d" % bank][:, 0:n], T[st + "c"][:, sa:sa + 128], T[st + "p"][:, sa:sa + 128],
+                                              T[mv + "c"][:, ma:ma + n], T[mv + "p"][:, ma:ma + n], start, stop),
+             [(st, sa, sa + 128), (st + "s", sa, sa + 128), (mv, ma, ma + n)], [("p%d" % bank, 0, 512)])
+
+    def zeros(name, a, b):
+        scaled("%s_%d" % (name, a + PAD), "sv", T[name][:, XB + 4 * a:XB + 4 * b], T.ONE[:, 0:4 * (b - a)], 0.0, [("ONE", 0, 192)], lanes(name, a, b))
+
+    def psum_copy(name, qs, out, oa, bank, n, scale):
+        scaled(name, qs, T[out][:, oa:oa + n], T["p%d" % bank][:, 0:n], scale, [("p%d" % bank, 0, 512)], [(out, oa, oa + n)])
+
+    def gather(name, qs, out, win, off, rd, wr):
+        step(name, qs, lambda q: V.tensor_copy(out, win.indirect(off)) if q == "v" else S.activation(out, win.indirect(off), F.Copy), rd, wr)
+
+    def psum_scan(out, bank, a, n):
+        step(out, "v", lambda q: V.tensor_tensor_scan(opd((out, 0, n))[0], T["p%d" % bank][:, a:a + n], opd(("NEG", 0, n))[0], -1.0e29, A.max, A.max),
+             [("p%d" % bank, 0, 512), ("NEG", 0, 72)], [(out, 0, n)])
+
+    dma("s", "u", T.UT[:, 0:512], T.u[:, 0:512], [], [("UT", 0, 512)])
+    for name, a, b in (("xm", 64, 192), ("xa", 0, 64), ("xb", 192, 256)):
+        dma("y", name, T.XW0[:, XB + 4 * a:XB + 4 * b], T.x[:, 4 * a:4 * b], [], lanes("XW0", a, b))
+    dma("y", "wc", T.Wc[:, 0:512].bitcast(dt.uint8), T.wc[:, 0:2048], [], [("W", 0, 512)])
+    dma("y", "ws", T.Wp[:, 0:512], T.ws[:, 0:512], [], [("Ws", 0, 512)])
+    dma("y", "v", T.VT[:, 0:512], T.v[:, 0:512], [], [("VT", 0, 512)])
+
+    def iota(out, pattern, step=0):
+        call("g", lambda q, o: g.iota(o, pattern, 0, step, allow_small_or_imprecise_dtypes=True), out)
+
+    def const(out, n, val):
+        lin("sv", out, ("ONE", 0, n), 0.0, val)
+    call("v", lambda q, o: V.memset(o, 32.0), ("ONE", 0, 192))
+    call("v", lambda q, o: V.memset(o, 0.0), ("EB", 0, 516))
+    iota(("IP", 0, 1), [[1, 1]], 1)
+    iota(("UI", 0, 16), [[1, 2], [16, 8]])
+    step("EBd", "g", lambda q: g.affine_select(T.EB[:, 4:516:4], T.ONE[:, 0:128], [[-1, 128]], A.is_equal, 0.0, 0, 1), [("ONE", 0, 192)], [("EB", 0, 516)])
+    iota("M16", [[16, 16]])
+    iota("M8", [[8, 32]])
+    ts(("IB", 0, 1), ("IP", 0, 1), 15, None, A.bitwise_and)
+    ts(("IB", 1, 2), ("IP", 0, 1), 3, None, A.bitwise_and)
+    ts(("IB", 2, 3), ("IP", 0, 1), 1, None, A.bitwise_and)
+    ts(("IB", 3, 4), ("IP", 0, 1), 1, 7, A.arith_shift_right, A.bitwise_and)
+    ts(("IB", 4, 5), ("IP", 0, 1), 1, 1, A.arith_shift_right, A.bitwise_and)
+    copy(("UO", 0, 16), ("UI", 0, 16))
+    copy("PB", ("IB", 0, 5))
+    scaled("BT0", "vs", T.BT[:, 384:512], T.ONE[:, 0:128], 0.0, [("ONE", 0, 192)], lanes("BT", 96, 128))
+    lin("vs", "NB", "PB", -1.0, 0.0)
+    const("NEG", 72, -1.0e29)
+    const(("MK", 17, 18), 1, 256.0)
+    const(("MC", 65, 66), 1, -640.0)
+    const("B0#0", 8, 0.0)
+    zeros("XW0", -PAD, 0)
+    zeros("XW0", C, C + PAD)
+    scaled("EB2", "sv", T.EB2[:, 0:516], T.EB[:, 0:516], 1.0 / 64, [("EB", 0, 516)], [("EB2", 0, 516)])
+    quant("QU", "QU", 0, 128, "UT", 0, [("UT", 0, 512)])
+
+    def pick(h):
+        off = T.UO[:, 8 * h:8 * h + 8]
+        gather("Us%d" % h, "s", T.UCp[:, 128 * h:128 * h + 128], T.QUp[:, 0:128], off, [("QU", 0, 128), ("UO", 0, 16)], [("UCs", 128 * h, 128 * h + 128)])
+        gather("Uc%d" % h, "v", T.UCc[:, 128 * h:128 * h + 128].bitcast(dt.uint32), T.QUc[:, 0:128].bitcast(dt.uint32), off,
+               [("QU", 0, 128), ("UO", 0, 16)], [("UC", 128 * h, 128 * h + 128)])
+
+    def e_quant(name, b):
+        if name == "E":
+            quant("E%d" % b, "E", 128 * b, 128, "EB", 4 - b, [("EB", 0, 516)])
+        else:
+            quant("H%d" % b, "EH", 64 * b - 64, 128, "EB2", 4 - b, [("EB2", 0, 516)])
+    pick(1)
+    quant("QM", "QM0", 0, 128, "XW0", XB + 4 * 64, lanes("XW0", 64, 192))
+    pick(0)
+    e_quant("E", 0)
+    lin("sv", "J16", "M16", 1.0, ("PB", 0, 1))
+    lin("sv", "J", "M8", 1.0, ("PB", 3, 4))
+    lin("sv", "Z0", ("J16", 0, 8), 1.0, ("NB", 1, 2))
+    lin("sv", "I1", "J16", 1.0, XB + 1024.0)
+    lin("sv", "B1#1", ("J16", 0, 8), 1.0, XB + 1280.0)
+    lin("sv", "Z2", "Z0", 2.0, 516.0)
+    lin("sv", "Z", "Z0", 1.0, 258.0)
+    lin("sv", "JO", "J", 1.0, 512.0)
+    lin("sv", ("J4h", 0, 32), "J", 4.0, -1022.0)
+    const(("J4h", 32, 33), 1, -512.5)
+    for i, val in enumerate((1.0 / 1024, -1.0 / 1024, 0.25)):
+        const(("CS", i, i + 1), 1, val)
+    lin("sv", "Jq", "J", 1.0 / 256, 0.5 / 256 - 1.0)
+
+    def list_constants():
+        const(("NK", 0, 32), 32, -1.0 / 512)
+        const(("NK", 32, 33), 1, -1.0)
+        const("D0#0", 32, -BIG)
+        const("D1#2", 33, -BIG)
+        lin("sv", "J4O", "J", 4.0, 2.5)
+        lin("sv", "L1#0", "J", 2.0, ("NB", 4, 5))
+        const("E0#0", 32, BIG)
+        lin("sv", "cb", ("PB", 2, 3), float(C), 255.625)
+        lin("sv", "lcb", ("PB", 2, 3), 1.0, 511.0)
+
+    dst = T.cores[(rank - 1) % len(T.cores)]
+    rid, pid = topo.addr(dst)[:2]
+    mask = topo.mask(core, dst)
+
+    def e_tile(b):
+        return ("E", 128 * b, 1.0 / 64) if b % 2 == 0 else ("EH", 64 * b - 64, 1.0)
+
+    def pages(qs, name, h, a, b):
+        gather("pg%d_%d" % (h, a), qs, T[name][:, XB + 4 * a + h:XB + 4 * b:2], T.YS[:, 2 * C * h:2 * C * h + 2 * C], T.LO[:, a // 8:b // 8],
+               [("YS", 2 * C * h, 2 * C * h + 2 * C), ("LO", 0, 32)], lanes(name, a, b, (h, h + 2)))
+
+    def window_copy(name, qs, b, bank, a, n, at):
+        w0 = 2 * AWID * (b % 2) + b // 2 + 2 * at
+        scaled(name, qs, T.AW[:, w0:w0 + 2 * n - 1:2], T["p%d" % bank][:, a:a + n], e_tile(b)[2], [("p%d" % bank, 0, 512)], lanes("AW", at, at + n, (b,)))
+
+    def send(t, QB, QX):
+        def fn(q):
+            g.remote_dma(out_ap=T[QX + "c"][:, C:AWID].bitcast(dt.uint8), in_ap=T[QB + "c"][:, 0:K].bitcast(dt.uint8),
+                         remote_sem=T.sem["arr%d" % t], local_sem=T.sem["loc%d" % t], pid=pid, routing_id=rid, dma_engine_mask=mask)
+            g.remote_dma(out_ap=T[QX + "p"][:, C:AWID], in_ap=T[QB + "p"][:, 0:K],
+                         remote_sem=T.sem["arr%d" % t], local_sem=T.sem["loc%d" % t], pid=pid, routing_id=rid, dma_engine_mask=mask)
+            return 2 * len(topo.engines(core, dst))
+        step("B>", "g", fn, [(QB, 0, K)], [(QX, C, AWID)], "arr%d" % t)
+
+    def add(h, b):
+        a = 128 * h
+        step("z%d%d" % (h, b), "v",
+             lambda q: V.tensor_tensor(T.ZT[:, 4 * a + b:4 * a + 512:4], T.AS[:, 2 * a + b // 2:2 * a + 256:2], T["p%d" % b][:, a:a + 128], A.add),
+             [("AS", 2 * a, 2 * a + 256), ("p%d" % b, 0, 512)], lanes("ZT", a, a + 128, (b,)))
+
+    def gather_add(a, b):
+        step("zz%d" % a, "v", lambda q: V.tensor_tensor(T.ZT[:, 4 * a:4 * b:2], T.AW[:, 0:2 * AWID].indirect(T.LC[:, a // 8:b // 8]), T.FH[:, 2 * a:2 * b], A.add),
+             lanes("AW", 0, AWID, (0, 2)) + lanes("FH", a, b, (0, 2)) + [("LC", 0, 32)], lanes("ZT", a, b, (0, 2)))
+
+    for t in range(R):
+        part[0] = str(t)
+        last = t == R - 1
+        XW, QX, QM, QB = "XW%d" % (t % 2), "QX%d" % t, "QM%d" % t, "QB%d" % t
+        NX = "XW%d" % ((t + 1) % 2)
+        if t > 0:
+            quant("QM", QM, 0, 128, XW, XB + 4 * 64, lanes(XW, 64, 192))
+        for h in (1, 0):
+            mm("S%d" % h, 4 + h, 128, "UC", 128 * h, QM, 0)
+        if t > 0:
+            pages("sv", XW, 0, 0, SA)
+            pages("vs", XW, 1, 0, SA)
+            pages("sv", XW, 0, SB, C)
+            pages("sv", XW, 1, SB, C)
+        psum_scan("PK", 5, 0, 17)
+        psum_scan("PC", 4, 32, 65)
+        ts(("MK", 0, 17), ("PK", 0, 17), ("PK", 16, 17), 4.0, A.is_lt, A.mult)
+        ts("sg", ("PC", 32, 33), ("PC", 64, 65), 0.5, A.is_ge, A.subtract)
+        total("K4", ("MK", 0, 18))
+        ts(("MC", 0, 65), ("PC", 0, 65), ("PC", 64, 65), 4.0, A.is_lt, A.mult)
+        ts("B0#1", "Z", "K4", 2.0, A.is_gt, A.mult)
+        ts("B1#0", "Z2", "sg", "K4", A.mult, A.min)
+        total("C4", ("MC", 0, 66))
+        scan("BO", "B0", "B1", A.mult, A.add)
+        ts(("LB", 0, 16), "I1", "C4", "K4", A.add, A.subtract)
+        ts(("LB", 16, 24), "BO#1", "C4", "K4", A.add, A.subtract)
+        lin("vs", "cs", "CS", "C4", 0.0)
+        act("ae", "J4h", -1.0, "C4", F.Abs)
+        allx = lanes(XW, -PAD, C + PAD)
+        gather("Ba", "sv", T.BT[:, 0:16 * NS], T[XW][:, 0:XWID], T.LB[:, 0:NS], allx + [("LB", 0, NS)], lanes("BT", 0, 4 * NS))
+        gather("Bb", "vs", T.BT[:, 16 * NS:384], T[XW][:, 0:XWID], T.LB[:, NS:24], allx + [("LB", NS, 24)], lanes("BT", 4 * NS, 96))
+        quant("QB", QB, 0, 128, "BT", 0, lanes("BT", 0, 128))
+        send(t, QB, QX)
+        quant("QX", QX, 0, C, XW, XB, lanes(XW, 0, C))
+        if t == 0:
+            list_constants()
+        act("D0#1", ("J4h", 0, 32), -1.0, "C4", F.Sign)
+        act("D1#0", "ae", -1.0, "K4", F.Sign)
+        lin("sv", "D0#2", "Jq", -1.0, ("cs", 0, 1))
+        lin("sv", "D1#1", "NK", "K4", 0.0)
+        lin("sv", "L0#0", "JO", 1.0, ("D1", 97, 98))
+        act("E1#1", ("ae", 0, 32), -1.0, "K4", F.Abs)
+        lin("sv", "s", "K4", -2.0, ("ae", 32, 33))
+        if t == 0:
+            for name, b in (("E", 2), ("EH", 1), ("EH", 3), ("E", 1), ("E", 3)):
+                e_quant(name, b)
+        lin("sv", "K4m", "K4", 1.0, -1.0)
+        for b in (0, 2, 1, 3):
+            e, ea, sc = e_tile(b)
+            mm("F%d" % b, b, C, e, ea, QX, 0)
+        for b in (0, 2, 1, 3):
+            window_copy("f%d" % b, "sv", b, b, 0, C, 0)
+            if b == 0:
+                step("h0", "g", lambda q: g.affine_select(T.FH[:, 0:2 * C:2], T.AW[:, 0:2 * C:2], [[1, C]], A.is_ge, 0.0, 0, 0),
+                     lanes("AW", 0, C, (0,)), lanes("FH", 0, C, (0,)))
+        scan("DO", "D0", ("D1", 0, 96), A.subtract, A.max)
+        lin("vs", "L1#1", "J4O", 1.0, "s")
+        ts("pm", "DO#2", ("cs", 1, 2), 0.5, A.is_le, A.subtract)
+        lin("vs", "L0#1", "L1#1", 1.0 / 3, 1024.0 / 3 - 1.0)
+        tt("dh", "DO#2", "pm", A.mult)
+        scan("LM", "L0", "L1", A.max, A.max)
+        lin("vs", "E1#0", "dh", 2048.0, "C4")
+        copy(("NI", 0, 32), "LM#1")
+        call("vs", lambda q, o, a: V.tensor_scalar(o, a, -1024.0, BIG, A.is_lt, A.mult) if q == "v" else S.activation(o, a, F.Relu, bias=-1024 * BIG, scale=-BIG),
+             "E0#1", "E1#0")
+        ts(("HI", 0, 32), ("NI", 0, 32), 2, None, A.bitwise_and)
+        scan("EO", "E0", "E1", A.add, A.min)
+        ts(("PI", 0, 32), ("NI", 0, 32), 1, None, A.bitwise_and)
+        ts(("LC", 0, 32), "EO#1", 0.5, "lcb", A.mult, A.add)
+        scaled("h2", "vs", T.FH[:, 1:2 * C:2], T.p2[:, 0:C], 1.0 / 64, [("p2", 0, 512)], lanes("FH", 0, C, (2,)))
+        if t == 1:
+            quant("QV", "QV", 0, 128, "VT", 0, [("VT", 0, 512)])
+        for b in (0, 2, 1, 3):
+            e, ea, sc = e_tile(b)
+            mm("G%d" % b, 4 + b, 128, e, ea, QX, AWID - 128)
+            window_copy("g%d" % b, ("vs", "sv")[b % 2], b, 4 + b, 128 - K, K, C)
+        for b in (0, 2):
+            mm("X1%d" % b, b, 128, "E", 128 * b, QX, 128, True, False)
+        for b in range(4):
+            mm("X0%d" % b, 4 + b, 128, "E", 128 * b, QX, 0, True, False)
+        ts("Et", ("HI", 0, 32), "K4m", -510.5, A.mult, A.add)
+        for h in range(2):
+            gather("A%d" % h, "s", T.AS[:, C * h:C * h + C], T.AW[:, 2 * AWID:4 * AWID], T.LC[:, 16 * h:16 * h + 16],
+                   lanes("AW", 0, AWID, (1, 3)) + [("LC", 0, 32)], [("AS", C * h, C * h + C)])
+        if t == 0:
+            for a, b in ((-PAD, 0), (C, C + PAD), (SB, 192)):
+                zeros("XW1", a, b)
+        gather_add(0, C)
+        for h in range(2):
+            a = 128 * h
+            for b in (1, 3):
+                add(h, b)
+            if h == 0:
+                tt("Dt", "Et", ("NI", 0, 32), A.add)
+            else:
+                ts("gt", ("PI", 0, 32), -0.5, 0.25, A.mult, A.add)
+                for b in (1, 3):
+                    mm("X1%d" % b, b, 128, "E", 128 * b, QX, 128, True, False)
+            quant("QZ%d" % h, "QZ", a, 128, "ZT", 4 * a, lanes("ZT", a, a + 128))
+            for b in range(4):
+                mm("W%d%d" % (h, b), b + 4 - 4 * h, 128, "W", 128 * b, "QZ", a, False, True)
+        tt("gD", "Dt", "gt", A.mult)
+        for qs, h, b in (("sv", 0, 0), ("sv", 0, 1), ("sv", 0, 2), ("vs", 0, 3), ("sv", 1, 0), ("vs", 1, 1), ("sv", 1, 2), ("vs", 1, 3)):
+            psum_copy("y%d%d" % (h, b), qs, "YS", C * (2 * (b % 2) + b // 2) + 128 * h, b + 4 - 4 * h, 128, 0.03125)
+            if (h, b) == (0, 3):
+                ts(("LO", 0, 32), "gD", ("cs", 2, 3), "cb", A.add, A.add)
+                if last:
+                    ts("OF", "gD", ("cs", 2, 3), "cb", A.add, A.add)
+        if last:
+            call("v", lambda q, o, a: V.transpose(o, a), "OT", "OF")
+        else:
+            pages("sv", NX, 0, SA, SB)
+            pages("vs", NX, 1, SA, SB)
+    part[0] = "z"
+    XW, QX = "XW%d" % (R % 2), "QX%d" % R
+    for h in range(2):
+        a = 128 * h
+        pages("sv", XW, 0, a, a + 128)
+        pages("vs", XW, 1, a, a + 128)
+        if h == 0:
+            lin("sv", "OC", "OT#0", 1.0, 0.0)
+            for e in range(2):
+                dma("ys", "lo%d" % e, T.lo[e:8:2, 0:C], opd(("OC", 8 * e, 8 * e + 8))[0], [("OC", 0, 16)], [])
+        quant("QX%d" % h, QX, a, 128, XW, XB + 4 * a, lanes(XW, a, a + 128))
+        mm("V%d" % h, 4 + h, 128, "QV", 0, QX, a)
+        dma("ys", "oc%d" % h, T.oc[:, 4 * a:4 * a + 512], T[QX + "c"][:, a:a + 128].bitcast(dt.uint8), [(QX, a, a + 128)], [])
+    for h in range(2):
+        a = 128 * h
+        psum_copy("y%d" % h, ("sv", "vs")[h], "YO", a, 4 + h, 128, 1.0)
+        dma(("sy", "ys")[h], "y%d" % h, T.y[:, a:a + 128], T.YO[:, a:a + 128], [("YO", a, a + 128)], [])
+    for i in range(4):
+        dma("sy", "os%d" % i, T.osc[4 * i:4 * i + 4, 0:C], T[QX + "p"][32 * i:32 * i + 4, 0:C], [(QX, 0, C)], [])
+    return steps
+
+
+def rank_program(g, core, T, topo):
+    if T.rank_of(core) is None:
         return
-    V, S, P, Y = g.vector, g.scalar, g.tensor, g.sync
-    queue = {"v": V, "s": S, "t": P, "g": g, "y": Y}
+    steps = plan(g, core, T, topo)
+    order = [x.split(":") for x in ORDER.split()] or [(name, s[1][0]) for name, s in steps.items()]
+    assert sorted(x[0] for x in order) == sorted(steps)
+    queue = {"v": g.vector, "s": g.scalar, "t": g.tensor, "g": g, "y": g.sync}
     count = {}
     waited = {}
     known = {q: {} for q in queue}
@@ -66,7 +424,7 @@ def rank_program(g, core, T, topo):
                 if x[3] != q:
                     if write or x[2] or name[0] == "p" and name[1:].isdigit():
                         out.append(x[4])
-                elif x[2] and not write:
+                elif x[2] and not write or q != "t" and write:
                     out.append(x[4])
 
     def note(q, name, a, b, write, ev):
@@ -84,7 +442,8 @@ def rank_program(g, core, T, topo):
         for s, n in list(behind.get(ev, {}).items()) + [(sem, val)]:
             known[q][s] = max(known[q].get(s, 0), n)
 
-    def pre(q, rd, wr):
+    for name, q in order:
+        kind, qs, fn, rd, wr = steps[name]
         evs = []
         for r in rd:
             need(q, r[0], r[1], r[2], False, evs)
@@ -95,343 +454,24 @@ def rank_program(g, core, T, topo):
             most[s] = max(most.get(s, 0), n)
         for s in sorted(most, key=lambda s: (s == "c" + q, s)):
             wait(q, (s, most[s]))
-
-    def emit(q, fn, rd, wr):
-        pre(q, rd, wr)
-        sem = "c" + q
-        count[sem] = count.get(sem, 0) + 1
-        fn().then_inc(T.sem[sem], 1)
+        if kind == "c":
+            who, sem = q, "c" + q
+            count[sem] = count.get(sem, 0) + 1
+            fn(q).then_inc(T.sem[sem], 1)
+        elif kind[0] == "d":
+            who = sem = kind
+            count[sem] = 16
+            fn(q).then_inc(T.sem[sem], 16)
+        else:
+            who = sem = kind
+            count[sem] = count["loc" + kind[3:]] = fn(q)
         ev = (sem, count[sem])
-        behind[ev] = dict(known[q])
-        for r in rd:
-            note(q, r[0], r[1], r[2], False, ev)
+        if kind[0] != "a":
+            behind[ev] = dict(known[q])
+            for r in rd:
+                note(who, r[0], r[1], r[2], False, ev)
         for r in wr:
-            note(q, r[0], r[1], r[2], True, ev)
-
-    def dma(q, name, out, in_, rd, wr):
-        pre(q, rd, wr)
-        sem = "d_" + name
-        count[sem] = 16
-        queue[q].dma_start(out, in_).then_inc(T.sem[sem], 16)
-        ev = (sem, 16)
-        behind[ev] = dict(known[q])
-        for r in rd:
-            note(sem, r[0], r[1], r[2], False, ev)
-        for r in wr:
-            note(sem, r[0], r[1], r[2], True, ev)
-
-    def opd(x):
-        if isinstance(x, str):
-            name, _, slot = x.partition("#")
-            a, w, m = WORK[name]
-            if slot:
-                return T.wk[:, a + int(slot):a + w * m:m], [(x, 0, w)]
-            return T.wk[:, a:a + w * m], [(x, 0, w)] if m == 1 else [("%s#%d" % (x, i), 0, w) for i in range(m)]
-        if x[0] in WORK:
-            a = WORK[x[0]][0]
-            return T.wk[:, a + x[1]:a + x[2]], [x]
-        return T[x[0]][:, x[1]:x[2]], [x]
-
-    def call(q, fn, out, *ins):
-        o, wr = opd(out)
-        rd, args = [], []
-        for x in ins:
-            if isinstance(x, (str, tuple)):
-                x, r = opd(x)
-                rd += r
-            args.append(x)
-        emit(q, lambda: fn(o, *args), rd, wr)
-
-    def lanes(name, a, b, which=range(4)):
-        return [(name + "#%d" % i, a, b) for i in which]
-
-    def ts(out, in0, s1, s2, op0, op1=None):
-        if op1 is None:
-            call("v", lambda o, x, a: V.tensor_scalar(o, x, a, None, op0), out, in0, s1)
-        else:
-            call("v", lambda o, x, a, b: V.tensor_scalar(o, x, a, b, op0, op1), out, in0, s1, s2)
-
-    def tt(out, x, y, op):
-        call("v", lambda o, a, b: V.tensor_tensor(o, a, b, op), out, x, y)
-
-    def scan(out, x, y, op0, op1, first=0.0):
-        call("v", lambda o, a, b: V.tensor_tensor_scan(o, a, b, first, op0, op1), out, x, y)
-
-    def total(out, x):
-        call("v", lambda o, a: V.tensor_reduce(o, a, AxisListType.X, A.add), out, x)
-
-    def copy(out, x):
-        call("v", V.tensor_copy, out, x)
-
-    def fill(out, val):
-        call("v", lambda o: V.memset(o, val), out)
-
-    def act(out, x, scale, bias, func=F.Identity):
-        call("s", lambda o, a, sc, bi: S.activation(o, a, func, bias=bi, scale=sc), out, x, scale, bias)
-
-    def quant(dst, a, n, src, sa, rd):
-        emit("v", lambda: V.quantize_mx(T[dst + "c"][:, a:a + n], T[dst + "p"][:, a:a + n], T[src][:, sa:sa + 4 * n]), rd, [(dst, a, a + n)])
-
-    def mm(bank, n, st, sa, mv, ma, start=True, stop=True):
-        emit("t", lambda: P.matmul_mx(T["p%d" % bank][:, 0:n], T[st + "c"][:, sa:sa + 128], T[st + "p"][:, sa:sa + 128],
-                                      T[mv + "c"][:, ma:ma + n], T[mv + "p"][:, ma:ma + n], start, stop),
-             [(st, sa, sa + 128), (mv, ma, ma + n)], [("p%d" % bank, 0, 512)])
-
-    def zeros(name, a, b):
-        emit("v", lambda: V.memset(T[name][:, XB + 4 * a:XB + 4 * b], 0.0), [], lanes(name, a, b))
-
-    def psum_copy(q, out, oa, bank, a, b, scale):
-        rd, wr = [("p%d" % bank, 0, 512)], [(out, oa, oa + b - a)]
-        src, to = T["p%d" % bank][:, a:b], T[out][:, oa:oa + b - a]
-        if q == "v":
-            emit("v", lambda: V.tensor_scalar(to, src, scale, None, A.mult), rd, wr)
-        else:
-            emit("s", lambda: S.activation(to, src, F.Copy, scale=scale), rd, wr)
-
-    def gather(q, out, win, off, rd, wr):
-        if q == "v":
-            emit("v", lambda: V.tensor_copy(out, win.indirect(off)), rd, wr)
-        else:
-            emit("s", lambda: S.activation(out, win.indirect(off), F.Copy), rd, wr)
-
-    def psum_scan(out, bank, a, n):
-        emit("v", lambda: V.tensor_tensor_scan(opd((out, 0, n))[0], T["p%d" % bank][:, a:a + n], opd(("NEG", 0, n))[0], -1.0e29, A.max, A.max),
-             [("p%d" % bank, 0, 512), ("NEG", 0, 72)], [(out, 0, n)])
-
-    dma("s", "u", T.UT[:, 0:512], T.u[:, 0:512], [], [("UT", 0, 512)])
-    for name, a, b in (("xm", 64, 192), ("xa", 0, 64), ("xb", 192, 256)):
-        dma("y", name, T.XW0[:, XB + 4 * a:XB + 4 * b], T.x[:, 4 * a:4 * b], [], lanes("XW0", a, b))
-    dma("y", "wc", T.Wc[:, 0:512].bitcast(dt.uint8), T.wc[:, 0:2048], [], [("W", 0, 512)])
-    dma("y", "ws", T.Wp[:, 0:512], T.ws[:, 0:512], [], [("Ws", 0, 512)])
-    dma("y", "v", T.VT[:, 0:512], T.v[:, 0:512], [], [("VT", 0, 512)])
-
-    def iota(out, pattern, step=0):
-        call("g", lambda o: g.iota(o, pattern, 0, step, allow_small_or_imprecise_dtypes=True), out)
-
-    def const(out, n, val):
-        act(out, ("ONE", 0, n), 0.0, val)
-    fill(("ONE", 0, 516), 32.0)
-    iota(("IP", 0, 1), [[1, 1]], 1)
-    iota(("UI", 0, 16), [[1, 2], [16, 8]])
-    iota("M16", [[16, 16]])
-    iota("M8", [[8, 32]])
-    emit("g", lambda: g.affine_select(T.EB[:, 0:516], T.ONE[:, 0:516], [[-1, 516]], A.is_equal, 0.0, 4, 4), [("ONE", 0, 516)], [("EB", 0, 516)])
-    iota(("PLACE", 0, C), [[1, C]])
-    ts(("IB", 0, 1), ("IP", 0, 1), 15, None, A.bitwise_and)
-    ts(("IB", 1, 2), ("IP", 0, 1), 3, None, A.bitwise_and)
-    ts(("IB", 2, 3), ("IP", 0, 1), 1, None, A.bitwise_and)
-    ts(("IB", 3, 4), ("IP", 0, 1), 1, 7, A.arith_shift_right, A.bitwise_and)
-    ts(("IB", 4, 5), ("IP", 0, 1), 1, 1, A.arith_shift_right, A.bitwise_and)
-    copy(("UO", 0, 16), ("UI", 0, 16))
-    copy("PB", ("IB", 0, 5))
-    zeros("XW0", -PAD, 0)
-    ts("NB", "PB", -1.0, None, A.mult)
-    zeros("XW0", C, C + PAD)
-    emit("v", lambda: V.memset(T.BT[:, 384:512], 0.0), [], lanes("BT", 96, 128))
-    const("NEG", 72, -1.0e29)
-    const(("MK", 17, 18), 1, 256.0)
-    const(("MC", 65, 66), 1, -640.0)
-    const("B0#0", 8, 0.0)
-    const("NK", 16, -1.0 / 512)
-    const("D0#0", 16, -BIG)
-    const("D1#2", 16, -BIG)
-    const("E0#0", 16, BIG)
-    act("J", "M16", 1.0, ("PB", 0, 1))
-    act("J32", "M8", 1.0, ("PB", 3, 4))
-    act("Z0", ("J", 0, 8), 1.0, ("NB", 1, 2))
-    act("I1", "J", 1.0, XB + 1024.0)
-    act("B1#1", ("J", 0, 8), 1.0, XB + 1280.0)
-    act("Z", "Z0", 1.0, 258.0)
-    act("Z2", "Z0", 2.0, 516.0)
-    quant("QU", 0, 128, "UT", 0, [("UT", 0, 512)])
-    emit("s", lambda: S.activation(T.UCp[:, 0:256], T.QUp[:, 0:128].indirect(T.UO[:, 0:16]), F.Copy), [("QU", 0, 128), ("UO", 0, 16)], [("UCs", 0, 256)])
-    emit("v", lambda: V.tensor_copy(T.UCc[:, 0:256].bitcast(dt.uint32), T.QUc[:, 0:128].bitcast(dt.uint32).indirect(T.UO[:, 0:16])),
-         [("QU", 0, 128), ("UO", 0, 16)], [("UC", 0, 256)])
-    quant("QM0", 0, 128, "XW0", XB + 4 * 64, lanes("XW0", 64, 192))
-    act("J4h", "J", 4.0, -1022.0)
-    act("Jq", "J", 1.0 / 256, 0.5 / 256 - 1.0)
-
-    def order_constants(w, j, odd):
-        act("JO" + w, j, 1.0, 512.0)
-        act("J4O" + w, j, 4.0, 2.5)
-        act("L1" + w + "#0", j, 2.0, odd)
-    order_constants("32", "J32", ("NB", 4, 5))
-    act("cb32", ("PB", 2, 3), 256.0, 255.625)
-    for a, b in ((-PAD, 0), (C, C + PAD), (SB, 192)):
-        emit("s", lambda: S.activation(T.XW1[:, XB + 4 * a:XB + 4 * b], T.ONE[:, 0:4 * (b - a)], F.Copy, scale=0.0), [("ONE", 0, 516)], lanes("XW1", a, b))
-
-    dst = T.cores[(rank - 1) % len(T.cores)]
-    rid, pid = topo.addr(dst)[:2]
-    mask = topo.mask(core, dst)
-    lands = 2 * len(topo.engines(core, dst))
-
-    def e_tile(b):
-        return ("E", 128 * b, 1.0 / 64) if b < 2 else ("EH", 128 * b - 256, 1.0)
-
-    def pages(q, name, h, a, b):
-        gather(q, T[name][:, XB + 4 * a + h:XB + 4 * b:2], T.YS[:, 2 * C * h:2 * C * h + 2 * C], T.LO[:, a // 8:b // 8],
-               [("YS", 2 * C * h, 2 * C * h + 2 * C), ("LO", 0, 32)], lanes(name, a, b, (h, h + 2)))
-
-    def ys(b):
-        return C * (2 * (b % 2) + b // 2)
-
-    for t in range(R):
-        last = t == R - 1
-        XW, QX, QM, QB = "XW%d" % (t % 2), "QX%d" % t, "QM%d" % t, "QB%d" % t
-        NX = "XW%d" % ((t + 1) % 2)
-        n = 16 if last else 32
-        w = str(n)
-        if t == 0:
-            pre("t", [("UCs", 0, 256)], [])
-        else:
-            quant(QM, 0, 128, XW, XB + 4 * 64, lanes(XW, 64, 192))
-        mm(5, 128, "UC", 128, QM, 0)
-        mm(4, 128, "UC", 0, QM, 0)
-        if t > 0:
-            pages("s", XW, 0, 0, SA)
-            pages("v", XW, 1, 0, SA)
-            pages("s", XW, 0, SB, C)
-            pages("s", XW, 1, SB, C)
-        psum_scan("PK", 5, 0, 17)
-        psum_scan("PC", 4, 32, 65)
-        ts(("MK", 0, 17), ("PK", 0, 17), ("PK", 16, 17), 4.0, A.is_lt, A.mult)
-        ts(("MC", 0, 65), ("PC", 0, 65), ("PC", 64, 65), 4.0, A.is_lt, A.mult)
-        total("K4", ("MK", 0, 18))
-        total("C4", ("MC", 0, 66))
-        ts("sg", ("PC", 32, 33), ("PC", 64, 65), 0.5, A.is_ge, A.subtract)
-        ts(("LB1", 0, 16), "I1", "C4", "K4", A.add, A.subtract)
-        ts("B1#0", "Z2", "sg", "K4", A.mult, A.min)
-        ts("B0#1", "Z", "K4", 2.0, A.is_gt, A.mult)
-        ts("L0" + w + "#0", "JO" + w, "K4", None, A.subtract)
-        scan("BO", "B0", "B1", A.mult, A.add)
-        ts("K4m", "K4", -1.0, None, A.add)
-        ts(("LB2", 0, 8), "BO#1", "C4", "K4", A.add, A.subtract)
-        ts("thr", "C4", -1.0 / 1024, None, A.mult)
-        allx = lanes(XW, -PAD, C + PAD)
-        gather("s", T.BT[:, 0:256], T[XW][:, 0:XWID], T.LB1[:, 0:16], allx + [("LB1", 0, 16)], lanes("BT", 0, 64))
-        gather("v", T.BT[:, 256:384], T[XW][:, 0:XWID], T.LB2[:, 0:8], allx + [("LB2", 0, 8)], lanes("BT", 64, 96))
-        quant(QB, 0, 128, "BT", 0, lanes("BT", 0, 128))
-        pre("g", [(QB, 0, 96)], [])
-        g.remote_dma(out_ap=T[QX + "c"][:, C:AWID].bitcast(dt.uint8), in_ap=T[QB + "c"][:, 0:K].bitcast(dt.uint8),
-                     remote_sem=T.sem["arr%d" % t], local_sem=T.sem["loc%d" % t], pid=pid, routing_id=rid, dma_engine_mask=mask)
-        g.remote_dma(out_ap=T[QX + "p"][:, C:AWID], in_ap=T[QB + "p"][:, 0:K],
-                     remote_sem=T.sem["arr%d" % t], local_sem=T.sem["loc%d" % t], pid=pid, routing_id=rid, dma_engine_mask=mask)
-        count["arr%d" % t] = lands
-        count["loc%d" % t] = lands
-        note("remote", QX, C, AWID, True, ("arr%d" % t, lands))
-        quant(QX, 0, C, XW, XB, lanes(XW, 0, C))
-        act("ae", "J4h", -1.0, "C4", F.Abs)
-        act("nthr", "C4", 1.0 / 1024, 0.0)
-        act("D0#1", "J4h", -1.0, "C4", F.Sign)
-        act("D1#0", "ae", -1.0, "K4", F.Sign)
-        act("D0#2", "Jq", -1.0, "nthr")
-        act("D1#1", "NK", "K4", 0.0)
-        act("ac4", "C4", 1.0, 512.5, F.Abs)
-        act("E1#1", "ae", -1.0, "K4", F.Abs)
-        act("s", "K4", -2.0, "ac4")
-        if t == 0:
-            for b in (0, 1):
-                quant("E", 128 * b, 128, "EB", 4 - b, [("EB", 0, 516)])
-            ts(("EB2", 0, 516), ("EB", 0, 516), 1.0 / 64, None, A.mult)
-            quant("E", 256, 128, "EB", 2, [("EB", 0, 516)])
-            for b in (2, 3):
-                quant("EH", 128 * b - 256, 128, "EB2", 4 - b, [("EB2", 0, 516)])
-        act("cm", "C4", 0.25, 255.625 if last else "cb32")
-        act("L1" + w + "#1", "J4O" + w, 1.0, "s")
-        for b in range(4):
-            e, ea, sc = e_tile(b)
-            mm(b, C, e, ea, QX, 0)
-
-        def f_copy(q, b):
-            psum_copy(q, "AW", AWID * b, b, 0, C, e_tile(b)[2])
-            if b < 2:
-                emit("g", lambda: g.affine_select(T.FH[:, C * b:C * b + C], T.AW[:, AWID * b:AWID * b + C], [[1, C]], A.is_ge, 0.0, 0, 0),
-                     [("AW", AWID * b, AWID * b + C)], [("FH", C * b, C * b + C)])
-        f_copy("s", 0)
-        act("L0" + w + "#1", "L1" + w + "#1", 1.0 / 3, 1024.0 / 3 - 1.0)
-        f_copy("s", 1)
-        f_copy("s", 2)
-        scan("DO", "D0", "D1", A.subtract, A.max)
-        ts("pm", "DO#2", "thr", 0.5, A.is_le, A.subtract)
-        tt("dh", "DO#2", "pm", A.mult)
-        scan("LM" + w, "L0" + w, "L1" + w, A.max, A.max)
-        ts("E1#0", "dh", 2048.0, "C4", A.mult, A.add)
-        copy(("NI", 0, n), "LM" + w + "#1")
-        ts("E0#1", "E1#0", -1024.0, BIG, A.is_lt, A.mult)
-        ts(("HI", 0, n), ("NI", 0, n), 2, None, A.bitwise_and)
-        scan("EO", "E0", "E1", A.add, A.min)
-        ts(("PI", 0, n), ("NI", 0, n), 1, None, A.bitwise_and)
-        ts(("LC", 0, 16), "EO#1", 0.25, 255.5, A.mult, A.add)
-        f_copy("v", 3)
-        if t == 0:
-            quant("E", 384, 128, "EB", 1, [("EB", 0, 516)])
-        if t == 1:
-            quant("QV", 0, 128, "VT", 0, [("VT", 0, 512)])
-        for b in (0, 2, 1, 3):
-            e, ea, sc = e_tile(b)
-            mm(4 + b, 128, e, ea, QX, AWID - 128)
-
-        def g_copy(q, b):
-            psum_copy(q, "AW", AWID * b + C, 4 + b, 128 - K, 128, e_tile(b)[2])
-
-        def a_gather(b):
-            gather("s", T.AS[:, C * b - 2 * C:C * b - C], T.AW[:, AWID * b:AWID * b + AWID], T.LC[:, 0:16],
-                   [("AW", AWID * b, AWID * b + AWID), ("LC", 0, 16)], [("AS", C * b - 2 * C, C * b - C)])
-        g_copy("v", 0)
-        g_copy("s", 2)
-        g_copy("s", 1)
-        g_copy("s", 3)
-        a_gather(2)
-        for b in (0, 1):
-            win = T.AW[:, AWID * b:AWID * b + AWID]
-            emit("v", lambda: V.tensor_tensor(T.ZT[:, b:4 * C:4], win.indirect(T.LC[:, 0:16]), T.FH[:, C * b:C * b + C], A.add),
-                 [("AW", AWID * b, AWID * b + AWID), ("FH", C * b, C * b + C), ("LC", 0, 16)], [("ZT#%d" % b, 0, C)])
-        a_gather(3)
-        if t == 0:
-            order_constants("16", "J", ("NB", 2, 3))
-        for b in (2, 3):
-            emit("v", lambda: V.tensor_tensor(T.ZT[:, b:4 * C:4], T.AS[:, C * b - 2 * C:C * b - C], T["p%d" % b][:, 0:C], A.add),
-                 [("AS", C * b - 2 * C, C * b - C), ("p%d" % b, 0, 512)], [("ZT#%d" % b, 0, C)])
-        quant("QZ", 0, C, "ZT", 0, lanes("ZT", 0, C))
-        for b in (0, 2, 1, 3):
-            mm(4 + b, C, "E", 128 * b, QX, 0, True, False)
-        if t == 0:
-            pre("t", [("Ws", 0, 512)], [])
-        for b in range(4):
-            mm(4 + b, C, "W", 128 * b, "QZ", 0, False, True)
-        ts("Et" + w, ("HI", 0, n), "K4m", -510.5, A.mult, A.add)
-        ts("gt" + w, ("PI", 0, n), -0.5, 0.25, A.mult, A.add)
-        tt("Dt" + w, "Et" + w, ("NI", 0, n), A.add)
-        tt("gD" + w, "Dt" + w, "gt" + w, A.mult)
-        ts(("LO", 0, n), "gD" + w, "cm", None, A.add)
-        for b in range(4):
-            psum_copy("sv"[b % 2], "YS", ys(b), 4 + b, 0, C, 0.03125)
-        if not last:
-            pages("s", NX, 0, SA, SB)
-            pages("v", NX, 1, SA, SB)
-    XW, QX = "XW%d" % (R % 2), "QX%d" % R
-
-    def page(q, b, a):
-        gather(q, T[XW][:, XB + 4 * a + b:XB + 4 * a + 512:4], T.YS[:, ys(b):ys(b) + C], T.LO[:, a // 16:a // 16 + 8],
-               [("YS", ys(b), ys(b) + C), ("LO", 0, 32)], [(XW + "#%d" % b, a, a + 128)])
-    for b in range(4):
-        page("sv"[b % 2], b, 0)
-    page("s", 0, 128)
-    page("s", 2, 128)
-    quant(QX, 0, 128, XW, XB, lanes(XW, 0, 128))
-    page("v", 1, 128)
-    page("v", 3, 128)
-    quant(QX, 128, 128, XW, XB + 512, lanes(XW, 128, 256))
-    gather("s", T.LOF[:, 0:C], T.PLACE[:, 0:C], T.LO[:, 0:16], [("PLACE", 0, C), ("LO", 0, 32)], [("LOF", 0, C)])
-    for h in range(2):
-        mm(h, 128, "QV", 0, QX, 128 * h)
-        psum_copy("v", "YO", 128 * h, h, 0, 128, 1.0)
-    dma("y", "oc", T.oc[:, 0:4 * C], T[QX + "c"][:, 0:C].bitcast(dt.uint8), [(QX, 0, C)], [])
-    dma("s", "lo", T.lo[:, 0:C], T.LOF[0:128:16, 0:C], [("LOF", 0, C)], [])
-    for i in range(4):
-        dma("yyss"[i], "os%d" % i, T.osc[4 * i:4 * i + 4, 0:C], T[QX + "p"][32 * i:32 * i + 4, 0:C], [(QX, 0, C)], [])
-    for h in range(2):
-        dma("y", "y%d" % h, T.y[:, 128 * h:128 * h + 128], T.YO[:, 128 * h:128 * h + 128], [("YO", 128 * h, 128 * h + 128)], [])
+            note(who, r[0], r[1], r[2], True, ev)
     for sem in sorted(count, key=lambda s: (s[0] == "d", s)):
         if waited.get(sem, 0) < count[sem]:
             wait("g", (sem, count[sem]))

@@ -1,4 +1,4 @@
-from concourse.mybir import dt, AluOpType as A, AxisListType, ActivationFunctionType as F
+from concourse.mybir import dt, AluOpType as A, ActivationFunctionType as F
 
 R, C, K = 3, 256, 96
 PAD = 48
@@ -9,34 +9,33 @@ BIG = 4096.0
 SA, SB = 64, 176
 NS = 14
 ORDER = """
-ad_u:s ad_xm:y aIP:g aM16:g ad_xa:y ad_xb:y ad_wc:y ad_ws:y ad_v:y aONE:v aEB:v aEBd:g 0NK:s aIB:v aIB2:v aIB1:v aIB4:v aJ4h32:s 0E0#0:s aCS1:s
-0NK32:s aIB3:v aUI:g aMK17:v aPB:v aCS:s aE0:v aB0#0:s aJ16:v 0XW1_224:s aMC65:s aCS2:s 0D0#0:s aNEG:s aNB:s aUO:v 0D1#2:s aEB2:s aQU:v aM8:g aJ:v
-aUs1:s aUs0:s aZ0:s aB1#1:s aUc1:v aUc0:v aQM:v aXW0_0:v 0H3:v 0S1:t aZ:s 0PK:v 0S0:t 0PC:v aJq:s aZ2:s aJO:s aJ4h:s 0MK:v 0sg:v aI1:s aXW0_304:s
-0K4:v 0MC:v aBT0:s 0B0#1:v 0B1#0:v 0C4:v 0BO:v 0LB:v 0cs:s 0LB16:v 0Ba:s 0ae:s 0D0#2:s 0D1#0:s 0Bb:v 0D1#1:s 0J4O:v 0s:s 0QB:v 0QX:v 0D0#1:s 0E2:v
-0DO:v 0F0:t 0L0#0:s 0F3:t 0E1:v 0L1#1:s 0pm:v 0F2:t 0cb:s 0L1#0:v 0dh:v 0L0#1:v 0f0:s 0H1:v 0E1#0:s 0E1#1:s 0XW1_0:v 0LM:v 0E0#1:v 0B>:g 0lcb:s 0X10:t
-0F1:t 0K4m:s 0f3:s 0f2:s 0NI:v 0h2:s 0EO:v 0HI:v 0X12:t 0PI:v 0f1:s 0gt:v 0h0:g 0XW1_304:v 0G0:t 0g0:s 0Et:v 0G2:t 0G1:t 0LC:v 0G3:t 0E3:v 0g1:s
-0X00:t 0g2:v 0Dt:v 0g3:s 0X02:t 0zz0:v 0A0:s 0z03:v 0X01:t 0A1:s 0X03:t 0z01:v 0gD:v 0QZ0:v 0z11:v 0W01:t 0y01:s 0W00:t 0z13:v 0QZ1:v 0W03:t 0W02:t
-0y00:s 0y02:s 0X11:t 0X13:t 0W10:t 0y10:s 0W11:t 0LO:v 0y03:v 0W12:t 0W13:t 0y11:v 0y13:v 0y12:s 0pg0_64:s 0pg1_64:v 1pg0_0:s 1QM:v 1pg1_176:s 1S1:t
-1PK:v 1S0:t 1PC:v 1pg0_176:s 1MK:v 1sg:v 1K4:v 1D1#1:s 1MC:v 1B1#0:v 1B0#1:v 1pg1_0:s 1C4:v 1BO:v 1LB:v 1D0#1:s 1cs:s 1LB16:v 1Bb:v 1Ba:s 1D0#2:v
-1ae:s 1QB:v 1D1#0:s 1L0#0:s 1E1#1:s 1QX:v 1F0:t 1DO:v 1K4m:v 1s:s 1pm:v 1F2:t 1L1#1:s 1L0#1:s 1f0:s 1dh:v 1LM:v 1E1#0:v 1B>:g 1F1:t 1F3:t 1NI:v 1f2:s
-1f1:s 1G2:t 1E0#1:v 1G3:t 1HI:v 1EO:v 1g2:s 1Et:v 1G0:t 1G1:t 1h0:g 1LC:v 1X10:t 1X02:t 1h2:v 1g0:v 1g3:s 1X03:t 1PI:v 1zz0:v 1X12:t 1g1:s 1f3:s 1A0:s
-1z03:v 1z01:v 1Dt:v 1X00:t 1X01:t 1QZ0:v 1W00:t 1A1:s 1W03:t 1W02:t 1W01:t 1z11:v 1X11:t 1y00:s 1z13:v 1gt:v 1X13:t 1QZ1:v 1y02:s 1W10:t 1W11:t 1y01:s
-1y03:s 1gD:v 1LO:v 1y10:s 1W12:t 1y12:s 1W13:t 1pg0_64:s 1y11:v 2pg0_0:s 1y13:v 1pg1_64:v 2QM:v 2pg1_0:s 1QV:v 2S1:t 2PK:v 2S0:t 2PC:v 2MK:v
-2pg1_176:s 2sg:v 2K4:v 2pg0_176:s 2MC:v 2B0#1:v 2B1#0:v 2C4:v 2ae:s 2BO:v 2LB:v 2Ba:s 2LB16:v 2Bb:v 2cs:v 2D1#1:s 2QB:v 2QX:v 2F0:t 2F2:t 2s:s 2D0#1:s
-2B>:g 2D0#2:s 2D1#0:s 2F1:t 2L0#0:s 2F3:t 2DO:v 2K4m:s 2pm:v 2L1#1:s 2L0#1:s 2G0:t 2E1#1:s 2G3:t 2dh:v 2LM:v 2E1#0:v 2NI:v 2E0#1:v 2HI:v 2f0:s 2f2:s
-2f1:s 2EO:v 2G2:t 2PI:v 2LC:v 2h0:g 2g0:s 2G1:t 2g3:s 2X10:t 2h2:v 2g2:v 2X00:t 2f3:s 2X12:t 2g1:s 2X03:t 2Et:v 2X02:t 2A0:s 2zz0:v 2A1:s 2z01:v
-2z03:v 2X01:t 2Dt:v 2QZ0:v 2W00:t 2z11:v 2z13:v 2X11:t 2W02:t 2W01:t 2gt:v 2QZ1:v 2y00:s 2W03:t 2X13:t 2gD:v 2W10:t 2y02:s 2W11:t 2y01:s 2W12:t 2y10:s
-2y12:s 2OF:v 2LO:v 2y03:s 2y11:v 2W13:t 2y13:v zpg0_0:s 2OT:v zOC:s zpg1_0:v zd_lo0:y zQX0:v zV0:t zd_lo1:y zd_oc0:y zpg1_128:v zpg0_128:s zQX1:v
-zy0:s zd_y0:s zV1:t zd_os3:y zd_oc1:s zd_os1:y zd_os2:y zd_os0:s zy1:s zd_y1:y
+ad_u:s ad_xm:y ad_xa:y ad_xb:y ad_v:y ad_wc:y ad_ws:y aONE:v aJh32:s aEB:v aB0#0:v 0D1#2:s aIP:g aIB:v aPK17:s 0E0#0:s aIB2:v aIB3:v aae33:s aIB4:v 0D0#0:s
+aIB1:v aUI:g aCS:s aCS2:s 0XW1_0:s aM16:g aNEG:v aCS1:v aPB:v aBT0:s 0NK:s aNB:s aJ16:s 0lcb:s 0NK33:v 0XW1_224:v aUO:v aEBd:g aEB2:v aQU:v 0cb:v 0NK32:s aUc1:v
+aUc0:v aM8:g aJ:s aB1#1:s aQM:v aXW0_304:s aJh:s 0L1#0:s aZ0:s 0H3:v aUs1:s aUs0:s aI1:s 0S1:t 0H2:v aZ:s 0PK:v aXW0_0:s aJO:s 0S0:t 0PC:v 0J4O:v aZ2:s 0sg:v
+0k:s 0B0#1:v 0c:s 0B1#0:v 0d:v 0BO:v 0D1#1:s 0LB:v 0LB16:v 0D0#2:v 0K4m:s 0D0#1:s 0ae:s 0Bb:v 0cm:s 0D1#0:s 0DO:v 0Ba:s 0s:s 0QB:v 0cs:s 0pm:v 0QXb:v 0E1#1:s
+0L1#1:s 0XW1_304:s 0L0#1:s 0L0#0:s 0QX:v 0dh:v 0LM:v 0E1#0:s 0H1:v 0E0#1:v 0F2:t aH0:v 0F1:t 0F0:t 0NI:v 0F3:t 0EO:v 0B>:g 0E2:v 0PI:v 0HI:v 0f2:s 0LC:v 0f1:s
+0E0:v 0Et:v 0f0:s 0E1:v 0Dt:v 0G0:t 0f3:s 0gt:v 0h0:v 0gD:v 0E3:v 0h1:s 0LO:v 0G2:t 0g2:v 0g0:s 0G1:t 0g1:v 0zz0:v 0G3:t 0g3:s 0zz1:v 0A1:s 0z1:v 0X02:t 0A0:s
+0X01:t 0QZ0:v 0X03:t 0z3:v 0X00:t 0X11:t 0z0:v 0W00:t 0y00:s 0W01:t 0W02:t 0y01:s 0y02:s 0z2:v 0QZ1:v 0QV:v 0W03:t 0X13:t 0y03:s 0X12:t 0X10:t 0W10:t 0y10:v
+0W11:t 0W12:t 0y11:v 0W13:t 0y12:s 0pg0_64:s 0y13:v 0pg1_64:v 1QM:v 1S1:t 1pg1_0:v 1S0:t 1PK:v 1pg0_0:s 1pg1_176:s 1PC:v 1k:s 1QX:v 1c:s 1pg0_176:s 1sg:v
+1B0#1:v 1D0#1:s 1ae:s 1B1#0:v 1d:v 1BO:v 1D1#1:s 1LB:v 1LB16:v 1QXb:v 1F3:t 1Ba:s 1Bb:v 1s:s 1D1#0:s 1D0#2:v 1cm:s 1QB:v 1DO:v 1F1:t 1L1#1:s 1L0#0:s 1L0#1:v
+1F2:t 1cs:s 1B>:g 1K4m:v 1pm:v 1LM:v 1F0:t 1G2:t 1E1#1:s 1f1:s 1G0:t 1f2:s 1dh:v 1NI:v 1E1#0:s 1E0#1:v 1HI:v 1PI:v 1EO:v 1G1:t 1Et:v 1gt:v 1LC:v 1f0:s 1Dt:v
+1f3:s 1h0:s 1g2:s 1G3:t 1h1:v 1g1:s 1g3:s 1X02:t 1g0:v 1X00:t 1gD:v 1zz0:v 1zz1:v 1X01:t 1X03:t 1A1:s 1z1:v 1X11:t 1QZ0:v 1A0:s 1W01:t 1y01:s 1z3:v 1W02:t
+1W03:t 1z2:v 1y02:s 1W00:t 1z0:v 1LO:v 1X12:t 1X13:t 1QZ1:v 1X10:t 1W10:t 1y00:v 1W11:t 1W12:t 1y03:s 1y10:s 1y12:s 1W13:t 1y11:v 1y13:v 1pg1_64:v 1pg0_64:s
+2QM:v 2S1:t 2S0:t 2pg1_0:s 2pg1_176:s 2pg0_0:v 2PK:v 2PC:v 2k:s 2QX:v 2c:s 2pg0_176:s 2sg:v 2ae:s 2B0#1:v 2D0#1:s 2cm:s 2B1#0:v 2d:v 2BO:v 2LB:v 2Ba:s 2D1#1:s
+2s:s 2LB16:v 2D1#0:s 2QXb:v 2F3:t 2Bb:v 2D0#2:v 2QB:v 2L1#1:v 2cs:s 2L0#0:s 2F0:t 2B>:g 2DO:v 2L0#1:v 2pm:v 2LM:v 2dh:v 2NI:v 2E1#0:v 2F1:t 2K4m:s 2E0#1:v 2HI:v
+2F2:t 2E1#1:s 2PI:v 2f3:s 2f0:s 2EO:v 2f2:s 2G2:t 2G0:t 2Et:v 2f1:s 2gt:v 2G3:t 2h0:s 2g2:s 2LC:v 2Dt:v 2G1:t 2g3:s 2h1:v 2g1:s 2g0:v 2gD:v 2X02:t 2X00:t 2X03:t
+2X01:t 2zz0:v 2zz1:v 2A0:s 2z0:v 2QZ0:v 2X10:t 2W01:t 2A1:s 2W00:t 2W03:t 2y01:s 2W02:t 2y00:s 2z1:v 2y03:s 2z3:v 2z2:v 2X11:t 2y02:s 2QZ1:v 2X13:t 2X12:t
+2W10:t 2OF:v 2LO:v 2OT:v 2W11:t zOC:v zd_lo1:y 2W12:t 2W13:t 2y10:s 2y11:v 2y12:s zd_lo0:y 2y13:v zpg1_0:v zpg0_0:s zpg0_128:s zQX0:v zV0:t zd_oc0:y zy0:s
+zpg1_128:v zQX1:v zd_y0:y zd_oc1:y zV1:t zd_os0:s zd_os1:s zd_os2:s zd_os3:s zy1:v zd_y1:y
 """
 
 WORK = {}
 _n = [0]
-for _name, _w, _m in (("NEG", 72, 1), ("PC", 72, 1), ("PK", 24, 1), ("MC", 72, 1), ("MK", 24, 1), ("C4", 1, 1), ("K4", 1, 1), ("sg", 1, 1),
-                      ("PB", 5, 1), ("NB", 5, 1), ("M16", 16, 1), ("M8", 32, 1), ("J", 32, 1), ("Z0", 8, 1), ("cb", 1, 1), ("J16", 16, 1),
+for _name, _w, _m in (("NEG", 72, 1), ("PC", 72, 1), ("PK", 88, 1), ("MC", 72, 1), ("MK", 88, 1), ("c", 1, 1), ("k", 1, 1), ("cm", 1, 1), ("sg", 1, 1),
+                      ("d", 1, 1), ("PB", 5, 1), ("NB", 5, 1), ("M16", 16, 1), ("M8", 32, 1), ("J", 32, 1), ("Z0", 8, 1), ("cb", 1, 1), ("J16", 16, 1),
                       ("I1", 16, 1), ("Z", 8, 1), ("Z2", 8, 1), ("B0", 8, 2), ("B1", 8, 2), ("BO", 8, 2),
-                      ("J4h", 33, 1), ("Jq", 32, 1), ("NK", 33, 1), ("CS", 3, 1), ("cs", 3, 1), ("ae", 33, 1), ("lcb", 1, 1),
-                      ("D0", 32, 3), ("D1", 33, 3), ("DO", 32, 3), ("pm", 32, 1), ("dh", 32, 1), ("E0", 32, 2), ("E1", 32, 2), ("EO", 32, 2),
+                      ("Jh", 33, 1), ("NK", 34, 1), ("CS", 3, 1), ("cs", 3, 1), ("ae", 34, 1), ("lcb", 1, 1),
+                      ("D0", 32, 3), ("D1", 34, 3), ("DO", 32, 3), ("pm", 32, 1), ("dh", 32, 1), ("E0", 32, 2), ("E1", 32, 2), ("EO", 32, 2),
                       ("s", 1, 1), ("K4m", 1, 1),
                       ("JO", 32, 1), ("J4O", 32, 1), ("L0", 32, 2), ("L1", 32, 2), ("LM", 32, 2), ("Et", 32, 1), ("gt", 32, 1),
                       ("Dt", 32, 1), ("gD", 32, 1), ("OF", 32, 1), ("OT", 16, 2), ("OC", 16, 1)):
@@ -55,7 +54,7 @@ SCRATCH = {
     "ZT": ("sbuf", [128, 4 * C], "bfloat16"), "YS": ("sbuf", [128, 4 * C], "bfloat16"), "AW": ("sbuf", [128, 4 * AWID], "bfloat16"),
     "FH": ("sbuf", [128, 2 * C], "bfloat16"), "AS": ("sbuf", [128, 2 * C], "bfloat16"),
 }
-for _name, _w in (("E", 512), ("EH", 256), ("QU", 128), ("UC", 256), ("QV", 128), ("W", 512), ("QZ", 256), ("QM0", 128), ("QM1", 128),
+for _name, _w in (("E", 512), ("EH", 512), ("QU", 128), ("UC", 256), ("QV", 128), ("W", 512), ("QZ", 256), ("QM0", 128), ("QM1", 128),
                   ("QM2", 128), ("QX0", AWID), ("QX1", AWID), ("QX2", AWID), ("QX3", C), ("QB0", 128), ("QB1", 128), ("QB2", 128)):
     SCRATCH[_name + "c"] = ("sbuf", [128, _w], "float8_e4m3fn_x4")
     SCRATCH[_name + "p"] = ("sbuf", [128, _w], "uint8")
@@ -120,8 +119,9 @@ def plan(g, core, T, topo):
     def scan(out, x, y, op0, op1, first=0.0):
         call("v", lambda q, o, a, b: V.tensor_tensor_scan(o, a, b, first, op0, op1), out, x, y)
 
-    def total(out, x):
-        call("v", lambda q, o, a: V.tensor_reduce(o, a, AxisListType.X, A.add), out, x)
+    def below(out, signs, x, top):
+        (o, wr), (sg, wr2), (a, rd), (b, rd2) = opd(out), opd(signs), opd(x), opd(top)
+        step(out, "s", lambda q: S.activation(sg, a, F.Sign, bias=b, scale=-1.0, accum_out=o), rd + rd2, wr + wr2)
 
     def copy(out, x):
         call("v", lambda q, o, a: V.tensor_copy(o, a), out, x)
@@ -162,9 +162,9 @@ def plan(g, core, T, topo):
     dma("s", "u", T.UT[:, 0:512], T.u[:, 0:512], [], [("UT", 0, 512)])
     for name, a, b in (("xm", 64, 192), ("xa", 0, 64), ("xb", 192, 256)):
         dma("y", name, T.XW0[:, XB + 4 * a:XB + 4 * b], T.x[:, 4 * a:4 * b], [], lanes("XW0", a, b))
+    dma("y", "v", T.VT[:, 0:512], T.v[:, 0:512], [], [("VT", 0, 512)])
     dma("y", "wc", T.Wc[:, 0:512].bitcast(dt.uint8), T.wc[:, 0:2048], [], [("W", 0, 512)])
     dma("y", "ws", T.Wp[:, 0:512], T.ws[:, 0:512], [], [("Ws", 0, 512)])
-    dma("y", "v", T.VT[:, 0:512], T.v[:, 0:512], [], [("VT", 0, 512)])
 
     def iota(out, pattern, step=0):
         call("g", lambda q, o: g.iota(o, pattern, 0, step, allow_small_or_imprecise_dtypes=True), out)
@@ -186,10 +186,10 @@ def plan(g, core, T, topo):
     copy(("UO", 0, 16), ("UI", 0, 16))
     copy("PB", ("IB", 0, 5))
     scaled("BT0", "vs", T.BT[:, 384:512], T.ONE[:, 0:128], 0.0, [("ONE", 0, 192)], lanes("BT", 96, 128))
-    lin("vs", "NB", "PB", -1.0, 0.0)
+    lin("vs", "NB", "PB", -0.25, 0.0)
     const("NEG", 72, -1.0e29)
-    const(("MK", 17, 18), 1, 256.0)
-    const(("MC", 65, 66), 1, -640.0)
+    const(("PK", 17, 81), 64, -1.0e29)
+    const(("ae", 33, 34), 1, 0.0)
     const("B0#0", 8, 0.0)
     zeros("XW0", -PAD, 0)
     zeros("XW0", C, C + PAD)
@@ -206,42 +206,40 @@ def plan(g, core, T, topo):
         if name == "E":
             quant("E%d" % b, "E", 128 * b, 128, "EB", 4 - b, [("EB", 0, 516)])
         else:
-            quant("H%d" % b, "EH", 64 * b - 64, 128, "EB2", 4 - b, [("EB2", 0, 516)])
+            quant("H%d" % b, "EH", 128 * b, 128, "EB2", 4 - b, [("EB2", 0, 516)])
     pick(1)
     quant("QM", "QM0", 0, 128, "XW0", XB + 4 * 64, lanes("XW0", 64, 192))
     pick(0)
-    e_quant("E", 0)
+    e_quant("EH", 0)
     lin("sv", "J16", "M16", 1.0, ("PB", 0, 1))
     lin("sv", "J", "M8", 1.0, ("PB", 3, 4))
-    lin("sv", "Z0", ("J16", 0, 8), 1.0, ("NB", 1, 2))
-    lin("sv", "I1", "J16", 1.0, XB + 1024.0)
-    lin("sv", "B1#1", ("J16", 0, 8), 1.0, XB + 1280.0)
-    lin("sv", "Z2", "Z0", 2.0, 516.0)
-    lin("sv", "Z", "Z0", 1.0, 258.0)
-    lin("sv", "JO", "J", 1.0, 512.0)
-    lin("sv", ("J4h", 0, 32), "J", 4.0, -1022.0)
-    const(("J4h", 32, 33), 1, -512.5)
-    for i, val in enumerate((1.0 / 1024, -1.0 / 1024, 0.25)):
+    lin("sv", "Z0", ("J16", 0, 8), 0.25, ("NB", 1, 2))
+    lin("sv", "I1", "J16", 0.25, PAD + 96.0)
+    lin("sv", "B1#1", ("J16", 0, 8), 0.25, PAD + 160.0)
+    lin("sv", "Z2", "Z0", 2.0, 129.0)
+    lin("sv", "Z", "Z0", 1.0, 64.5)
+    lin("sv", "JO", "J", 0.25, 128.0)
+    lin("sv", ("Jh", 0, 32), "J", 1.0, -95.5)
+    const(("Jh", 32, 33), 1, 31.875)
+    for i, val in enumerate((-1.0 / 256, 1.0 / 512, 1.0 / 1024)):
         const(("CS", i, i + 1), 1, val)
-    lin("sv", "Jq", "J", 1.0 / 256, 0.5 / 256 - 1.0)
 
     def list_constants():
-        const(("NK", 0, 32), 32, -1.0 / 512)
+        const(("NK", 0, 32), 32, -1.0 / 128)
         const(("NK", 32, 33), 1, -1.0)
+        const(("NK", 33, 34), 1, 1.0 / 1024)
         const("D0#0", 32, -BIG)
-        const("D1#2", 33, -BIG)
-        lin("sv", "J4O", "J", 4.0, 2.5)
-        lin("sv", "L1#0", "J", 2.0, ("NB", 4, 5))
+        const("D1#2", 34, -BIG)
+        lin("sv", "J4O", "J", 1.0, 0.625)
+        lin("sv", "L1#0", "J", 0.5, ("NB", 4, 5))
         const("E0#0", 32, BIG)
         lin("sv", "cb", ("PB", 2, 3), float(C), 255.625)
         lin("sv", "lcb", ("PB", 2, 3), 1.0, 511.0)
 
     dst = T.cores[(rank - 1) % len(T.cores)]
     rid, pid = topo.addr(dst)[:2]
-    mask = topo.mask(core, dst)
-
-    def e_tile(b):
-        return ("E", 128 * b, 1.0 / 64) if b % 2 == 0 else ("EH", 64 * b - 64, 1.0)
+    used = topo.engines(core, dst)
+    mask = sum(1 << e for e in used)
 
     def pages(qs, name, h, a, b):
         gather("pg%d_%d" % (h, a), qs, T[name][:, XB + 4 * a + h:XB + 4 * b:2], T.YS[:, 2 * C * h:2 * C * h + 2 * C], T.LO[:, a // 8:b // 8],
@@ -249,7 +247,7 @@ def plan(g, core, T, topo):
 
     def window_copy(name, qs, b, bank, a, n, at):
         w0 = 2 * AWID * (b % 2) + b // 2 + 2 * at
-        scaled(name, qs, T.AW[:, w0:w0 + 2 * n - 1:2], T["p%d" % bank][:, a:a + n], e_tile(b)[2], [("p%d" % bank, 0, 512)], lanes("AW", at, at + n, (b,)))
+        scaled(name, qs, T.AW[:, w0:w0 + 2 * n - 1:2], T["p%d" % bank][:, a:a + n], 1.0, [("p%d" % bank, 0, 512)], lanes("AW", at, at + n, (b,)))
 
     def send(t, QB, QX):
         def fn(q):
@@ -257,18 +255,23 @@ def plan(g, core, T, topo):
                          remote_sem=T.sem["arr%d" % t], local_sem=T.sem["loc%d" % t], pid=pid, routing_id=rid, dma_engine_mask=mask)
             g.remote_dma(out_ap=T[QX + "p"][:, C:AWID], in_ap=T[QB + "p"][:, 0:K],
                          remote_sem=T.sem["arr%d" % t], local_sem=T.sem["loc%d" % t], pid=pid, routing_id=rid, dma_engine_mask=mask)
-            return 2 * len(topo.engines(core, dst))
+            return 2 * len(used)
         step("B>", "g", fn, [(QB, 0, K)], [(QX, C, AWID)], "arr%d" % t)
 
-    def add(h, b):
-        a = 128 * h
-        step("z%d%d" % (h, b), "v",
-             lambda q: V.tensor_tensor(T.ZT[:, 4 * a + b:4 * a + 512:4], T.AS[:, 2 * a + b // 2:2 * a + 256:2], T["p%d" % b][:, a:a + 128], A.add),
-             [("AS", 2 * a, 2 * a + 256), ("p%d" % b, 0, 512)], lanes("ZT", a, a + 128, (b,)))
+    def twin(h):
+        to, src = T.FH[:, C * h:C * h + C], T.AW[:, 2 * AWID * h:2 * AWID * h + C]
+        step("h%d" % h, "vs", lambda q: V.tensor_copy(to, src) if q == "v" else S.activation(to, src, F.Copy),
+             lanes("AW", 0, 128, (h, h + 2)), [("FH", C * h, C * h + C)])
 
-    def gather_add(a, b):
-        step("zz%d" % a, "v", lambda q: V.tensor_tensor(T.ZT[:, 4 * a:4 * b:2], T.AW[:, 0:2 * AWID].indirect(T.LC[:, a // 8:b // 8]), T.FH[:, 2 * a:2 * b], A.add),
-             lanes("AW", 0, AWID, (0, 2)) + lanes("FH", a, b, (0, 2)) + [("LC", 0, 32)], lanes("ZT", a, b, (0, 2)))
+    def gather_add(h):
+        step("zz%d" % h, "v", lambda q: V.tensor_tensor(T.ZT[:, h:512:2], T.AW[:, 2 * AWID * h:2 * AWID * (h + 1)].indirect(T.LC[:, 0:16]),
+                                                       T.FH[:, C * h:C * h + C], A.add),
+             lanes("AW", 0, AWID, (h, h + 2)) + [("FH", C * h, C * h + C), ("LC", 0, 32)], lanes("ZT", 0, 128, (h, h + 2)))
+
+    def add(b):
+        a = C * (b % 2)
+        step("z%d" % b, "v", lambda q: V.tensor_tensor(T.ZT[:, 512 + b:1024:4], T.AS[:, a + b // 2:a + C:2], T["p%d" % b][:, 128:C], A.add),
+             [("AS", a, a + C), ("p%d" % b, 0, 512)], lanes("ZT", 128, C, (b,)))
 
     for t in range(R):
         part[0] = str(t)
@@ -286,87 +289,82 @@ def plan(g, core, T, topo):
             pages("sv", XW, 1, SB, C)
         psum_scan("PK", 5, 0, 17)
         psum_scan("PC", 4, 32, 65)
-        ts(("MK", 0, 17), ("PK", 0, 17), ("PK", 16, 17), 4.0, A.is_lt, A.mult)
+        below("k", ("MK", 0, 81), ("PK", 0, 81), ("PK", 16, 17))
         ts("sg", ("PC", 32, 33), ("PC", 64, 65), 0.5, A.is_ge, A.subtract)
-        total("K4", ("MK", 0, 18))
-        ts(("MC", 0, 65), ("PC", 0, 65), ("PC", 64, 65), 4.0, A.is_lt, A.mult)
-        ts("B0#1", "Z", "K4", 2.0, A.is_gt, A.mult)
-        ts("B1#0", "Z2", "sg", "K4", A.mult, A.min)
-        total("C4", ("MC", 0, 66))
+        below("c", ("MC", 0, 65), ("PC", 0, 65), ("PC", 64, 65))
+        ts("B0#1", "Z", "k", 2.0, A.is_gt, A.mult)
+        ts("B1#0", "Z2", "sg", "k", A.mult, A.min)
+        ts("d", "c", "k", None, A.subtract)
         scan("BO", "B0", "B1", A.mult, A.add)
-        ts(("LB", 0, 16), "I1", "C4", "K4", A.add, A.subtract)
-        ts(("LB", 16, 24), "BO#1", "C4", "K4", A.add, A.subtract)
-        lin("vs", "cs", "CS", "C4", 0.0)
-        act("ae", "J4h", -1.0, "C4", F.Abs)
+        ts(("LB", 0, 16), "I1", "d", 4.0, A.add, A.mult)
+        ts(("LB", 16, 24), "BO#1", "d", 4.0, A.add, A.mult)
+        lin("vs", "cm", "c", 1.0, -160.0)
+        act(("ae", 0, 33), "Jh", -1.0, "c", F.Abs)
         allx = lanes(XW, -PAD, C + PAD)
         gather("Ba", "sv", T.BT[:, 0:16 * NS], T[XW][:, 0:XWID], T.LB[:, 0:NS], allx + [("LB", 0, NS)], lanes("BT", 0, 4 * NS))
         gather("Bb", "vs", T.BT[:, 16 * NS:384], T[XW][:, 0:XWID], T.LB[:, NS:24], allx + [("LB", NS, 24)], lanes("BT", 4 * NS, 96))
         quant("QB", QB, 0, 128, "BT", 0, lanes("BT", 0, 128))
         send(t, QB, QX)
-        quant("QX", QX, 0, C, XW, XB, lanes(XW, 0, C))
+        quant("QX", QX, 0, 128, XW, XB, lanes(XW, 0, 128))
+        quant("QXb", QX, 128, 128, XW, XB + 512, lanes(XW, 128, C))
         if t == 0:
             list_constants()
-        act("D0#1", ("J4h", 0, 32), -1.0, "C4", F.Sign)
-        act("D1#0", "ae", -1.0, "K4", F.Sign)
-        lin("sv", "D0#2", "Jq", -1.0, ("cs", 0, 1))
-        lin("sv", "D1#1", "NK", "K4", 0.0)
+        lin("sv", "cs", "CS", "cm", 0.0)
+        act("D0#1", ("Jh", 0, 32), -1.0, "c", F.Sign)
+        act("D1#0", "ae", -1.0, "k", F.Sign)
+        ts("D0#2", ("Jh", 0, 32), "c", -1.0 / 256, A.subtract, A.mult)
+        lin("sv", "D1#1", "NK", "k", 0.0)
         lin("sv", "L0#0", "JO", 1.0, ("D1", 97, 98))
-        act("E1#1", ("ae", 0, 32), -1.0, "K4", F.Abs)
-        lin("sv", "s", "K4", -2.0, ("ae", 32, 33))
+        act("E1#1", ("ae", 0, 32), -1.0 / 1024, ("D1", 100, 101), F.Abs)
+        lin("sv", "s", "k", -2.0, ("ae", 32, 33))
         if t == 0:
-            for name, b in (("E", 2), ("EH", 1), ("EH", 3), ("E", 1), ("E", 3)):
+            for name, b in (("EH", 2), ("EH", 1), ("EH", 3), ("E", 0), ("E", 2), ("E", 1), ("E", 3)):
                 e_quant(name, b)
-        lin("sv", "K4m", "K4", 1.0, -1.0)
+        lin("sv", "K4m", "k", 4.0, -1.0)
         for b in (0, 2, 1, 3):
-            e, ea, sc = e_tile(b)
-            mm("F%d" % b, b, C, e, ea, QX, 0)
+            mm("F%d" % b, b, C, "EH", 128 * b, QX, 0)
         for b in (0, 2, 1, 3):
             window_copy("f%d" % b, "sv", b, b, 0, C, 0)
-            if b == 0:
-                step("h0", "g", lambda q: g.affine_select(T.FH[:, 0:2 * C:2], T.AW[:, 0:2 * C:2], [[1, C]], A.is_ge, 0.0, 0, 0),
-                     lanes("AW", 0, C, (0,)), lanes("FH", 0, C, (0,)))
         scan("DO", "D0", ("D1", 0, 96), A.subtract, A.max)
         lin("vs", "L1#1", "J4O", 1.0, "s")
-        ts("pm", "DO#2", ("cs", 1, 2), 0.5, A.is_le, A.subtract)
-        lin("vs", "L0#1", "L1#1", 1.0 / 3, 1024.0 / 3 - 1.0)
+        ts("pm", "DO#2", ("cs", 0, 1), 0.5, A.is_le, A.subtract)
+        lin("vs", "L0#1", "L1#1", 1.0 / 3, 256.0 / 3 - 0.25)
         tt("dh", "DO#2", "pm", A.mult)
         scan("LM", "L0", "L1", A.max, A.max)
-        lin("vs", "E1#0", "dh", 2048.0, "C4")
-        copy(("NI", 0, 32), "LM#1")
-        call("vs", lambda q, o, a: V.tensor_scalar(o, a, -1024.0, BIG, A.is_lt, A.mult) if q == "v" else S.activation(o, a, F.Relu, bias=-1024 * BIG, scale=-BIG),
-             "E0#1", "E1#0")
+        lin("vs", "E1#0", "dh", 0.5, ("cs", 2, 3))
+        ts(("NI", 0, 32), "LM#1", 4.0, None, A.mult)
+        ts("E0#1", "dh", ("cs", 1, 2), -0.5, A.add, A.is_lt)
         ts(("HI", 0, 32), ("NI", 0, 32), 2, None, A.bitwise_and)
         scan("EO", "E0", "E1", A.add, A.min)
         ts(("PI", 0, 32), ("NI", 0, 32), 1, None, A.bitwise_and)
-        ts(("LC", 0, 32), "EO#1", 0.5, "lcb", A.mult, A.add)
-        scaled("h2", "vs", T.FH[:, 1:2 * C:2], T.p2[:, 0:C], 1.0 / 64, [("p2", 0, 512)], lanes("FH", 0, C, (2,)))
-        if t == 1:
+        ts(("LC", 0, 32), "EO#1", 2048.0, "lcb", A.mult, A.add)
+        twin(0)
+        twin(1)
+        if t == 0:
             quant("QV", "QV", 0, 128, "VT", 0, [("VT", 0, 512)])
         for b in (0, 2, 1, 3):
-            e, ea, sc = e_tile(b)
-            mm("G%d" % b, 4 + b, 128, e, ea, QX, AWID - 128)
+            mm("G%d" % b, 4 + b, 128, "EH", 128 * b, QX, AWID - 128)
             window_copy("g%d" % b, ("vs", "sv")[b % 2], b, 4 + b, 128 - K, K, C)
-        for b in (0, 2):
-            mm("X1%d" % b, b, 128, "E", 128 * b, QX, 128, True, False)
         for b in range(4):
             mm("X0%d" % b, 4 + b, 128, "E", 128 * b, QX, 0, True, False)
         ts("Et", ("HI", 0, 32), "K4m", -510.5, A.mult, A.add)
-        for h in range(2):
-            gather("A%d" % h, "s", T.AS[:, C * h:C * h + C], T.AW[:, 2 * AWID:4 * AWID], T.LC[:, 16 * h:16 * h + 16],
-                   lanes("AW", 0, AWID, (1, 3)) + [("LC", 0, 32)], [("AS", C * h, C * h + C)])
+        for h in (1, 0):
+            gather("A%d" % h, "s", T.AS[:, C * h:C * h + C], T.AW[:, 2 * AWID * h:2 * AWID * (h + 1)], T.LC[:, 16:32],
+                   lanes("AW", 0, AWID, (h, h + 2)) + [("LC", 0, 32)], [("AS", C * h, C * h + C)])
         if t == 0:
             for a, b in ((-PAD, 0), (C, C + PAD), (SB, 192)):
                 zeros("XW1", a, b)
-        gather_add(0, C)
+        gather_add(0)
+        gather_add(1)
         for h in range(2):
             a = 128 * h
-            for b in (1, 3):
-                add(h, b)
+            for b in ((1,), (3, 0, 2))[h]:
+                add(b)
             if h == 0:
                 tt("Dt", "Et", ("NI", 0, 32), A.add)
             else:
                 ts("gt", ("PI", 0, 32), -0.5, 0.25, A.mult, A.add)
-                for b in (1, 3):
+                for b in (1, 3, 0, 2):
                     mm("X1%d" % b, b, 128, "E", 128 * b, QX, 128, True, False)
             quant("QZ%d" % h, "QZ", a, 128, "ZT", 4 * a, lanes("ZT", a, a + 128))
             for b in range(4):
@@ -375,9 +373,9 @@ def plan(g, core, T, topo):
         for qs, h, b in (("sv", 0, 0), ("sv", 0, 1), ("sv", 0, 2), ("vs", 0, 3), ("sv", 1, 0), ("vs", 1, 1), ("sv", 1, 2), ("vs", 1, 3)):
             psum_copy("y%d%d" % (h, b), qs, "YS", C * (2 * (b % 2) + b // 2) + 128 * h, b + 4 - 4 * h, 128, 0.03125)
             if (h, b) == (0, 3):
-                ts(("LO", 0, 32), "gD", ("cs", 2, 3), "cb", A.add, A.add)
+                ts(("LO", 0, 32), "gD", "cm", "cb", A.add, A.add)
                 if last:
-                    ts("OF", "gD", ("cs", 2, 3), "cb", A.add, A.add)
+                    ts("OF", "gD", "cm", "cb", A.add, A.add)
         if last:
             call("v", lambda q, o, a: V.transpose(o, a), "OT", "OF")
         else:

@@ -9,30 +9,31 @@ BIG = 4096.0
 SA, SB = 64, 176
 NS = 14
 ORDER = """
-ad_u:s ad_xm:y ad_xa:y ad_xb:y ad_v:y ad_wc:y ad_ws:y aONE:v aJh32:s aEB:v aB0#0:v 0D1#2:s aIP:g aIB:v aPK17:s 0E0#0:s aIB2:v aIB3:v aae33:s aIB4:v 0D0#0:s
-aIB1:v aUI:g aCS:s aCS2:s 0XW1_0:s aM16:g aNEG:v aCS1:v aPB:v aBT0:s 0NK:s aNB:s aJ16:s 0lcb:s 0NK33:v 0XW1_224:v aUO:v aEBd:g aEB2:v aQU:v 0cb:v 0NK32:s aUc1:v
-aUc0:v aM8:g aJ:s aB1#1:s aQM:v aXW0_304:s aJh:s 0L1#0:s aZ0:s 0H3:v aUs1:s aUs0:s aI1:s 0S1:t 0H2:v aZ:s 0PK:v aXW0_0:s aJO:s 0S0:t 0PC:v 0J4O:v aZ2:s 0sg:v
-0k:s 0B0#1:v 0c:s 0B1#0:v 0d:v 0BO:v 0D1#1:s 0LB:v 0LB16:v 0D0#2:v 0K4m:s 0D0#1:s 0ae:s 0Bb:v 0cm:s 0D1#0:s 0DO:v 0Ba:s 0s:s 0QB:v 0cs:s 0pm:v 0QXb:v 0E1#1:s
-0L1#1:s 0XW1_304:s 0L0#1:s 0L0#0:s 0QX:v 0dh:v 0LM:v 0E1#0:s 0H1:v 0E0#1:v 0F2:t aH0:v 0F1:t 0F0:t 0NI:v 0F3:t 0EO:v 0B>:g 0E2:v 0PI:v 0HI:v 0f2:s 0LC:v 0f1:s
-0E0:v 0Et:v 0f0:s 0E1:v 0Dt:v 0G0:t 0f3:s 0gt:v 0h0:v 0gD:v 0E3:v 0h1:s 0LO:v 0G2:t 0g2:v 0g0:s 0G1:t 0g1:v 0zz0:v 0G3:t 0g3:s 0zz1:v 0A1:s 0z1:v 0X02:t 0A0:s
-0X01:t 0QZ0:v 0X03:t 0z3:v 0X00:t 0X11:t 0z0:v 0W00:t 0y00:s 0W01:t 0W02:t 0y01:s 0y02:s 0z2:v 0QZ1:v 0QV:v 0W03:t 0X13:t 0y03:s 0X12:t 0X10:t 0W10:t 0y10:v
-0W11:t 0W12:t 0y11:v 0W13:t 0y12:s 0pg0_64:s 0y13:v 0pg1_64:v 1QM:v 1S1:t 1pg1_0:v 1S0:t 1PK:v 1pg0_0:s 1pg1_176:s 1PC:v 1k:s 1QX:v 1c:s 1pg0_176:s 1sg:v
-1B0#1:v 1D0#1:s 1ae:s 1B1#0:v 1d:v 1BO:v 1D1#1:s 1LB:v 1LB16:v 1QXb:v 1F3:t 1Ba:s 1Bb:v 1s:s 1D1#0:s 1D0#2:v 1cm:s 1QB:v 1DO:v 1F1:t 1L1#1:s 1L0#0:s 1L0#1:v
-1F2:t 1cs:s 1B>:g 1K4m:v 1pm:v 1LM:v 1F0:t 1G2:t 1E1#1:s 1f1:s 1G0:t 1f2:s 1dh:v 1NI:v 1E1#0:s 1E0#1:v 1HI:v 1PI:v 1EO:v 1G1:t 1Et:v 1gt:v 1LC:v 1f0:s 1Dt:v
-1f3:s 1h0:s 1g2:s 1G3:t 1h1:v 1g1:s 1g3:s 1X02:t 1g0:v 1X00:t 1gD:v 1zz0:v 1zz1:v 1X01:t 1X03:t 1A1:s 1z1:v 1X11:t 1QZ0:v 1A0:s 1W01:t 1y01:s 1z3:v 1W02:t
-1W03:t 1z2:v 1y02:s 1W00:t 1z0:v 1LO:v 1X12:t 1X13:t 1QZ1:v 1X10:t 1W10:t 1y00:v 1W11:t 1W12:t 1y03:s 1y10:s 1y12:s 1W13:t 1y11:v 1y13:v 1pg1_64:v 1pg0_64:s
-2QM:v 2S1:t 2S0:t 2pg1_0:s 2pg1_176:s 2pg0_0:v 2PK:v 2PC:v 2k:s 2QX:v 2c:s 2pg0_176:s 2sg:v 2ae:s 2B0#1:v 2D0#1:s 2cm:s 2B1#0:v 2d:v 2BO:v 2LB:v 2Ba:s 2D1#1:s
-2s:s 2LB16:v 2D1#0:s 2QXb:v 2F3:t 2Bb:v 2D0#2:v 2QB:v 2L1#1:v 2cs:s 2L0#0:s 2F0:t 2B>:g 2DO:v 2L0#1:v 2pm:v 2LM:v 2dh:v 2NI:v 2E1#0:v 2F1:t 2K4m:s 2E0#1:v 2HI:v
-2F2:t 2E1#1:s 2PI:v 2f3:s 2f0:s 2EO:v 2f2:s 2G2:t 2G0:t 2Et:v 2f1:s 2gt:v 2G3:t 2h0:s 2g2:s 2LC:v 2Dt:v 2G1:t 2g3:s 2h1:v 2g1:s 2g0:v 2gD:v 2X02:t 2X00:t 2X03:t
-2X01:t 2zz0:v 2zz1:v 2A0:s 2z0:v 2QZ0:v 2X10:t 2W01:t 2A1:s 2W00:t 2W03:t 2y01:s 2W02:t 2y00:s 2z1:v 2y03:s 2z3:v 2z2:v 2X11:t 2y02:s 2QZ1:v 2X13:t 2X12:t
-2W10:t 2OF:v 2LO:v 2OT:v 2W11:t zOC:v zd_lo1:y 2W12:t 2W13:t 2y10:s 2y11:v 2y12:s zd_lo0:y 2y13:v zpg1_0:v zpg0_0:s zpg0_128:s zQX0:v zV0:t zd_oc0:y zy0:s
-zpg1_128:v zQX1:v zd_y0:y zd_oc1:y zV1:t zd_os0:s zd_os1:s zd_os2:s zd_os3:s zy1:v zd_y1:y
+ad_u:s ad_xm:y ad_xa:y ad_xb:y ad_v:y ad_wc:y aIP:g ad_ws:y aONE:v 0D1#2:s aUI:g 0NK33:s aEB:v aIB:v aJh32:s aIB2:v aM16:g aEBd:g aXW0_304:v aCS:s 0NK32:s
+0E0#0:s aIB4:v aB0#0:s 0XW1_224:s aM8:g 0TD:g aIB1:v aIB3:v aCS1:s aIB5:v 0NK:v aBT0:s 0XW1_304:s 0D0#0:v 0XW1_0:v aUO:v aCS2:s aXW0_0:s aPB:v aJ:s 0TK:g 0lcb:s
+aEB2:v aNB:s 0tq1:s aQU:v aJh:s 0J4O:s aNEG:v aJ16:v aUc1:v aQM:v aUs1:s aZ0:s aUc0:v 0TZ:g 0tq2:v aUs0:s 0S1:t aZ:v 0PK:v 0cb:s aZ2:s 0tj:s aPK17:s aB1#1:s
+0S0:t 0H2:v 0L1#0:s 0tq:s aI1:s 0PC:v 0k:s 0QX:v 0c:s 0D1#1:s aae33:s 0sg:v 0ae:s aJO:v 0D0#1:s 0B0#1:v 0TN:s 0B1#0:v 0d:v 0D0#2:v 0BO:v 0LB:v 0K4m:s 0cm:v
+0TA:s 0LB16:v 0Ba:s 0s:s 0cs:s 0QXb:v 0Bb:v 0D1#0:s 0L0#0:s 0H1:v 0L1#1:s 0QB:v 0F2:t 0DO:v 0E1#1:s 0H3:v 0L0#1:s 0F1:t 0F3:t 0pm:v 0B>:g 0LM:v aH0:v 0F0:t
+0f2:s 0dh:v 0NI:v 0f1:s 0E0:v 0E0#1:v 0PI:v 0E1#0:s 0HI:v 0TM:v 0gt:v 0Et:v 0G0:t 0G2:t 0f3:s 0EO:v 0E2:v 0Dt:v 0f0:s 0G3:t 0LC:v 0E3:v 0h1:s 0h0:s 0g0:s 0E1:v
+0g3:s 0G1:t 0gD:v 0TQ:v 0g1:s 0A1:s 0TP:v 0X00:t 0g2:v 0X02:t 0QV:v 0zz0:v 0X03:t 0zz1:v 0X01:t 0z1:v 0X11:t 0QZ0:v 0W01:t 0z3:v 0A0:s 0z0:v 0W02:t 0y01:s
+0y02:s 0W03:t 0y03:s 0W00:t 0z2:v 0X13:t 0X12:t 0y00:s 0LO:v 0X10:t 0QZ1:v 0TB136:v 0W12:t 0W10:t 0W11:t 0TB:v 0y10:s 0y12:v 0y11:s 0pg0_64:s 0W13:t 0y13:v
+1pg1_0:s 0pg1_64:v 1QM:v 1pg0_176:v 1pg0_0:s 1S1:t 1PK:v 1S0:t 1PC:v 1pg1_176:s 1QX:v 1sg:v 1k:s 1c:s 1QXb:v 1Ik:v 1D1#1:s 1TO:v 1K4m:s 1ae:s 1D0#2:v 1LB:v
+1D0#1:s 1cm:s 1LB16:v 1s:v 1L0#0:s 1D1#0:s 1Bb:v 1Ba:s 1F1:t 1cs:s 1F3:t 1L1#1:v 1E1#1:s 1DO:v 1L0#1:s 1F0:t 1f3:s 1QB:v 1pm:v 1f1:s 1F2:t 1B>:g 1LM:v 1G0:t
+1f0:s 1dh:v 1G2:t 1f2:s 1G3:t 1NI:v 1E1#0:v 1h0:s 1E0#1:v 1PI:v 1HI:v 1h1:v 1G1:t 1EO:v 1g0:s 1X00:t 1Et:v 1gt:v 1g3:s 1LC:v 1g1:s 1Dt:v 1gD:v 1g2:v 1A1:s 1LO:v
+1X02:t 1X03:t 1zz0:v 1zz1:v 1X01:t 1z1:v 1QZ0:v 1z3:v 1A0:s 1X11:t 1z2:v 1z0:v 1QZ1:v 1W01:t 1y01:s 1W00:t 1W03:t 1W02:t 1X12:t 1X10:t 1y02:v 1y00:s 1y03:s
+1X13:t 1W11:t 1y11:s 1W10:t 1y10:v 1W12:t 1y12:s 1W13:t 1y13:v 1pg1_64:v 1pg0_64:s 2pg1_0:s 2QM:v 2pg0_176:v 2pg0_0:s 2S1:t 2pg1_176:s 2S0:t 2PK:v 2k:s 2PC:v
+2c:s 2QX:v 2sg:v 2D1#1:s 2K4m:s 2QXb:v 2ae:s 2Ik:v 2D0#1:s 2L0#0:s 2cm:s 2D1#0:s 2TO:v 2F2:t 2D0#2:v 2LB:v 2LB16:v 2F0:t 2s:v 2Bb:v 2Ba:s 2L1#1:v 2F3:t 2E1#1:s
+2cs:v 2L0#1:s 2F1:t 2f0:s 2f1:s 2QB:v 2B>:g 2G0:t 2DO:v 2f3:s 2LM:v 2f2:s 2pm:v 2G2:t 2NI:v 2dh:v 2HI:v 2PI:v 2E0#1:v 2E1#0:v 2Et:v 2h1:s 2gt:v 2EO:v 2Dt:v
+2g0:s 2h0:v 2G1:t 2G3:t 2gD:v 2LC:v 2g2:v 2g1:s 2g3:s 2A0:s 2OF:v 2X00:t 2LO:v 2X02:t 2X01:t 2zz0:v 2X03:t 2zz1:v 2z2:v 2X12:t 2z0:v 2A1:s 2X10:t 2z1:v 2X11:t
+2z3:v 2QZ0:v 2OT:v 2X13:t 2QZ1:v 2W02:t zOC:v zd_lo1:y 2W01:t 2W00:t 2W10:t 2W03:t 2W11:t 2W12:t 2y01:v 2y02:s 2y00:s 2y10:v 2y11:v 2y03:s 2y12:s 2W13:t 2y13:v
+zd_lo0:y zpg1_0:v zpg1_128:v zpg0_0:s zQX0:v zd_oc0:y zV0:t zpg0_128:s zQX1:v zd_os0:s zd_oc1:y zV1:t zd_os1:s zd_os2:s zd_os3:s zy0:v zy1:v zd_y0:y zd_y1:y
 """
 
 WORK = {}
 _n = [0]
 for _name, _w, _m in (("NEG", 72, 1), ("PC", 72, 1), ("PK", 88, 1), ("MC", 72, 1), ("MK", 88, 1), ("c", 1, 1), ("k", 1, 1), ("cm", 1, 1), ("sg", 1, 1),
-                      ("d", 1, 1), ("PB", 5, 1), ("NB", 5, 1), ("M16", 16, 1), ("M8", 32, 1), ("J", 32, 1), ("Z0", 8, 1), ("cb", 1, 1), ("J16", 16, 1),
+                      ("d", 1, 1), ("Ik", 16, 1), ("tj", 1, 1), ("tq", 3, 1), ("TD", 136, 1), ("TK", 136, 1), ("TZ", 136, 1), ("TM", 136, 1),
+                      ("TA", 136, 1), ("TN", 136, 1), ("TP", 136, 1), ("TQ", 136, 1), ("PB", 6, 1), ("NB", 6, 1), ("M16", 16, 1), ("M8", 32, 1), ("J", 32, 1), ("Z0", 8, 1), ("cb", 1, 1), ("J16", 16, 1),
                       ("I1", 16, 1), ("Z", 8, 1), ("Z2", 8, 1), ("B0", 8, 2), ("B1", 8, 2), ("BO", 8, 2),
                       ("Jh", 33, 1), ("NK", 34, 1), ("CS", 3, 1), ("cs", 3, 1), ("ae", 34, 1), ("lcb", 1, 1),
                       ("D0", 32, 3), ("D1", 34, 3), ("DO", 32, 3), ("pm", 32, 1), ("dh", 32, 1), ("E0", 32, 2), ("E1", 32, 2), ("EO", 32, 2),
@@ -47,7 +48,7 @@ SCRATCH = {
     "IP": ("sbuf", [128, 1], "int32"), "IB": ("sbuf", [128, 8], "int32"), "UI": ("sbuf", [128, 16], "int32"),
     "NI": ("sbuf", [128, 32], "int32"), "PI": ("sbuf", [128, 32], "int32"), "HI": ("sbuf", [128, 32], "int32"),
     "YO": ("sbuf", [128, C], "float32"),
-    "UO": ("sbuf", [128, 16], "uint16"), "LB": ("sbuf", [128, 24], "uint16"),
+    "UO": ("sbuf", [128, 16], "uint16"), "LB": ("sbuf", [128, 32], "uint16"), "TO": ("sbuf", [128, 2], "uint16"), "TB": ("sbuf", [128, 272], "float32"),
     "LC": ("sbuf", [128, 32], "uint16"), "LO": ("sbuf", [128, 32], "uint16"),
     "ONE": ("sbuf", [128, 192], "bfloat16"), "EB": ("sbuf", [128, 516], "bfloat16"), "EB2": ("sbuf", [128, 516], "bfloat16"),
     "UT": ("sbuf", [128, 512], "bfloat16"), "VT": ("sbuf", [128, 512], "bfloat16"), "BT": ("sbuf", [128, 512], "bfloat16"),
@@ -162,18 +163,18 @@ def plan(g, core, T, topo):
     dma("s", "u", T.UT[:, 0:512], T.u[:, 0:512], [], [("UT", 0, 512)])
     for name, a, b in (("xm", 64, 192), ("xa", 0, 64), ("xb", 192, 256)):
         dma("y", name, T.XW0[:, XB + 4 * a:XB + 4 * b], T.x[:, 4 * a:4 * b], [], lanes("XW0", a, b))
-    dma("y", "v", T.VT[:, 0:512], T.v[:, 0:512], [], [("VT", 0, 512)])
+    dma("y", "v", T.VT[:, 0:512], T.v[:, 0:512], lanes("XW0", 64, 192), [("VT", 0, 512)])
     dma("y", "wc", T.Wc[:, 0:512].bitcast(dt.uint8), T.wc[:, 0:2048], [], [("W", 0, 512)])
     dma("y", "ws", T.Wp[:, 0:512], T.ws[:, 0:512], [], [("Ws", 0, 512)])
 
-    def iota(out, pattern, step=0):
-        call("g", lambda q, o: g.iota(o, pattern, 0, step, allow_small_or_imprecise_dtypes=True), out)
+    def iota(out, pattern, base=0, step=0):
+        call("g", lambda q, o: g.iota(o, pattern, base, step, allow_small_or_imprecise_dtypes=True), out)
 
     def const(out, n, val):
         lin("sv", out, ("ONE", 0, n), 0.0, val)
     call("v", lambda q, o: V.memset(o, 32.0), ("ONE", 0, 192))
     call("v", lambda q, o: V.memset(o, 0.0), ("EB", 0, 516))
-    iota(("IP", 0, 1), [[1, 1]], 1)
+    iota(("IP", 0, 1), [[1, 1]], 0, 1)
     iota(("UI", 0, 16), [[1, 2], [16, 8]])
     step("EBd", "g", lambda q: g.affine_select(T.EB[:, 4:516:4], T.ONE[:, 0:128], [[-1, 128]], A.is_equal, 0.0, 0, 1), [("ONE", 0, 192)], [("EB", 0, 516)])
     iota("M16", [[16, 16]])
@@ -184,7 +185,8 @@ def plan(g, core, T, topo):
     ts(("IB", 3, 4), ("IP", 0, 1), 1, 7, A.arith_shift_right, A.bitwise_and)
     ts(("IB", 4, 5), ("IP", 0, 1), 1, 1, A.arith_shift_right, A.bitwise_and)
     copy(("UO", 0, 16), ("UI", 0, 16))
-    copy("PB", ("IB", 0, 5))
+    ts(("IB", 5, 6), ("IP", 0, 1), 7, None, A.bitwise_and)
+    copy("PB", ("IB", 0, 6))
     scaled("BT0", "vs", T.BT[:, 384:512], T.ONE[:, 0:128], 0.0, [("ONE", 0, 192)], lanes("BT", 96, 128))
     lin("vs", "NB", "PB", -0.25, 0.0)
     const("NEG", 72, -1.0e29)
@@ -224,6 +226,22 @@ def plan(g, core, T, topo):
     for i, val in enumerate((-1.0 / 256, 1.0 / 512, 1.0 / 1024)):
         const(("CS", i, i + 1), 1, val)
 
+    def stack_table():
+        iota("TD", [[4, 8], [-1, 17]])
+        iota("TK", [[0, 8], [2, 17]], 128)
+        iota("TZ", [[-8, 8], [0, 17]])
+        lin("sv", "tj", ("PB", 5, 6), 17.0, -64.0)
+        lin("sv", ("tq", 0, 1), ("Z0", 0, 1), 1.0, 0.5)
+        lin("sv", ("tq", 1, 2), ("PB", 0, 1), 0.25, PAD + 96.0)
+        lin("sv", ("tq", 2, 3), ("Z0", 0, 1), -2.0, -129.0)
+        ts("TM", "TD", ("tq", 0, 1), 0.0, A.add, A.is_gt)
+        lin("sv", "TA", "TD", 1.0, ("tq", 1, 2))
+        lin("sv", "TN", "TZ", 1.0, ("tq", 2, 3))
+        tt("TP", "TM", "TK", A.mult)
+        tt("TQ", "TM", "TN", A.mult)
+        tt(("TB", 0, 136), "TP", "TA", A.add)
+        tt(("TB", 136, 272), "TQ", "TA", A.add)
+
     def list_constants():
         const(("NK", 0, 32), 32, -1.0 / 128)
         const(("NK", 32, 33), 1, -1.0)
@@ -239,7 +257,6 @@ def plan(g, core, T, topo):
     dst = T.cores[(rank - 1) % len(T.cores)]
     rid, pid = topo.addr(dst)[:2]
     used = topo.engines(core, dst)
-    mask = sum(1 << e for e in used)
 
     def pages(qs, name, h, a, b):
         gather("pg%d_%d" % (h, a), qs, T[name][:, XB + 4 * a + h:XB + 4 * b:2], T.YS[:, 2 * C * h:2 * C * h + 2 * C], T.LO[:, a // 8:b // 8],
@@ -251,11 +268,12 @@ def plan(g, core, T, topo):
 
     def send(t, QB, QX):
         def fn(q):
-            g.remote_dma(out_ap=T[QX + "c"][:, C:AWID].bitcast(dt.uint8), in_ap=T[QB + "c"][:, 0:K].bitcast(dt.uint8),
-                         remote_sem=T.sem["arr%d" % t], local_sem=T.sem["loc%d" % t], pid=pid, routing_id=rid, dma_engine_mask=mask)
-            g.remote_dma(out_ap=T[QX + "p"][:, C:AWID], in_ap=T[QB + "p"][:, 0:K],
-                         remote_sem=T.sem["arr%d" % t], local_sem=T.sem["loc%d" % t], pid=pid, routing_id=rid, dma_engine_mask=mask)
-            return 2 * len(used)
+            codes, scales = (used[0::2], used[1::2]) if t == 0 else (used, used)
+            g.remote_dma(out_ap=T[QX + "c"][:, C:AWID].bitcast(dt.uint8), in_ap=T[QB + "c"][:, 0:K].bitcast(dt.uint8), remote_sem=T.sem["arr%d" % t],
+                         local_sem=T.sem["loc%d" % t], pid=pid, routing_id=rid, dma_engine_mask=sum(1 << e for e in codes))
+            g.remote_dma(out_ap=T[QX + "p"][:, C:AWID], in_ap=T[QB + "p"][:, 0:K], remote_sem=T.sem["arr%d" % t],
+                         local_sem=T.sem["loc%d" % t], pid=pid, routing_id=rid, dma_engine_mask=sum(1 << e for e in scales))
+            return len(codes) + len(scales)
         step("B>", "g", fn, [(QB, 0, K)], [(QX, C, AWID)], "arr%d" % t)
 
     def twin(h):
@@ -290,14 +308,22 @@ def plan(g, core, T, topo):
         psum_scan("PK", 5, 0, 17)
         psum_scan("PC", 4, 32, 65)
         below("k", ("MK", 0, 81), ("PK", 0, 81), ("PK", 16, 17))
-        ts("sg", ("PC", 32, 33), ("PC", 64, 65), 0.5, A.is_ge, A.subtract)
         below("c", ("MC", 0, 65), ("PC", 0, 65), ("PC", 64, 65))
-        ts("B0#1", "Z", "k", 2.0, A.is_gt, A.mult)
-        ts("B1#0", "Z2", "sg", "k", A.mult, A.min)
-        ts("d", "c", "k", None, A.subtract)
-        scan("BO", "B0", "B1", A.mult, A.add)
-        ts(("LB", 0, 16), "I1", "d", 4.0, A.add, A.mult)
-        ts(("LB", 16, 24), "BO#1", "d", 4.0, A.add, A.mult)
+        if t == 0:
+            ts("sg", ("PC", 32, 33), ("PC", 64, 65), 0.5, A.is_ge, A.subtract)
+            ts("B0#1", "Z", "k", 2.0, A.is_gt, A.mult)
+            ts("B1#0", "Z2", "sg", "k", A.mult, A.min)
+            ts("d", "c", "k", None, A.subtract)
+            scan("BO", "B0", "B1", A.mult, A.add)
+            ts(("LB", 0, 16), "I1", "d", 4.0, A.add, A.mult)
+            ts(("LB", 16, 24), "BO#1", "d", 4.0, A.add, A.mult)
+        else:
+            ts("sg", ("PC", 32, 33), ("PC", 64, 65), 136.0, A.is_lt, A.mult)
+            ts(("TO", 0, 1), "tj", "k", "sg", A.add, A.add)
+            ts("Ik", "I1", "k", None, A.subtract)
+            step("LB16", "v", lambda q: V.tensor_scalar(T.LB[:, 16:32], T.TB[:, 0:272].indirect(T.TO[:, 0:1]), opd("c")[0], 4.0, A.add, A.mult),
+                 [("TB", 0, 272), ("TO", 0, 1), ("c", 0, 1)], [("LB", 16, 32)])
+            ts(("LB", 0, 16), "Ik", "c", 4.0, A.add, A.mult)
         lin("vs", "cm", "c", 1.0, -160.0)
         act(("ae", 0, 33), "Jh", -1.0, "c", F.Abs)
         allx = lanes(XW, -PAD, C + PAD)
@@ -309,6 +335,7 @@ def plan(g, core, T, topo):
         quant("QXb", QX, 128, 128, XW, XB + 512, lanes(XW, 128, C))
         if t == 0:
             list_constants()
+            stack_table()
         lin("sv", "cs", "CS", "cm", 0.0)
         act("D0#1", ("Jh", 0, 32), -1.0, "c", F.Sign)
         act("D1#0", "ae", -1.0, "k", F.Sign)

from concourse.mybir import dt, AluOpType as A, ActivationFunctionType as F

R, C, K = 3, 256, 96
PAD = 48
XWID = 4 * (C + 2 * PAD)
XB = 4 * PAD
AWID = C + K
BIG = 4096.0
SA, SB = 64, 176
NS = 14
ORDER = """
ad_u:s ad_xm:y ad_xa:y ad_xb:y ad_v:y ad_wc:y aIP:g ad_ws:y aONE:v 0D1#2:s aUI:g 0NK33:s aEB:v aIB:v aJh32:s aIB2:v aM16:g aEBd:g aXW0_304:v aCS:s 0NK32:s
0E0#0:s aIB4:v aB0#0:s 0XW1_224:s aM8:g 0TD:g aIB1:v aIB3:v aCS1:s aIB5:v 0NK:v aBT0:s 0XW1_304:s 0D0#0:v 0XW1_0:v aUO:v aCS2:s aXW0_0:s aPB:v aJ:s 0TK:g 0lcb:s
aEB2:v aNB:s 0tq1:s aQU:v aJh:s 0J4O:s aNEG:v aJ16:v aUc1:v aQM:v aUs1:s aZ0:s aUc0:v 0TZ:g 0tq2:v aUs0:s 0S1:t aZ:v 0PK:v 0cb:s aZ2:s 0tj:s aPK17:s aB1#1:s
0S0:t 0H2:v 0L1#0:s 0tq:s aI1:s 0PC:v 0k:s 0QX:v 0c:s 0D1#1:s aae33:s 0sg:v 0ae:s aJO:v 0D0#1:s 0B0#1:v 0TN:s 0B1#0:v 0d:v 0D0#2:v 0BO:v 0LB:v 0K4m:s 0cm:v
0TA:s 0LB16:v 0Ba:s 0s:s 0cs:s 0QXb:v 0Bb:v 0D1#0:s 0L0#0:s 0H1:v 0L1#1:s 0QB:v 0F2:t 0DO:v 0E1#1:s 0H3:v 0L0#1:s 0F1:t 0F3:t 0pm:v 0B>:g 0LM:v aH0:v 0F0:t
0f2:s 0dh:v 0NI:v 0f1:s 0E0:v 0E0#1:v 0PI:v 0E1#0:s 0HI:v 0TM:v 0gt:v 0Et:v 0G0:t 0G2:t 0f3:s 0EO:v 0E2:v 0Dt:v 0f0:s 0G3:t 0LC:v 0E3:v 0h1:s 0h0:s 0g0:s 0E1:v
0g3:s 0G1:t 0gD:v 0TQ:v 0g1:s 0A1:s 0TP:v 0X00:t 0g2:v 0X02:t 0QV:v 0zz0:v 0X03:t 0zz1:v 0X01:t 0z1:v 0X11:t 0QZ0:v 0W01:t 0z3:v 0A0:s 0z0:v 0W02:t 0y01:s
0y02:s 0W03:t 0y03:s 0W00:t 0z2:v 0X13:t 0X12:t 0y00:s 0LO:v 0X10:t 0QZ1:v 0TB136:v 0W12:t 0W10:t 0W11:t 0TB:v 0y10:s 0y12:v 0y11:s 0pg0_64:s 0W13:t 0y13:v
1pg1_0:s 0pg1_64:v 1QM:v 1pg0_176:v 1pg0_0:s 1S1:t 1PK:v 1S0:t 1PC:v 1pg1_176:s 1QX:v 1sg:v 1k:s 1c:s 1QXb:v 1Ik:v 1D1#1:s 1TO:v 1K4m:s 1ae:s 1D0#2:v 1LB:v
1D0#1:s 1cm:s 1LB16:v 1s:v 1L0#0:s 1D1#0:s 1Bb:v 1Ba:s 1F1:t 1cs:s 1F3:t 1L1#1:v 1E1#1:s 1DO:v 1L0#1:s 1F0:t 1f3:s 1QB:v 1pm:v 1f1:s 1F2:t 1B>:g 1LM:v 1G0:t
1f0:s 1dh:v 1G2:t 1f2:s 1G3:t 1NI:v 1E1#0:v 1h0:s 1E0#1:v 1PI:v 1HI:v 1h1:v 1G1:t 1EO:v 1g0:s 1X00:t 1Et:v 1gt:v 1g3:s 1LC:v 1g1:s 1Dt:v 1gD:v 1g2:v 1A1:s 1LO:v
1X02:t 1X03:t 1zz0:v 1zz1:v 1X01:t 1z1:v 1QZ0:v 1z3:v 1A0:s 1X11:t 1z2:v 1z0:v 1QZ1:v 1W01:t 1y01:s 1W00:t 1W03:t 1W02:t 1X12:t 1X10:t 1y02:v 1y00:s 1y03:s
1X13:t 1W11:t 1y11:s 1W10:t 1y10:v 1W12:t 1y12:s 1W13:t 1y13:v 1pg1_64:v 1pg0_64:s 2pg1_0:s 2QM:v 2pg0_176:v 2pg0_0:s 2S1:t 2pg1_176:s 2S0:t 2PK:v 2k:s 2PC:v
2c:s 2QX:v 2sg:v 2D1#1:s 2K4m:s 2QXb:v 2ae:s 2Ik:v 2D0#1:s 2L0#0:s 2cm:s 2D1#0:s 2TO:v 2F2:t 2D0#2:v 2LB:v 2LB16:v 2F0:t 2s:v 2Bb:v 2Ba:s 2L1#1:v 2F3:t 2E1#1:s
2cs:v 2L0#1:s 2F1:t 2f0:s 2f1:s 2QB:v 2B>:g 2G0:t 2DO:v 2f3:s 2LM:v 2f2:s 2pm:v 2G2:t 2NI:v 2dh:v 2HI:v 2PI:v 2E0#1:v 2E1#0:v 2Et:v 2h1:s 2gt:v 2EO:v 2Dt:v
2g0:s 2h0:v 2G1:t 2G3:t 2gD:v 2LC:v 2g2:v 2g1:s 2g3:s 2A0:s 2OF:v 2X00:t 2LO:v 2X02:t 2X01:t 2zz0:v 2X03:t 2zz1:v 2z2:v 2X12:t 2z0:v 2A1:s 2X10:t 2z1:v 2X11:t
2z3:v 2QZ0:v 2OT:v 2X13:t 2QZ1:v 2W02:t zOC:v zd_lo1:y 2W01:t 2W00:t 2W10:t 2W03:t 2W11:t 2W12:t 2y01:v 2y02:s 2y00:s 2y10:v 2y11:v 2y03:s 2y12:s 2W13:t 2y13:v
zd_lo0:y zpg1_0:v zpg1_128:v zpg0_0:s zQX0:v zd_oc0:y zV0:t zpg0_128:s zQX1:v zd_os0:s zd_oc1:y zV1:t zd_os1:s zd_os2:s zd_os3:s zy0:v zy1:v zd_y0:y zd_y1:y
"""

WORK = {}
_n = [0]
for _name, _w, _m in (("NEG", 72, 1), ("PC", 72, 1), ("PK", 88, 1), ("MC", 72, 1), ("MK", 88, 1), ("c", 1, 1), ("k", 1, 1), ("cm", 1, 1), ("sg", 1, 1),
                      ("d", 1, 1), ("Ik", 16, 1), ("tj", 1, 1), ("tq", 3, 1), ("TD", 136, 1), ("TK", 136, 1), ("TZ", 136, 1), ("TM", 136, 1),
                      ("TA", 136, 1), ("TN", 136, 1), ("TP", 136, 1), ("TQ", 136, 1), ("PB", 6, 1), ("NB", 6, 1), ("M16", 16, 1), ("M8", 32, 1), ("J", 32, 1), ("Z0", 8, 1), ("cb", 1, 1), ("J16", 16, 1),
                      ("I1", 16, 1), ("Z", 8, 1), ("Z2", 8, 1), ("B0", 8, 2), ("B1", 8, 2), ("BO", 8, 2),
                      ("Jh", 33, 1), ("NK", 34, 1), ("CS", 3, 1), ("cs", 3, 1), ("ae", 34, 1), ("lcb", 1, 1),
                      ("D0", 32, 3), ("D1", 34, 3), ("DO", 32, 3), ("pm", 32, 1), ("dh", 32, 1), ("E0", 32, 2), ("E1", 32, 2), ("EO", 32, 2),
                      ("s", 1, 1), ("K4m", 1, 1),
                      ("JO", 32, 1), ("J4O", 32, 1), ("L0", 32, 2), ("L1", 32, 2), ("LM", 32, 2), ("Et", 32, 1), ("gt", 32, 1),
                      ("Dt", 32, 1), ("gD", 32, 1), ("OF", 32, 1), ("OT", 16, 2), ("OC", 16, 1)):
    WORK[_name] = (_n[0], _w, _m)
    _n[0] += -(-_w * _m // 8) * 8

SCRATCH = {
    "wk": ("sbuf", [128, _n[0]], "float32"),
    "IP": ("sbuf", [128, 1], "int32"), "IB": ("sbuf", [128, 8], "int32"), "UI": ("sbuf", [128, 16], "int32"),
    "NI": ("sbuf", [128, 32], "int32"), "PI": ("sbuf", [128, 32], "int32"), "HI": ("sbuf", [128, 32], "int32"),
    "YO": ("sbuf", [128, C], "float32"),
    "UO": ("sbuf", [128, 16], "uint16"), "LB": ("sbuf", [128, 32], "uint16"), "TO": ("sbuf", [128, 2], "uint16"), "TB": ("sbuf", [128, 272], "float32"),
    "LC": ("sbuf", [128, 32], "uint16"), "LO": ("sbuf", [128, 32], "uint16"),
    "ONE": ("sbuf", [128, 192], "bfloat16"), "EB": ("sbuf", [128, 516], "bfloat16"), "EB2": ("sbuf", [128, 516], "bfloat16"),
    "UT": ("sbuf", [128, 512], "bfloat16"), "VT": ("sbuf", [128, 512], "bfloat16"), "BT": ("sbuf", [128, 512], "bfloat16"),
    "ZT": ("sbuf", [128, 4 * C], "bfloat16"), "YS": ("sbuf", [128, 4 * C], "bfloat16"), "AW": ("sbuf", [128, 4 * AWID], "bfloat16"),
    "FH": ("sbuf", [128, 2 * C], "bfloat16"), "AS": ("sbuf", [128, 2 * C], "bfloat16"),
}
for _name, _w in (("E", 512), ("EH", 512), ("QU", 128), ("UC", 256), ("QV", 128), ("W", 512), ("QZ", 256), ("QM0", 128), ("QM1", 128),
                  ("QM2", 128), ("QX0", AWID), ("QX1", AWID), ("QX2", AWID), ("QX3", C), ("QB0", 128), ("QB1", 128), ("QB2", 128)):
    SCRATCH[_name + "c"] = ("sbuf", [128, _w], "float8_e4m3fn_x4")
    SCRATCH[_name + "p"] = ("sbuf", [128, _w], "uint8")
for _t in range(2):
    SCRATCH["XW%d" % _t] = ("sbuf", [128, XWID], "bfloat16")
for _b in range(8):
    SCRATCH["p%d" % _b] = ("psum", [128, 512], "float32")
LOADS = ["xm", "xa", "xb", "u", "v", "wc", "ws"]
STORES = ["oc0", "oc1", "os0", "os1", "os2", "os3", "y0", "y1", "lo0", "lo1"]
SEMAPHORES = ["cv", "cs", "ct", "cg"] + ["d_" + n for n in LOADS + STORES] + ["arr%d" % t for t in range(R)] + ["loc%d" % t for t in range(R)]


def plan(g, core, T, topo):
    rank = T.rank_of(core)
    V, S, P = g.vector, g.scalar, g.tensor
    queue = {"v": V, "s": S, "t": P, "g": g, "y": g.sync}
    steps = {}
    part = ["a"]

    def step(name, qs, fn, rd, wr, kind="c"):
        name = part[0] + name
        assert name not in steps
        steps[name] = (kind, qs, fn, rd, wr)

    def dma(qs, name, out, in_, rd, wr):
        step("d_" + name, qs, lambda q: queue[q].dma_start(out, in_), rd, wr, "d_" + name)

    def opd(x):
        if isinstance(x, str):
            name, _, slot = x.partition("#")
            a, w, m = WORK[name]
            if slot:
                return T.wk[:, a + int(slot):a + w * m:m], [(x, 0, w)]
            return T.wk[:, a:a + w * m], [(x, 0, w)] if m == 1 else [("%s#%d" % (x, i), 0, w) for i in range(m)]
        if x[0] in WORK:
            a, w, m = WORK[x[0]]
            return T.wk[:, a + x[1]:a + x[2]], [x] if m == 1 else [("%s#%d" % (x[0], i), 0, w) for i in range(m) if x[2] - x[1] > 1 or x[1] % m == i]
        return T[x[0]][:, x[1]:x[2]], [x]

    def call(qs, fn, out, *ins):
        o, wr = opd(out)
        rd, args = [], []
        for x in ins:
            if isinstance(x, (str, tuple)):
                x, r = opd(x)
                rd += r
            args.append(x)
        step(out if isinstance(out, str) else out[0] + str(out[1] or ""), qs, lambda q: fn(q, o, *args), rd, wr)

    def lanes(name, a, b, which=range(4)):
        return [(name + "#%d" % i, a, b) for i in which]

    def ts(out, in0, s1, s2, op0, op1=None):
        if op1 is None:
            call("v", lambda q, o, x, a: V.tensor_scalar(o, x, a, None, op0), out, in0, s1)
        else:
            call("v", lambda q, o, x, a, b: V.tensor_scalar(o, x, a, b, op0, op1), out, in0, s1, s2)

    def tt(out, x, y, op):
        call("v", lambda q, o, a, b: V.tensor_tensor(o, a, b, op), out, x, y)

    def scan(out, x, y, op0, op1, first=0.0):
        call("v", lambda q, o, a, b: V.tensor_tensor_scan(o, a, b, first, op0, op1), out, x, y)

    def below(out, signs, x, top):
        (o, wr), (sg, wr2), (a, rd), (b, rd2) = opd(out), opd(signs), opd(x), opd(top)
        step(out, "s", lambda q: S.activation(sg, a, F.Sign, bias=b, scale=-1.0, accum_out=o), rd + rd2, wr + wr2)

    def copy(out, x):
        call("v", lambda q, o, a: V.tensor_copy(o, a), out, x)

    def act(out, x, scale, bias, func):
        call("s", lambda q, o, a, sc, bi: S.activation(o, a, func, bias=bi, scale=sc), out, x, scale, bias)

    def times_plus(q, o, a, sc, bi):
        return V.tensor_scalar(o, a, sc, bi, A.mult, A.add) if q == "v" else S.activation(o, a, F.Identity, bias=bi, scale=sc)

    def lin(qs, out, x, scale, bias):
        call(qs, times_plus, out, x, scale, bias)

    def scaled(name, qs, to, src, sc, rd, wr):
        step(name, qs, lambda q: V.tensor_scalar(to, src, sc, None, A.mult) if q == "v" else S.activation(to, src, F.Copy, scale=sc), rd, wr)

    def quant(name, dst, a, n, src, sa, rd):
        step(name, "v", lambda q: V.quantize_mx(T[dst + "c"][:, a:a + n], T[dst + "p"][:, a:a + n], T[src][:, sa:sa + 4 * n]), rd, [(dst, a, a + n)])

    def mm(name, bank, n, st, sa, mv, ma, start=True, stop=True):
        step(name, "t", lambda q: P.matmul_mx(T["p%d" % bank][:, 0:n], T[st + "c"][:, sa:sa + 128], T[st + "p"][:, sa:sa + 128],
                                              T[mv + "c"][:, ma:ma + n], T[mv + "p"][:, ma:ma + n], start, stop),
             [(st, sa, sa + 128), (st + "s", sa, sa + 128), (mv, ma, ma + n)], [("p%d" % bank, 0, 512)])

    def zeros(name, a, b):
        scaled("%s_%d" % (name, a + PAD), "sv", T[name][:, XB + 4 * a:XB + 4 * b], T.ONE[:, 0:4 * (b - a)], 0.0, [("ONE", 0, 192)], lanes(name, a, b))

    def psum_copy(name, qs, out, oa, bank, n, scale):
        scaled(name, qs, T[out][:, oa:oa + n], T["p%d" % bank][:, 0:n], scale, [("p%d" % bank, 0, 512)], [(out, oa, oa + n)])

    def gather(name, qs, out, win, off, rd, wr):
        step(name, qs, lambda q: V.tensor_copy(out, win.indirect(off)) if q == "v" else S.activation(out, win.indirect(off), F.Copy), rd, wr)

    def psum_scan(out, bank, a, n):
        step(out, "v", lambda q: V.tensor_tensor_scan(opd((out, 0, n))[0], T["p%d" % bank][:, a:a + n], opd(("NEG", 0, n))[0], -1.0e29, A.max, A.max),
             [("p%d" % bank, 0, 512), ("NEG", 0, 72)], [(out, 0, n)])

    dma("s", "u", T.UT[:, 0:512], T.u[:, 0:512], [], [("UT", 0, 512)])
    for name, a, b in (("xm", 64, 192), ("xa", 0, 64), ("xb", 192, 256)):
        dma("y", name, T.XW0[:, XB + 4 * a:XB + 4 * b], T.x[:, 4 * a:4 * b], [], lanes("XW0", a, b))
    dma("y", "v", T.VT[:, 0:512], T.v[:, 0:512], lanes("XW0", 64, 192), [("VT", 0, 512)])
    dma("y", "wc", T.Wc[:, 0:512].bitcast(dt.uint8), T.wc[:, 0:2048], [], [("W", 0, 512)])
    dma("y", "ws", T.Wp[:, 0:512], T.ws[:, 0:512], [], [("Ws", 0, 512)])

    def iota(out, pattern, base=0, step=0):
        call("g", lambda q, o: g.iota(o, pattern, base, step, allow_small_or_imprecise_dtypes=True), out)

    def const(out, n, val):
        lin("sv", out, ("ONE", 0, n), 0.0, val)
    call("v", lambda q, o: V.memset(o, 32.0), ("ONE", 0, 192))
    call("v", lambda q, o: V.memset(o, 0.0), ("EB", 0, 516))
    iota(("IP", 0, 1), [[1, 1]], 0, 1)
    iota(("UI", 0, 16), [[1, 2], [16, 8]])
    step("EBd", "g", lambda q: g.affine_select(T.EB[:, 4:516:4], T.ONE[:, 0:128], [[-1, 128]], A.is_equal, 0.0, 0, 1), [("ONE", 0, 192)], [("EB", 0, 516)])
    iota("M16", [[16, 16]])
    iota("M8", [[8, 32]])
    ts(("IB", 0, 1), ("IP", 0, 1), 15, None, A.bitwise_and)
    ts(("IB", 1, 2), ("IP", 0, 1), 3, None, A.bitwise_and)
    ts(("IB", 2, 3), ("IP", 0, 1), 1, None, A.bitwise_and)
    ts(("IB", 3, 4), ("IP", 0, 1), 1, 7, A.arith_shift_right, A.bitwise_and)
    ts(("IB", 4, 5), ("IP", 0, 1), 1, 1, A.arith_shift_right, A.bitwise_and)
    copy(("UO", 0, 16), ("UI", 0, 16))
    ts(("IB", 5, 6), ("IP", 0, 1), 7, None, A.bitwise_and)
    copy("PB", ("IB", 0, 6))
    scaled("BT0", "vs", T.BT[:, 384:512], T.ONE[:, 0:128], 0.0, [("ONE", 0, 192)], lanes("BT", 96, 128))
    lin("vs", "NB", "PB", -0.25, 0.0)
    const("NEG", 72, -1.0e29)
    const(("PK", 17, 81), 64, -1.0e29)
    const(("ae", 33, 34), 1, 0.0)
    const("B0#0", 8, 0.0)
    zeros("XW0", -PAD, 0)
    zeros("XW0", C, C + PAD)
    scaled("EB2", "sv", T.EB2[:, 0:516], T.EB[:, 0:516], 1.0 / 64, [("EB", 0, 516)], [("EB2", 0, 516)])
    quant("QU", "QU", 0, 128, "UT", 0, [("UT", 0, 512)])

    def pick(h):
        off = T.UO[:, 8 * h:8 * h + 8]
        gather("Us%d" % h, "s", T.UCp[:, 128 * h:128 * h + 128], T.QUp[:, 0:128], off, [("QU", 0, 128), ("UO", 0, 16)], [("UCs", 128 * h, 128 * h + 128)])
        gather("Uc%d" % h, "v", T.UCc[:, 128 * h:128 * h + 128].bitcast(dt.uint32), T.QUc[:, 0:128].bitcast(dt.uint32), off,
               [("QU", 0, 128), ("UO", 0, 16)], [("UC", 128 * h, 128 * h + 128)])

    def e_quant(name, b):
        if name == "E":
            quant("E%d" % b, "E", 128 * b, 128, "EB", 4 - b, [("EB", 0, 516)])
        else:
            quant("H%d" % b, "EH", 128 * b, 128, "EB2", 4 - b, [("EB2", 0, 516)])
    pick(1)
    quant("QM", "QM0", 0, 128, "XW0", XB + 4 * 64, lanes("XW0", 64, 192))
    pick(0)
    e_quant("EH", 0)
    lin("sv", "J16", "M16", 1.0, ("PB", 0, 1))
    lin("sv", "J", "M8", 1.0, ("PB", 3, 4))
    lin("sv", "Z0", ("J16", 0, 8), 0.25, ("NB", 1, 2))
    lin("sv", "I1", "J16", 0.25, PAD + 96.0)
    lin("sv", "B1#1", ("J16", 0, 8), 0.25, PAD + 160.0)
    lin("sv", "Z2", "Z0", 2.0, 129.0)
    lin("sv", "Z", "Z0", 1.0, 64.5)
    lin("sv", "JO", "J", 0.25, 128.0)
    lin("sv", ("Jh", 0, 32), "J", 1.0, -95.5)
    const(("Jh", 32, 33), 1, 31.875)
    for i, val in enumerate((-1.0 / 256, 1.0 / 512, 1.0 / 1024)):
        const(("CS", i, i + 1), 1, val)

    def stack_table():
        iota("TD", [[4, 8], [-1, 17]])
        iota("TK", [[0, 8], [2, 17]], 128)
        iota("TZ", [[-8, 8], [0, 17]])
        lin("sv", "tj", ("PB", 5, 6), 17.0, -64.0)
        lin("sv", ("tq", 0, 1), ("Z0", 0, 1), 1.0, 0.5)
        lin("sv", ("tq", 1, 2), ("PB", 0, 1), 0.25, PAD + 96.0)
        lin("sv", ("tq", 2, 3), ("Z0", 0, 1), -2.0, -129.0)
        ts("TM", "TD", ("tq", 0, 1), 0.0, A.add, A.is_gt)
        lin("sv", "TA", "TD", 1.0, ("tq", 1, 2))
        lin("sv", "TN", "TZ", 1.0, ("tq", 2, 3))
        tt("TP", "TM", "TK", A.mult)
        tt("TQ", "TM", "TN", A.mult)
        tt(("TB", 0, 136), "TP", "TA", A.add)
        tt(("TB", 136, 272), "TQ", "TA", A.add)

    def list_constants():
        const(("NK", 0, 32), 32, -1.0 / 128)
        const(("NK", 32, 33), 1, -1.0)
        const(("NK", 33, 34), 1, 1.0 / 1024)
        const("D0#0", 32, -BIG)
        const("D1#2", 34, -BIG)
        lin("sv", "J4O", "J", 1.0, 0.625)
        lin("sv", "L1#0", "J", 0.5, ("NB", 4, 5))
        const("E0#0", 32, BIG)
        lin("sv", "cb", ("PB", 2, 3), float(C), 255.625)
        lin("sv", "lcb", ("PB", 2, 3), 1.0, 511.0)

    dst = T.cores[(rank - 1) % len(T.cores)]
    rid, pid = topo.addr(dst)[:2]
    used = topo.engines(core, dst)

    def pages(qs, name, h, a, b):
        gather("pg%d_%d" % (h, a), qs, T[name][:, XB + 4 * a + h:XB + 4 * b:2], T.YS[:, 2 * C * h:2 * C * h + 2 * C], T.LO[:, a // 8:b // 8],
               [("YS", 2 * C * h, 2 * C * h + 2 * C), ("LO", 0, 32)], lanes(name, a, b, (h, h + 2)))

    def window_copy(name, qs, b, bank, a, n, at):
        w0 = 2 * AWID * (b % 2) + b // 2 + 2 * at
        scaled(name, qs, T.AW[:, w0:w0 + 2 * n - 1:2], T["p%d" % bank][:, a:a + n], 1.0, [("p%d" % bank, 0, 512)], lanes("AW", at, at + n, (b,)))

    def send(t, QB, QX):
        def fn(q):
            codes, scales = (used[0::2], used[1::2]) if t == 0 else (used, used)
            g.remote_dma(out_ap=T[QX + "c"][:, C:AWID].bitcast(dt.uint8), in_ap=T[QB + "c"][:, 0:K].bitcast(dt.uint8), remote_sem=T.sem["arr%d" % t],
                         local_sem=T.sem["loc%d" % t], pid=pid, routing_id=rid, dma_engine_mask=sum(1 << e for e in codes))
            g.remote_dma(out_ap=T[QX + "p"][:, C:AWID], in_ap=T[QB + "p"][:, 0:K], remote_sem=T.sem["arr%d" % t],
                         local_sem=T.sem["loc%d" % t], pid=pid, routing_id=rid, dma_engine_mask=sum(1 << e for e in scales))
            return len(codes) + len(scales)
        step("B>", "g", fn, [(QB, 0, K)], [(QX, C, AWID)], "arr%d" % t)

    def twin(h):
        to, src = T.FH[:, C * h:C * h + C], T.AW[:, 2 * AWID * h:2 * AWID * h + C]
        step("h%d" % h, "vs", lambda q: V.tensor_copy(to, src) if q == "v" else S.activation(to, src, F.Copy),
             lanes("AW", 0, 128, (h, h + 2)), [("FH", C * h, C * h + C)])

    def gather_add(h):
        step("zz%d" % h, "v", lambda q: V.tensor_tensor(T.ZT[:, h:512:2], T.AW[:, 2 * AWID * h:2 * AWID * (h + 1)].indirect(T.LC[:, 0:16]),
                                                       T.FH[:, C * h:C * h + C], A.add),
             lanes("AW", 0, AWID, (h, h + 2)) + [("FH", C * h, C * h + C), ("LC", 0, 32)], lanes("ZT", 0, 128, (h, h + 2)))

    def add(b):
        a = C * (b % 2)
        step("z%d" % b, "v", lambda q: V.tensor_tensor(T.ZT[:, 512 + b:1024:4], T.AS[:, a + b // 2:a + C:2], T["p%d" % b][:, 128:C], A.add),
             [("AS", a, a + C), ("p%d" % b, 0, 512)], lanes("ZT", 128, C, (b,)))

    for t in range(R):
        part[0] = str(t)
        last = t == R - 1
        XW, QX, QM, QB = "XW%d" % (t % 2), "QX%d" % t, "QM%d" % t, "QB%d" % t
        NX = "XW%d" % ((t + 1) % 2)
        if t > 0:
            quant("QM", QM, 0, 128, XW, XB + 4 * 64, lanes(XW, 64, 192))
        for h in (1, 0):
            mm("S%d" % h, 4 + h, 128, "UC", 128 * h, QM, 0)
        if t > 0:
            pages("sv", XW, 0, 0, SA)
            pages("vs", XW, 1, 0, SA)
            pages("sv", XW, 0, SB, C)
            pages("sv", XW, 1, SB, C)
        psum_scan("PK", 5, 0, 17)
        psum_scan("PC", 4, 32, 65)
        below("k", ("MK", 0, 81), ("PK", 0, 81), ("PK", 16, 17))
        below("c", ("MC", 0, 65), ("PC", 0, 65), ("PC", 64, 65))
        if t == 0:
            ts("sg", ("PC", 32, 33), ("PC", 64, 65), 0.5, A.is_ge, A.subtract)
            ts("B0#1", "Z", "k", 2.0, A.is_gt, A.mult)
            ts("B1#0", "Z2", "sg", "k", A.mult, A.min)
            ts("d", "c", "k", None, A.subtract)
            scan("BO", "B0", "B1", A.mult, A.add)
            ts(("LB", 0, 16), "I1", "d", 4.0, A.add, A.mult)
            ts(("LB", 16, 24), "BO#1", "d", 4.0, A.add, A.mult)
        else:
            ts("sg", ("PC", 32, 33), ("PC", 64, 65), 136.0, A.is_lt, A.mult)
            ts(("TO", 0, 1), "tj", "k", "sg", A.add, A.add)
            ts("Ik", "I1", "k", None, A.subtract)
            step("LB16", "v", lambda q: V.tensor_scalar(T.LB[:, 16:32], T.TB[:, 0:272].indirect(T.TO[:, 0:1]), opd("c")[0], 4.0, A.add, A.mult),
                 [("TB", 0, 272), ("TO", 0, 1), ("c", 0, 1)], [("LB", 16, 32)])
            ts(("LB", 0, 16), "Ik", "c", 4.0, A.add, A.mult)
        lin("vs", "cm", "c", 1.0, -160.0)
        act(("ae", 0, 33), "Jh", -1.0, "c", F.Abs)
        allx = lanes(XW, -PAD, C + PAD)
        gather("Ba", "sv", T.BT[:, 0:16 * NS], T[XW][:, 0:XWID], T.LB[:, 0:NS], allx + [("LB", 0, NS)], lanes("BT", 0, 4 * NS))
        gather("Bb", "vs", T.BT[:, 16 * NS:384], T[XW][:, 0:XWID], T.LB[:, NS:24], allx + [("LB", NS, 24)], lanes("BT", 4 * NS, 96))
        quant("QB", QB, 0, 128, "BT", 0, lanes("BT", 0, 128))
        send(t, QB, QX)
        quant("QX", QX, 0, 128, XW, XB, lanes(XW, 0, 128))
        quant("QXb", QX, 128, 128, XW, XB + 512, lanes(XW, 128, C))
        if t == 0:
            list_constants()
            stack_table()
        lin("sv", "cs", "CS", "cm", 0.0)
        act("D0#1", ("Jh", 0, 32), -1.0, "c", F.Sign)
        act("D1#0", "ae", -1.0, "k", F.Sign)
        ts("D0#2", ("Jh", 0, 32), "c", -1.0 / 256, A.subtract, A.mult)
        lin("sv", "D1#1", "NK", "k", 0.0)
        lin("sv", "L0#0", "JO", 1.0, ("D1", 97, 98))
        act("E1#1", ("ae", 0, 32), -1.0 / 1024, ("D1", 100, 101), F.Abs)
        lin("sv", "s", "k", -2.0, ("ae", 32, 33))
        if t == 0:
            for name, b in (("EH", 2), ("EH", 1), ("EH", 3), ("E", 0), ("E", 2), ("E", 1), ("E", 3)):
                e_quant(name, b)
        lin("sv", "K4m", "k", 4.0, -1.0)
        for b in (0, 2, 1, 3):
            mm("F%d" % b, b, C, "EH", 128 * b, QX, 0)
        for b in (0, 2, 1, 3):
            window_copy("f%d" % b, "sv", b, b, 0, C, 0)
        scan("DO", "D0", ("D1", 0, 96), A.subtract, A.max)
        lin("vs", "L1#1", "J4O", 1.0, "s")
        ts("pm", "DO#2", ("cs", 0, 1), 0.5, A.is_le, A.subtract)
        lin("vs", "L0#1", "L1#1", 1.0 / 3, 256.0 / 3 - 0.25)
        tt("dh", "DO#2", "pm", A.mult)
        scan("LM", "L0", "L1", A.max, A.max)
        lin("vs", "E1#0", "dh", 0.5, ("cs", 2, 3))
        ts(("NI", 0, 32), "LM#1", 4.0, None, A.mult)
        ts("E0#1", "dh", ("cs", 1, 2), -0.5, A.add, A.is_lt)
        ts(("HI", 0, 32), ("NI", 0, 32), 2, None, A.bitwise_and)
        scan("EO", "E0", "E1", A.add, A.min)
        ts(("PI", 0, 32), ("NI", 0, 32), 1, None, A.bitwise_and)
        ts(("LC", 0, 32), "EO#1", 2048.0, "lcb", A.mult, A.add)
        twin(0)
        twin(1)
        if t == 0:
            quant("QV", "QV", 0, 128, "VT", 0, [("VT", 0, 512)])
        for b in (0, 2, 1, 3):
            mm("G%d" % b, 4 + b, 128, "EH", 128 * b, QX, AWID - 128)
            window_copy("g%d" % b, ("vs", "sv")[b % 2], b, 4 + b, 128 - K, K, C)
        for b in range(4):
            mm("X0%d" % b, 4 + b, 128, "E", 128 * b, QX, 0, True, False)
        ts("Et", ("HI", 0, 32), "K4m", -510.5, A.mult, A.add)
        for h in (1, 0):
            gather("A%d" % h, "s", T.AS[:, C * h:C * h + C], T.AW[:, 2 * AWID * h:2 * AWID * (h + 1)], T.LC[:, 16:32],
                   lanes("AW", 0, AWID, (h, h + 2)) + [("LC", 0, 32)], [("AS", C * h, C * h + C)])
        if t == 0:
            for a, b in ((-PAD, 0), (C, C + PAD), (SB, 192)):
                zeros("XW1", a, b)
        gather_add(0)
        gather_add(1)
        for h in range(2):
            a = 128 * h
            for b in ((1,), (3, 0, 2))[h]:
                add(b)
            if h == 0:
                tt("Dt", "Et", ("NI", 0, 32), A.add)
            else:
                ts("gt", ("PI", 0, 32), -0.5, 0.25, A.mult, A.add)
                for b in (1, 3, 0, 2):
                    mm("X1%d" % b, b, 128, "E", 128 * b, QX, 128, True, False)
            quant("QZ%d" % h, "QZ", a, 128, "ZT", 4 * a, lanes("ZT", a, a + 128))
            for b in range(4):
                mm("W%d%d" % (h, b), b + 4 - 4 * h, 128, "W", 128 * b, "QZ", a, False, True)
        tt("gD", "Dt", "gt", A.mult)
        for qs, h, b in (("sv", 0, 0), ("sv", 0, 1), ("sv", 0, 2), ("vs", 0, 3), ("sv", 1, 0), ("vs", 1, 1), ("sv", 1, 2), ("vs", 1, 3)):
            psum_copy("y%d%d" % (h, b), qs, "YS", C * (2 * (b % 2) + b // 2) + 128 * h, b + 4 - 4 * h, 128, 0.03125)
            if (h, b) == (0, 3):
                ts(("LO", 0, 32), "gD", "cm", "cb", A.add, A.add)
                if last:
                    ts("OF", "gD", "cm", "cb", A.add, A.add)
        if last:
            call("v", lambda q, o, a: V.transpose(o, a), "OT", "OF")
        else:
            pages("sv", NX, 0, SA, SB)
            pages("vs", NX, 1, SA, SB)
    part[0] = "z"
    XW, QX = "XW%d" % (R % 2), "QX%d" % R
    for h in range(2):
        a = 128 * h
        pages("sv", XW, 0, a, a + 128)
        pages("vs", XW, 1, a, a + 128)
        if h == 0:
            lin("sv", "OC", "OT#0", 1.0, 0.0)
            for e in range(2):
                dma("ys", "lo%d" % e, T.lo[e:8:2, 0:C], opd(("OC", 8 * e, 8 * e + 8))[0], [("OC", 0, 16)], [])
        quant("QX%d" % h, QX, a, 128, XW, XB + 4 * a, lanes(XW, a, a + 128))
        mm("V%d" % h, 4 + h, 128, "QV", 0, QX, a)
        dma("ys", "oc%d" % h, T.oc[:, 4 * a:4 * a + 512], T[QX + "c"][:, a:a + 128].bitcast(dt.uint8), [(QX, a, a + 128)], [])
    for h in range(2):
        a = 128 * h
        psum_copy("y%d" % h, ("sv", "vs")[h], "YO", a, 4 + h, 128, 1.0)
        dma(("sy", "ys")[h], "y%d" % h, T.y[:, a:a + 128], T.YO[:, a:a + 128], [("YO", a, a + 128)], [])
    for i in range(4):
        dma("sy", "os%d" % i, T.osc[4 * i:4 * i + 4, 0:C], T[QX + "p"][32 * i:32 * i + 4, 0:C], [(QX, 0, C)], [])
    return steps


def rank_program(g, core, T, topo):
    if T.rank_of(core) is None:
        return
    steps = plan(g, core, T, topo)
    order = [x.split(":") for x in ORDER.split()] or [(name, s[1][0]) for name, s in steps.items()]
    assert sorted(x[0] for x in order) == sorted(steps)
    queue = {"v": g.vector, "s": g.scalar, "t": g.tensor, "g": g, "y": g.sync}
    count = {}
    waited = {}
    known = {q: {} for q in queue}
    behind = {}
    log = {}

    def need(q, name, a, b, write, out):
        for x in log.get(name, ()):
            if x[0] < b and a < x[1]:
                if x[3] != q:
                    if write or x[2] or name[0] == "p" and name[1:].isdigit():
                        out.append(x[4])
                elif x[2] and not write or q != "t" and write:
                    out.append(x[4])

    def note(q, name, a, b, write, ev):
        rows = log.setdefault(name, [])
        if write:
            rows[:] = [x for x in rows if not (a <= x[0] and x[1] <= b)]
        rows.append((a, b, write, q, ev))

    def wait(q, ev):
        sem, val = ev
        if known[q].get(sem, 0) >= val:
            return
        queue[q].wait_ge(T.sem[sem], val)
        waited[sem] = max(waited.get(sem, 0), val)
        for s, n in list(behind.get(ev, {}).items()) + [(sem, val)]:
            known[q][s] = max(known[q].get(s, 0), n)

    for name, q in order:
        kind, qs, fn, rd, wr = steps[name]
        evs = []
        for r in rd:
            need(q, r[0], r[1], r[2], False, evs)
        for r in wr:
            need(q, r[0], r[1], r[2], True, evs)
        most = {}
        for s, n in evs:
            most[s] = max(most.get(s, 0), n)
        for s in sorted(most, key=lambda s: (s == "c" + q, s)):
            wait(q, (s, most[s]))
        if kind == "c":
            who, sem = q, "c" + q
            count[sem] = count.get(sem, 0) + 1
            fn(q).then_inc(T.sem[sem], 1)
        elif kind[0] == "d":
            who = sem = kind
            count[sem] = 16
            fn(q).then_inc(T.sem[sem], 16)
        else:
            who = sem = kind
            count[sem] = count["loc" + kind[3:]] = fn(q)
        ev = (sem, count[sem])
        if kind[0] != "a":
            behind[ev] = dict(known[q])
            for r in rd:
                note(who, r[0], r[1], r[2], False, ev)
        for r in wr:
            note(who, r[0], r[1], r[2], True, ev)
    for sem in sorted(count, key=lambda s: (s[0] == "d", s)):
        if waited.get(sem, 0) < count[sem]:
            wait("g", (sem, count[sem]))
